import numpy as np, ml_dtypes
CORES = [66,74,82,90,194,202,210,218]
N = 8
import mx_ref
BF = ml_dtypes.bfloat16
def entries(a):
    return np.ascontiguousarray(a.T).reshape(-1)
def table(e):
    return np.ascontiguousarray(np.reshape(e, (-1, 16)).T).astype(np.int32)
def cols(t, e):
    v = np.concatenate([t.reshape(128, -1, 4), np.zeros((128, 1, 4), BF)], axis=1)
    return np.ascontiguousarray(v[:, e]).reshape(128, -1)
def f(rng, *shape):
    return mx_ref.flush((rng.standard_normal(shape, dtype=np.float32) * np.exp2(rng.integers(-2, 3, shape[:-1] + (1,)))).astype(BF))
def wide(rng, *shape, cols=0):
    v = rng.standard_normal(shape, dtype=np.float32) * np.exp2(rng.integers(-12, 13, shape)).astype(np.float32)
    if cols: v *= np.repeat(np.exp2(rng.integers(-cols, cols + 1, shape[:-2] + (1, shape[-1] // 4))) * (rng.random(shape[:-2] + (1, shape[-1] // 4)) > 0.0625), 4, axis=-1).astype(np.float32)
    return mx_ref.flush(v.astype(BF))
T, S, O, CAPP = 128, 256, 2, (64, 96, 128)
B = len(CAPP)
def wanters(q, b):
    return sum(1 << e for e in range(N) if (e ^ q ^ (1 << b)) % (2 << b) == 0)
def holders(q, b):
    return (q >> b) << b, ((q >> b) + 1) << b
def limit(rng, m, keep, lo, hi, s, most):
    v = m.reshape(-1)
    e = np.flatnonzero(v[lo * T:hi * T] & s) + lo * T
    e = e[np.argsort(rng.random(len(e)) - ((keep.reshape(-1)[e] & s) != 0))][most:]
    v[e] &= ~s
def masks(rng, keep=None, off=None, share=0.55):
    keep = np.zeros((N, T), int) if keep is None else keep
    off = np.zeros((N, T), bool) if off is None else off
    for r in range(N):
        if not ((keep >> r) & 1).any(): keep[r, rng.choice(np.flatnonzero(~off[r]))] |= 1 << r
    n = rng.integers(1, 4, (N, T)) * (rng.random((N, T)) < share)
    m = ((np.argsort(rng.random((N, T, N)), axis=2) < n[:, :, None]) * (1 << np.arange(N))).sum(axis=2)
    m = np.ascontiguousarray(np.where(off, 0, m) | keep)
    for b in range(B):
        for q in range(N): limit(rng, m, keep, *holders(q, b), wanters(q, b), CAPP[b])
    for r in range(N): limit(rng, m, keep, 0, N, 1 << r, S)
    return {"dm": np.stack([table(v) for v in m])}
def setup_inputs(rng):
    return {"x": f(rng, N, 128, 4 * T), **masks(rng), "w": f(rng, N, 128, 512 * O)}
def setup_inputs_comb(rng):
    k = np.zeros((N, T), int); c = np.arange(T); s = int(rng.integers(0, 16)); p = int(rng.integers(0, N)); g = p ^ (N >> 1)
    for e in range(N): k[:, (c - e - s) % 4 == 0] |= 1 << e
    lo, hi = holders(p, B - 1)
    k[lo:hi] &= ~(1 << g)
    k[p, c % 16 != s] |= 1 << g
    assert not check_inputs({"dm": np.stack([table(v) for v in k])})
    return {**setup_inputs(rng), **masks(rng, k)}
def setup_inputs_turn(rng):
    k = np.zeros((N, T), int); g = int(rng.integers(0, N))
    k[g ^ 1, rng.permutation(T)[:CAPP[0]]] |= 1 << g
    k[g ^ 3, rng.permutation(T)[:CAPP[0]]] |= 1 << g
    h = rng.permutation(T)
    k[g, h[:CAPP[0]]] |= 1 << (g ^ 3)
    k[g, h[CAPP[0]:2 * CAPP[0]]] |= 1 << (g ^ 2)
    if N == 8: k[g ^ 6, rng.permutation(T)[:CAPP[1]]] |= 1 << (g ^ 4)
    return {**setup_inputs(rng), **masks(rng, k)}
def setup_inputs_none(rng):
    z = np.zeros((N, T), bool); k = np.zeros((N, T), int); p = int(rng.integers(0, N))
    for r in range(N): z[r, rng.permutation(T)[:T // 2]] = True
    k[p ^ 1, rng.choice(np.flatnonzero(~z[p ^ 1]))] |= 1 << p
    d = {**setup_inputs(rng), **masks(rng, k, off=z, share=1)}
    d["dm"][p] = 0
    return d
def setup_inputs_full(rng):
    k = np.zeros((N, T), int); g = int(rng.integers(0, N)); s = int(rng.integers(0, T))
    k[g ^ 1, (np.arange(CAPP[0]) + s) % T] |= 1 << (g ^ 2)
    k[g, (np.arange(S - sum(CAPP[1:])) + s) % T] |= 1 << g
    for b in range(1, B):
        for r in range(N):
            if r >> b == (g >> b) ^ 1: k[r, (np.arange(CAPP[b] >> b) + s) % T] |= 1 << g
    assert not check_inputs({"dm": np.stack([table(v) for v in k])})
    return {**setup_inputs(rng), **masks(rng, k, share=1)}
def setup_inputs_spread(rng):
    d = setup_inputs(rng); d["x"] = wide(rng, N, 128, 4 * T, cols=8); return d
def check_inputs(d):
    bad = []
    m = np.stack([entries(v) for v in d["dm"]]).astype(np.int64)
    if m.min() < 0 or m.max() >= 1 << N: bad.append("dm")
    for r in range(N):
        if ((m >> r) & 1).sum() > S: bad.append("arrivals")
    for b in range(B):
        for q in range(N):
            lo, hi = holders(q, b)
            if ((m[lo:hi] & wanters(q, b)) != 0).sum() > CAPP[b]: bad.append("CAPP_" + str(b))
    return bad
def reference(x, dm, w):
    m = np.stack([entries(v) for v in dm])
    every = np.concatenate(list(x), axis=1)
    y = np.zeros((N, 128, O * S), np.float32); ln = np.zeros((N, 1, 2), np.float32)
    for r in range(N):
        e = np.flatnonzero((m.reshape(-1) >> r) & 1); n = len(e)
        k = np.full(S, -1); k[:n] = e
        a = mx_ref.quantize(cols(every, k))
        for o in range(O):
            y[r][:, S * o:S * o + n] = mx_ref.matmul(mx_ref.quantize(np.ascontiguousarray(w[r][:, 512 * o:512 * o + 512])), a)[:, :n]
        ln[r, 0, 0] = n; ln[r, 0, 1] = np.count_nonzero((m[r] >> r) & 1)
    return {"y": y, "ln": ln}

@@ -1,0 +1,447 @@
+from concourse.mybir import dt, AluOpType, ActivationFunctionType
+
+A = AluOpType
+F = ActivationFunctionType
+U8, U32 = dt.uint8, dt.uint32
+N, COLS, S = 8, 128, 256
+BIG = 1024.0
+H0, E1, L1, E2, L2 = 64, 32, 64, 32, 96
+
+CODE, PLANE = "float8_e4m3fn_x4", "uint8"
+SCRATCH = {
+    "dmi": ("sbuf", [128, 8], "int32"), "xt": ("sbuf", [128, 512], "bfloat16"), "wt": ("sbuf", [128, 1024], "bfloat16"),
+    "c0c": ("sbuf", [128, 128], CODE), "c0s": ("sbuf", [128, 128], PLANE),
+    "c1c": ("sbuf", [128, 320], CODE), "c1s": ("sbuf", [128, 320], PLANE),
+    "c2c": ("sbuf", [128, 352], CODE), "c2s": ("sbuf", [128, 352], PLANE),
+    "a2c": ("sbuf", [128, 128], CODE), "a2s": ("sbuf", [128, 128], PLANE),
+    "nnc": ("sbuf", [128, 288], CODE), "nns": ("sbuf", [128, 288], PLANE),
+    "wqc": ("sbuf", [128, 256], CODE), "wqs": ("sbuf", [128, 256], PLANE),
+    "sl0c": ("sbuf", [128, H0], CODE), "sl0s": ("sbuf", [128, H0], PLANE),
+    "se1c": ("sbuf", [128, E1], CODE), "se1s": ("sbuf", [128, E1], PLANE),
+    "sl1c": ("sbuf", [128, L1], CODE), "sl1s": ("sbuf", [128, L1], PLANE),
+    "sl2c": ("sbuf", [128, L2], CODE), "sl2s": ("sbuf", [128, L2], PLANE),
+    "pair": ("sbuf", [128, 16], "uint16"), "tabb": ("sbuf", [128, 16], "uint16"),
+    "run": ("sbuf", [128, 16], "float32"), "fmo": ("sbuf", [128, 16], "float32"),
+    "lv": ("sbuf", [128, 256], "int32"), "zi": ("sbuf", [128, 16], "int32"), "zr": ("sbuf", [128, 16], "int32"),
+    "zm": ("sbuf", [128, 16], "int32"), "kq": ("sbuf", [128, 16], "float32"), "kf": ("sbuf", [128, 16], "float32"),
+    "gr": ("sbuf", [128, 8], "int32"), "gm": ("sbuf", [128, 8], "int32"), "gq": ("sbuf", [128, 8], "float32"),
+    "kg": ("sbuf", [128, 8], "float32"), "z7": ("sbuf", [128, 8], "int32"), "o8": ("sbuf", [128, 8], "uint16"),
+    "cu": ("sbuf", [128, 4], "uint16"), "k8a": ("sbuf", [128, 128], "float32"), "k8": ("sbuf", [128, 128], "float32"),
+    "s8": ("sbuf", [128, 128], "bfloat16"), "b1a": ("sbuf", [128, 256], "bfloat16"),
+    "la": ("sbuf", [128, 3 * 256], "int32"), "lut": ("sbuf", [128, 6 * 256], "bfloat16"), "sg": ("sbuf", [128, 512], "bfloat16"),
+    "fl": ("sbuf", [128, 2048], "bfloat16"), "inc": ("sbuf", [128, 1024], "bfloat16"),
+    "k0": ("sbuf", [128, 128], "bfloat16"), "k1": ("sbuf", [128, 256], "bfloat16"), "k2": ("sbuf", [128, 256], "bfloat16"),
+    "kso": ("sbuf", [128, 128], "bfloat16"), "ks1": ("sbuf", [128, 128], "bfloat16"),
+    "kb2": ("sbuf", [128, 256], "bfloat16"), "kbs": ("sbuf", [128, 256], "bfloat16"), "prs": ("sbuf", [128, 256], "bfloat16"),
+    "js": ("sbuf", [128, 8192], "bfloat16"), "jv": ("sbuf", [128, 4096], "bfloat16"), "jw": ("sbuf", [128, 4096], "bfloat16"),
+    "cs": ("sbuf", [128, 16], "float32"), "rr": ("sbuf", [128, 128], "float32"), "ra": ("sbuf", [128, 96], "float32"),
+    "rb": ("sbuf", [128, 192], "float32"), "rc": ("sbuf", [128, 192], "float32"),
+    "col": ("sbuf", [128, 16], "float32"), "ke": ("sbuf", [128, 2], "float32"), "kl": ("sbuf", [128, 4], "float32"),
+    "kl2": ("sbuf", [128, 3], "float32"), "ba": ("sbuf", [128, 12], "float32"), "nc": ("sbuf", [128, 12], "float32"),
+    "sx": ("sbuf", [128, 16], "float32"), "dz": ("sbuf", [128, 8], "float32"), "dd": ("sbuf", [128, 8], "float32"),
+    "tm": ("sbuf", [128, 384], "float32"), "tg": ("sbuf", [128, 16], "float32"), "lnb": ("sbuf", [1, 2], "float32"),
+    "t0": ("sbuf", [128, 4], "uint16"), "te": ("sbuf", [128, 2], "uint16"), "t1": ("sbuf", [128, 4], "uint16"),
+    "tp": ("sbuf", [128, 8], "uint16"), "t2": ("sbuf", [128, 6], "uint16"), "tn": ("sbuf", [128, 18], "uint16"),
+    "tf": ("sbuf", [128, 16], "uint16"),
+    "g0": ("sbuf", [128, 432], "float32"), "g1": ("sbuf", [128, 432], "float32"),
+    "y0": ("sbuf", [128, 256], "float32"), "y1": ("sbuf", [128, 256], "float32"),
+    "ps": ("psum", [128, 2048], "float32"),
+}
+ARR = ["rma", "rmb", "rmc", "h0c", "h0s", "e1c", "e1s", "l1c", "l1s", "e2c", "e2s", "l2c", "l2s"]
+SEMAPHORES = ["qv", "qs", "qt", "qp", "ld", "lx", "lw", "sya", "syb", "sln", "loc"] + ARR
+
+
+def rank_program(g, core, T, topo):
+    q = T.rank_of(core)
+    if q is None:
+        return
+    V, SC, TE = g.vector, g.scalar, g.tensor
+    queue = {"v": V, "s": SC, "t": TE, "p": g, "y": g.sync}
+    done = {"v": 0, "s": 0, "t": 0, "p": 0}
+    seen = {}
+
+    def need(e, *deps):
+        best = {}
+        for d in deps:
+            best[d[0]] = max(best.get(d[0], 0), d[1])
+        for s in best:
+            if seen.get((e, s), 0) < best[s]:
+                queue[e].wait_ge(T.sem[s], best[s])
+                seen[(e, s)] = best[s]
+
+    def mark(e, ins):
+        ins.then_inc(T.sem["q" + e], 1)
+        done[e] += 1
+        return ("q" + e, done[e])
+
+    sent = [0]
+
+    def send(dst, out, in_, sem, *deps):
+        need("p", *deps)
+        rid, pid = topo.addr(dst, core)
+        g.remote_dma(out, in_, T.sem[sem], T.sem["loc"], pid, rid, topo.mask(core, dst))
+        sent[0] += len(topo.engines(core, dst))
+
+    def arrived(sem, src):
+        return (sem, len(topo.engines(src, core)))
+
+    peer = [T.cores[q ^ (1 << b)] for b in range(3)]
+    codes = lambda t, a, b: t[:, a:b].bitcast(U8)
+    words = lambda t, a, b: t[:, a:b].bitcast(U32)
+
+    for i in range(8):
+        (g.sync if i % 2 == 0 else SC).dma_start(T.dmi[16 * i:16 * i + 16, :], T.dm[:, :]).then_inc(T.sem.ld, 16)
+    g.sync.dma_start(T.xt[:, :], T.x[:, :]).then_inc(T.sem.lx, 16)
+
+    odd = sum(1 << r for r in range(N) if (r ^ q) & 1)
+    even = sum(1 << r for r in range(N) if not (r ^ q) & 1)
+    bit = lambda r: 1 << r
+
+    def iota(o, pat, base=0):
+        return mark("p", g.iota(o, pat, base, 0, allow_small_or_imprecise_dtypes=True))
+    tlv = mark("p", g.iota(T.lv[:, :], [[1, 256]], 0, 0))
+    tzi = mark("p", g.iota(T.zi[:, :], [[128, 16]], 0, 1))
+    M0, M1, M2, MS, B0, B1 = range(6)
+    tl = {}
+    look = lambda l: T.lut[:, 256 * l:256 * l + 256]
+    bits = lambda r, c: [[0, 256 >> (r + 1)], [c, 2], [0, 1 << r]]
+
+    def lut(i, j, m, absent):
+        need("v", tlv)
+        a = mark("v", V.tensor_scalar(T.la[:, 256 * j:256 * j + 256], T.lv[:, :], m, None, A.bitwise_and))
+        need("v", a)
+        i_ = T.la[:, 256 * j:256 * j + 256]
+        if absent:
+            return mark("v", V.tensor_scalar(look(i), i_, 0.0, BIG, A.is_equal, A.mult))
+        return mark("v", V.tensor_scalar(look(i), i_, 0.0, None, A.is_gt))
+    a = mark("v", V.memset(T.sg[:, :], 1.0))
+    need("v", a)
+    tsg = mark("v", V.memset(T.sg[:, 256:257], 0.0))
+    tl[M0] = lut(M0, 0, odd, False)
+    need("v", tzi)
+    tzr = mark("v", V.tensor_scalar(T.zr[:, :], T.zi[:, :], 15, None, A.bitwise_and))
+    a = mark("v", V.tensor_scalar(T.zm[:, :], T.zi[:, :], 3, 240, A.logical_shift_right, A.bitwise_and))
+    need("v", a, tzr)
+    tkq = mark("v", V.tensor_tensor(T.kq[:, :], T.zr[:, :], T.zm[:, :], A.add))
+    need("v", tkq)
+    tkf = mark("v", V.tensor_scalar(T.kf[:, :], T.kq[:, :], 0.5, None, A.add))
+    mark("v", V.tensor_scalar(T.gr[:, :], T.zi[:, 0:8], 31, None, A.bitwise_and))
+    a = mark("v", V.tensor_scalar(T.gm[:, :], T.zi[:, 0:8], 2, 224, A.logical_shift_right, A.bitwise_and))
+    need("v", a)
+    a = mark("v", V.tensor_tensor(T.gq[:, :], T.gr[:, :], T.gm[:, :], A.add))
+    need("v", a)
+    tkg = mark("v", V.tensor_scalar(T.kg[:, :], T.gq[:, :], 0.5, None, A.add))
+    tl[M2] = iota(look(M2), bits(q ^ 4, 1))
+    tl[MS] = iota(look(MS), bits(q, 1))
+
+    use = {"js": 0, "jv": 0, "cs": 0, "fl": 0}
+
+    def take(name, n):
+        o = use[name]
+        use[name] += n
+        return o
+
+    def scan(out, fl, n, init, *deps):
+        need("v", tsg, *deps)
+        return mark("v", V.tensor_tensor_scan(out, T.sg[:, 0:n], fl, init, A.mult, A.add))
+
+    def flags(e, l, tab, n, *deps):
+        o = take("fl", n)
+        need(e, tl[l], *deps)
+        out, src = T.fl[:, o:o + n], look(l).indirect(tab)
+        if e == "v":
+            return out, mark(e, V.tensor_copy(out, src))
+        return out, mark(e, SC.activation(out, src, F.Copy))
+
+    def held(l, tab, inc, out, *deps):
+        need("v", tl[l], *deps)
+        return mark("v", V.tensor_tensor(out, look(l).indirect(tab), inc, A.add))
+
+    def on_vector(key, n, kcols, nv, *deps):
+        o = take("jv", nv * n)
+        need("v", *deps)
+        for i in range(nv):
+            a_ = mark("v", V.tensor_scalar(T.jv[:, o + i * n:o + i * n + n], key, kcols(i), 2.0, A.is_le, A.mult))
+        need("v", a_, tsg)
+        sg = T.sg[:, 256 - n:256 - n + nv * n] if nv == 2 else T.sg[:, 0:n]
+        a_ = mark("v", V.tensor_tensor_scan(T.jw[:, o:o + nv * n], sg, T.jv[:, o:o + nv * n], 0.0, A.mult, A.add))
+        return T.jw[:, o + n - 1:o + nv * n:n], a_
+
+    def on_scalar(key, n, kcols, ns, out, at, *deps):
+        need("s", *deps)
+        for i in range(ns):
+            o = take("js", n)
+            a_ = mark("s", SC.activation(T.js[:, o:o + n], key, F.Sign, bias=kcols(i), scale=-1.0, accum_out=out[:, at + i:at + i + 1]))
+        return a_
+
+    def table(tab, key, n, kt, nv, ns, *deps):
+        o = take("cs", ns)
+        b_ = on_scalar(key, n, lambda i: kt[:, nv + i:nv + i + 1], ns, T.cs, o, *deps)
+        s_, a_ = on_vector(key, n, lambda i: kt[:, i:i + 1], nv, *deps)
+        return (tab, nv, ns, s_, a_, o, b_, n)
+
+    def finish(tab, nv, ns, s_, a_, o, b_, n):
+        need("v", a_)
+        mark("v", V.tensor_scalar(tab[:, 0:nv], s_, 0.5, None, A.mult))
+        need("v", b_)
+        return mark("v", V.tensor_scalar(tab[:, nv:nv + ns], T.cs[:, o:o + ns], 0.5, n / 2, A.mult, A.add))
+
+    def turn(tab, j, n, at, c, *deps):
+        need("v", *deps)
+        a_ = mark("v", V.transpose(T.ra[:, 32 * j:32 * j + 32], T.rr[:, at:at + 32]))
+        need("v", a_, tcu)
+        a_ = mark("v", V.tensor_copy(T.rb[:, 64 * j:64 * j + 64], T.ra[:, 32 * j:32 * j + 32].indirect(T.cu[:, :])))
+        need("v", a_)
+        a_ = mark("v", V.transpose(T.rc[:, 64 * j:64 * j + 64], T.rb[:, 64 * j:64 * j + 64]))
+        need("v", a_)
+        mark("v", V.tensor_scalar(tab[:, 0:2 * n:2], T.rc[:, 64 * j:64 * j + n], 0.5, c, A.mult, A.add))
+        return mark("v", V.tensor_scalar(tab[:, 1:2 * n:2], T.rc[:, 64 * j + 32:64 * j + 32 + n], 0.5, c, A.mult, A.add))
+
+    def pick(out, oa, ob, src, n, tab, *deps):
+        need("v", *deps)
+        a_ = mark("v", V.tensor_copy(words(T[out + "c"], oa, ob), words(T[src + "c"], 0, n).indirect(tab)))
+        need("s", *deps)
+        b_ = mark("s", SC.activation(T[out + "s"][:, oa:ob], T[src + "s"][:, 0:n].indirect(tab), F.Copy))
+        return a_, b_
+
+    def quant(c, a_, b_):
+        return mark("v", V.quantize_mx(T[c + "c"][:, a_:b_], T[c + "s"][:, a_:b_], T.xt[:, :]))
+
+    def ship(dst, to, a_, b_, src, sa, sb, sem, tok):
+        send(dst, codes(T[to + "c"], a_, b_), codes(T[src + "c"], sa, sb), sem + "c", tok[0])
+        send(dst, T[to + "s"][:, a_:b_], T[src + "s"][:, sa:sb], sem + "s", tok[1])
+
+    own, ot1 = T.pair[:, 0:8], T.pair[:, 8:16]
+    INC = {"1r": 0, "2r": 128, "sr": 256, "2b": 384, "sb": 640}
+    inc = lambda k, n=128: T.inc[:, INC[k]:INC[k] + n]
+    last = lambda k, n=128: T.inc[:, INC[k] + n - 1:INC[k] + n]
+    col = lambda i: T.col[:, i:i + 1]
+    kgc = lambda o: (lambda i: T.kg[:, o + i:o + i + 1])
+
+    need("v", ("ld", 128))
+    tpo = mark("v", V.tensor_copy(own, T.dmi[:, :]))
+    send(peer[0], T.pair[:, 8:16], own, "rma", tpo)
+
+    f0, f = flags("v", M0, own, 128, tpo)
+    ti = scan(T.k0[:, :], f0, 128, 0.0, f)
+    c0 = table(T.t0, T.k0[:, 0:127], 127, T.kf, 1, 3, ti, tkf)
+    need("v", ("lx", 16))
+    tq0 = quant("c0", 0, 128)
+    t0 = finish(*c0)
+    p0 = pick("sl0", 0, H0, "c0", 128, T.t0[:, :], t0, tq0)
+    ship(peer[0], "c1", 128, 128 + H0, "sl0", 0, H0, "h0", p0)
+
+    h = 4 * (q >> 2)
+    cnt_at = lambda r: 4 + r
+    bas_at = lambda r: r if r < 4 else 8 + r
+    near = lambda x: h + ((q & 3) ^ x)
+    rc_ = lambda x: T.run[:, cnt_at(near(x)):cnt_at(near(x)) + 1]
+    rb_ = lambda x: T.run[:, bas_at(near(x)):bas_at(near(x)) + 1]
+    need("s", tkf)
+    const = lambda o, n, c: mark("s", SC.activation(o, T.kf[:, 0:n], F.Copy, bias=c, scale=0.0))
+    const(T.sx[:, 7:8], 1, 0.0)
+    const(T.dd[:, 7:8], 1, 4096.0)
+    for x in range(3):
+        const(rb_(x), 1, (0.0, 128.0, 192.0)[x])
+    const(T.g0[:, 416:432], 16, 0.0)
+    tcg = const(T.g1[:, 416:432], 16, 0.0)
+
+    tl[M1] = lut(M1, 1, bit(q ^ 2) | bit(q ^ 6), False)
+    f1fl, f1f = flags("s", M1, own, 128, tpo)
+    quant("c1", 0, 128)
+    tq1 = quant("c1", 192, 320)
+    t1o = scan(T.k1[:, 0:128], f1fl, 128, 0.0, f1f)
+    n1o = T.k1[:, 127:128]
+    need("v", t1o)
+    ta = mark("v", V.tensor_scalar(col(0), n1o, float(E1), None, A.min))
+    need("v", ta, tkf)
+    tke = mark("v", V.tensor_scalar(T.ke[:, :], T.kf[:, 0:2], col(0), -float(E1), A.add, A.add))
+    tkl = mark("v", V.tensor_scalar(T.kl[:, :], T.kf[:, 0:4], col(0), None, A.add))
+    ce = table(T.te, T.k1[:, 0:127], 127, T.ke, 1, 1, t1o, tke)
+    te = finish(*ce)
+    pe = pick("se1", 0, E1, "c0", 128, T.te[:, :], te, tq0)
+    ship(peer[1], "c2", 128, 128 + E1, "se1", 0, E1, "e1", pe)
+    need("y", pe[0])
+    g.sync.dma_start(T.wt[:, :], T.w[:, :]).then_inc(T.sem.lw, 16)
+
+    arm = arrived("rma", peer[0])
+    send(peer[1], T.tabb[:, :], T.pair[:, :], "rmb", arm, tpo)
+    iota(T.nc[:, 0:4], [[0, 4]], 128)
+    iota(T.nc[:, 4:6], [[0, 2]], 384)
+    tcn = iota(T.nc[:, 9:12], [[0, 3]], 512)
+    tk8 = iota(T.k8a[:, :], [[16, 16], [0, 8]])
+    need("p", tsg)
+    ts8 = mark("p", g.affine_select(T.s8[:, :], T.sg[:, 0:128], [[0, 16], [1, 8]], A.not_equal, 0.0, 0, 0))
+
+    tl[B0] = lut(B0, 2, even, True)
+    f2ol, f2o = flags("s", M2, own, 128, tpo)
+    fsol, fso = flags("s", MS, own, 128, tpo)
+    f2fl, f2f = flags("s", M2, ot1, 128, arm)
+    f1l, f = flags("v", M1, ot1, 128, arm)
+    f1r = scan(inc("1r"), f1l, 128, n1o, f, t1o)
+    tk1b = held(B0, ot1, inc("1r"), T.k1[:, 128:256], f1r, arm)
+    c1 = table(T.t1, T.k1[:, :], 256, T.kl, 2, 2, t1o, tk1b, tkl)
+    t2o = scan(T.k2[:, 0:128], f2ol, 128, 0.0, f2o)
+    tso = scan(T.kso[:, :], fsol, 128, 0.0, fso)
+    trr = mark("v", V.memset(T.rr[:, :], 0.0))
+    on_scalar(T.kso[:, :], 128, kgc(0), 2, T.rr, 64, tso, tkg, trr)
+    tt1 = finish(*c1)
+    h0a = [arrived("h0c", peer[0]), arrived("h0s", peer[0])]
+    p1 = pick("sl1", 0, L1, "c1", 200, T.t1[:, :], tt1, tq1, *h0a)
+    ship(peer[1], "c2", 160, 160 + L1, "sl1", 0, L1, "l1", p1)
+
+    a = iota(T.b1a[:, :], bits(q, -int(BIG)), int(BIG))
+    need("p", a)
+    tl[B1] = mark("p", g.affine_select(look(B1), T.b1a[:, :], bits(q ^ 4, 1), A.is_equal, 0.0, 0, 0))
+
+    f2r = scan(inc("2r"), f2fl, 128, T.k2[:, 127:128], f2f, t2o)
+    tk2 = held(B0, ot1, inc("2r"), T.k2[:, 128:256], f2r, arm)
+    tcp = on_scalar(T.k2[:, :], 256, kgc(1), 3, T.rr, 1, t2o, tk2, tkg, trr)
+    s_, a = on_vector(T.k2[:, :], 256, kgc(0), 1, tk2, tkg)
+    need("v", a, trr)
+    tcv = mark("v", V.tensor_scalar(T.rr[:, 0:1], s_, -256.0, None, A.add))
+    brm = arrived("rmb", peer[1])
+    np_ = last("2r")
+    need("v", f2r)
+    ta = mark("v", V.tensor_scalar(col(1), np_, float(E2), None, A.min))
+    need("v", ta)
+    tkl2 = mark("v", V.tensor_scalar(T.kl2[:, :], T.kg[:, 0:3], col(1), None, A.add))
+    fc = lambda x: T.fmo[:, cnt_at(near(x)):cnt_at(near(x)) + 1]
+    fb = lambda x: T.fmo[:, bas_at(near(x)):bas_at(near(x)) + 1]
+    c_1, c_3, c_4 = T.k2[:, 127:128], T.inc[:, INC["2b"] + 127:INC["2b"] + 128], T.inc[:, INC["2b"] + 255:INC["2b"] + 256]
+    mark("v", V.memset(fb(0), 288.0))
+    mark("v", V.tensor_scalar(fb(1), c_1, 288.0, None, A.add))
+    tfb = mark("v", V.tensor_scalar(fb(2), np_, float(E2), 288.0, A.max, A.add))
+    cnp2, cof2, cdl, cpa = col(2), col(3), col(4), col(5)
+    a = mark("v", V.tensor_scalar(cnp2, np_, 2.0, None, A.mult))
+    need("v", tkl2)
+    b = mark("v", V.tensor_scalar(T.ba[:, 0:3], T.kl2[:, :], 2.0, -1.0, A.mult, A.add))
+    need("v", a, b)
+    tba = mark("v", V.tensor_scalar(T.ba[:, 3:6], T.ba[:, 0:3], cnp2, None, A.min))
+    mark("v", V.tensor_scalar(T.cu[:, 0:2], T.zr[:, 0:2], 0.0, None, A.add))
+    tcu = mark("v", V.tensor_scalar(T.cu[:, 2:4], T.zr[:, 2:4], 16.0, None, A.add))
+    ttp = turn(T.tp, 0, 4, 0, 128.0, tcv, tcp)
+
+    fl2b, ff2b = flags("s", M2, T.tabb[:, :], 256, brm)
+    f2b = scan(inc("2b", 256), fl2b, 256, np_, ff2b, f2r)
+    pp = pick("c2", 0, 128, "c1", 200, T.tp[:, :], ttp, tq1, *h0a)
+    ship(peer[2], "a2", 0, E2, "c2", 0, E2, "e2", pp)
+    tkb2 = held(B1, T.tabb[:, :], inc("2b", 256), T.kb2[:, :], f2b, brm)
+    need("s", tl[B1], brm)
+    a = mark("s", SC.activation(T.prs[:, 0:128], look(B1).indirect(T.tabb[:, 0:8]), F.Copy))
+    need("s", a)
+    tpa = mark("s", SC.activation(T.prs[:, 128:256], T.prs[:, 0:128], F.Copy, accum_out=cpa))
+    need("s", tpa)
+    tof = mark("s", SC.activation(cof2, cpa, F.Relu, bias=-2.0 * (COLS - E1), scale=2.0 / BIG))
+    need("s", t2o, f2r, f2b, tfb)
+    mark("s", SC.activation(fc(0), c_1, F.Copy))
+    mark("s", SC.activation(fc(1), c_1, F.Identity, bias=np_, scale=-1.0))
+    a = mark("s", SC.activation(fc(2), np_, F.Identity, bias=c_3, scale=-1.0))
+    mark("s", SC.activation(fc(3), c_3, F.Identity, bias=c_4, scale=-1.0))
+    need("s", a)
+    tfs = mark("s", SC.activation(fb(3), fc(2), F.Identity, bias=fb(2)))
+    send(peer[2], T.run[:, 2 * h:2 * h + 8], T.fmo[:, 2 * h:2 * h + 8], "rmc", tfb, tfs)
+    oc = take("cs", 2)
+    tcb = on_scalar(T.kb2[:, :], 256, lambda i: T.kl2[:, 1 + i:2 + i], 2, T.cs, oc, tkb2, tkl2)
+    fslr, fsrf = flags("s", MS, ot1, 128, arm)
+    fslb, fsbf = flags("s", MS, T.tabb[:, :], 256, brm)
+    s_, tcv = on_vector(T.kb2[:, :], 256, lambda i: T.kl2[:, i:i + 1], 1, tkb2, tkl2)
+    need("v", tof)
+    a = mark("v", V.tensor_scalar(cdl, cof2, 256.0, cnp2, A.add, A.subtract))
+    need("v", a, tba)
+    a = mark("v", V.tensor_scalar(T.ba[:, 6:9], T.ba[:, 0:3], cnp2, cdl, A.is_ge, A.mult))
+    need("v", a)
+    tb = mark("v", V.tensor_tensor(T.ba[:, 9:12], T.ba[:, 3:6], T.ba[:, 6:9], A.add))
+    need("v", tcv, tb, trr)
+    a = mark("v", V.tensor_scalar(T.rr[:, 32:33], s_, T.ba[:, 9:10], -256.0, A.add, A.add))
+    tq2 = quant("c2", 224, 352)
+    need("v", tcb)
+    b = mark("v", V.tensor_tensor(T.rr[:, 33:35], T.cs[:, oc:oc + 2], T.ba[:, 10:12], A.add))
+    tt2 = turn(T.t2, 1, 3, 32, 128.0, a, b)
+    l1a = [arrived(k, peer[1]) for k in ("e1c", "e1s", "l1c", "l1s")]
+    p2 = pick("sl2", 0, L2, "c2", 232, T.t2[:, :], tt2, tq2, pp[0], pp[1], *l1a)
+    ship(peer[2], "a2", E2, 128, "sl2", 0, L2, "l2", p2)
+
+    tno = on_scalar(T.kso[:, :], 128, kgc(2), 2, T.rr, 66, tso, tkg, trr)
+    fsr = scan(inc("sr"), fslr, 128, 0.0, fsrf)
+    tks1 = held(B0, ot1, inc("sr"), T.ks1[:, :], fsr, arm)
+    tn1 = on_scalar(T.ks1[:, :], 128, kgc(0), 2, T.rr, 68, tks1, tkg, trr)
+    fsb = scan(inc("sb", 256), fslb, 256, 0.0, fsbf)
+    tkbs = held(B1, T.tabb[:, :], inc("sb", 256), T.kbs[:, :], fsb, brm)
+    need("s", tso, fsr, fsb)
+    mark("s", SC.activation(rc_(0), T.kso[:, 127:128], F.Copy))
+    mark("s", SC.activation(rc_(1), last("sr"), F.Copy))
+    mark("s", SC.activation(rc_(2), last("sb"), F.Copy))
+    tr2 = mark("s", SC.activation(rc_(3), last("sb"), F.Identity, bias=last("sb", 256), scale=-1.0))
+    tl2 = mark("s", SC.activation(T.lnb[0:1, 1:2], T.kso[0:1, 127:128], F.Copy))
+    tn2 = on_scalar(T.kbs[:, :], 256, kgc(0), 3, T.rr, 70, tkbs, tkg, trr)
+    need("v", ("lw", 16))
+    tqw = mark("v", V.quantize_mx(T.wqc[:, :], T.wqs[:, :], T.wt[:, :]))
+    need("v", tof, tcn)
+    tnc = mark("v", V.tensor_scalar(T.nc[:, 6:9], T.nc[:, 9:12], cof2, None, A.add))
+    need("v", tk8, tkf)
+    tk8 = mark("v", V.tensor_scalar(T.k8[:, :], T.k8a[:, :], T.kf[:, 0:1], None, A.add))
+    a = mark("v", V.tensor_scalar(T.z7[:, :], T.zi[:, 0:8], 7, None, A.bitwise_and))
+    need("v", a)
+    to8 = mark("v", V.tensor_copy(T.o8[:, :], T.z7[:, :]))
+    tr1 = mark("v", V.tensor_scalar(rb_(3), last("sb"), 192.0, None, A.add))
+
+    need("v", arrived("rmc", peer[2]), tr1, tr2, tcg)
+    tsx = mark("v", V.tensor_tensor_scan(T.sx[:, 8:16], T.sg[:, 0:8], T.run[:, 4:12], 0.0, A.mult, A.add))
+    need("v", tsx)
+    mark("v", V.tensor_tensor(T.dz[:, 0:4], T.run[:, 0:4], T.sx[:, 7:11], A.subtract))
+    b = mark("v", V.tensor_tensor(T.dz[:, 4:8], T.run[:, 12:16], T.sx[:, 11:15], A.subtract))
+    need("v", b)
+    tdd = mark("v", V.tensor_tensor(T.dd[:, 0:7], T.dz[:, 1:8], T.dz[:, 0:7], A.subtract))
+
+    need("v", tnc, tno, tn1, tn2)
+    a = mark("v", V.tensor_tensor(T.rr[:, 96:105], T.rr[:, 64:73], T.nc[:, 0:9], A.add))
+    tn = turn(T.tn, 2, 9, 96, 0.0, a)
+    na = pick("nn", 0, 192, "c1", 200, T.tn[:, 0:12], tn, tq1, *h0a)
+    nb = pick("nn", 192, 288, "c2", 232, T.tn[:, 12:18], tn, tq2, pp[0], pp[1], *l1a)
+
+    def product(o, bank, c, n, *deps):
+        need("t", tqw, *deps)
+        return mark("t", TE.matmul_mx(T.ps[:, 512 * bank:512 * bank + n], T.wqc[:, 128 * o:128 * o + 128], T.wqs[:, 128 * o:128 * o + 128],
+                                      T[c + "c"][:, 0:n], T[c + "s"][:, 0:n], True, True))
+    m0 = product(0, 0, "nn", 288, na[0], na[1], nb[0], nb[1])
+    m1 = product(1, 1, "nn", 288)
+    need("s", m0)
+    g0a = mark("s", SC.activation(T.g0[:, 0:288], T.ps[:, 0:288], F.Copy))
+    need("s", m1)
+    g1a = mark("s", SC.activation(T.g1[:, 0:288], T.ps[:, 512:800], F.Copy))
+
+    need("s", tsx)
+    tln = mark("s", SC.activation(T.lnb[0:1, 0:1], T.sx[0:1, 15:16], F.Copy))
+    need("v", to8, tk8)
+    c = mark("v", V.tensor_tensor(T.tm[:, 0:128], T.sx[:, 8:16].indirect(T.o8[:, :]), T.k8[:, :], A.is_le))
+    need("v", c, tdd)
+    a = mark("v", V.tensor_tensor(T.tm[:, 128:256], T.dd[:, 0:8].indirect(T.o8[:, :]), T.tm[:, 0:128], A.mult))
+    need("v", a, ts8)
+    a = mark("v", V.tensor_tensor_scan(T.tm[:, 256:384], T.s8[:, :], T.tm[:, 128:256], 0.0, A.mult, A.add))
+    need("v", a)
+    a = mark("v", V.tensor_tensor(T.tg[:, :], T.tm[:, 263:384:8], T.kq[:, :], A.add))
+    need("v", a)
+    ttf = mark("v", V.tensor_scalar(T.tf[:, :], T.tg[:, :], T.dz[:, 0:1], 416.0, A.add, A.min))
+
+    l2a = [arrived(k, peer[2]) for k in ("e2c", "e2s", "l2c", "l2s")]
+    m2 = product(0, 2, "a2", 128, *l2a)
+    m3 = product(1, 3, "a2", 128)
+    need("v", m2)
+    b0 = mark("v", V.tensor_copy(T.g0[:, 288:416], T.ps[:, 1024:1152]))
+    need("s", m3)
+    b1 = mark("s", SC.activation(T.g1[:, 288:416], T.ps[:, 1536:1664], F.Copy))
+    need("v", b0, g0a, tcg, ttf)
+    y0 = mark("v", V.tensor_copy(T.y0[:, :], T.g0[:, :].indirect(T.tf[:, :])))
+    need("s", b1, g1a, tcg, ttf)
+    y1 = mark("s", SC.activation(T.y1[:, :], T.g1[:, :].indirect(T.tf[:, :]), F.Copy))
+    need("y", tln, tl2)
+    g.sync.dma_start(T.ln[:, :], T.lnb[:, :]).then_inc(T.sem.sln, 16)
+    need("y", y0)
+    g.sync.dma_start(T.y[:, 0:S], T.y0[:, :]).then_inc(T.sem.sya, 16)
+    need("s", y1)
+    SC.dma_start(T.y[:, S:2 * S], T.y1[:, :]).then_inc(T.sem.syb, 16)
+
+    need("p", ("loc", sent[0]), ("qv", done["v"]), ("qs", done["s"]), ("qt", done["t"]), ("qp", done["p"]))
+    need("y", ("sln", 16), ("sya", 16))
+    need("s", ("syb", 16))

@@ -1,3 +1,4 @@
+from concourse.bass import DstId, RemoteDMATransfer
 from concourse.mybir import dt, AluOpType, ActivationFunctionType
 
 A = AluOpType
@@ -5,58 +6,60 @@ F = ActivationFunctionType
 U8, U32 = dt.uint8, dt.uint32
 N, COLS, S = 8, 128, 256
 BIG = 1024.0
-H0, E1, L1, E2, L2 = 64, 32, 64, 32, 96
+H0, H1, H2 = 64, 96, 128
+PAIR = COLS + H0
+NEAR = PAIR + H1
+ZERO = NEAR + H2
 
 CODE, PLANE = "float8_e4m3fn_x4", "uint8"
 SCRATCH = {
     "dmi": ("sbuf", [128, 8], "int32"), "xt": ("sbuf", [128, 512], "bfloat16"), "wt": ("sbuf", [128, 1024], "bfloat16"),
-    "c0c": ("sbuf", [128, 128], CODE), "c0s": ("sbuf", [128, 128], PLANE),
-    "c1c": ("sbuf", [128, 320], CODE), "c1s": ("sbuf", [128, 320], PLANE),
-    "c2c": ("sbuf", [128, 352], CODE), "c2s": ("sbuf", [128, 352], PLANE),
-    "a2c": ("sbuf", [128, 128], CODE), "a2s": ("sbuf", [128, 128], PLANE),
-    "nnc": ("sbuf", [128, 288], CODE), "nns": ("sbuf", [128, 288], PLANE),
+    "c0c": ("sbuf", [128, COLS], CODE), "c0s": ("sbuf", [128, COLS], PLANE),
+    "c1c": ("sbuf", [128, PAIR], CODE), "c1s": ("sbuf", [128, PAIR], PLANE),
+    "c2c": ("sbuf", [128, NEAR], CODE), "c2s": ("sbuf", [128, NEAR], PLANE),
+    "a2c": ("sbuf", [128, H2], CODE), "a2s": ("sbuf", [128, H2], PLANE),
     "wqc": ("sbuf", [128, 256], CODE), "wqs": ("sbuf", [128, 256], PLANE),
     "sl0c": ("sbuf", [128, H0], CODE), "sl0s": ("sbuf", [128, H0], PLANE),
-    "se1c": ("sbuf", [128, E1], CODE), "se1s": ("sbuf", [128, E1], PLANE),
-    "sl1c": ("sbuf", [128, L1], CODE), "sl1s": ("sbuf", [128, L1], PLANE),
-    "sl2c": ("sbuf", [128, L2], CODE), "sl2s": ("sbuf", [128, L2], PLANE),
-    "pair": ("sbuf", [128, 16], "uint16"), "tabb": ("sbuf", [128, 16], "uint16"),
-    "run": ("sbuf", [128, 16], "float32"), "fmo": ("sbuf", [128, 16], "float32"),
-    "lv": ("sbuf", [128, 256], "int32"), "zi": ("sbuf", [128, 16], "int32"), "zr": ("sbuf", [128, 16], "int32"),
-    "zm": ("sbuf", [128, 16], "int32"), "kq": ("sbuf", [128, 16], "float32"), "kf": ("sbuf", [128, 16], "float32"),
-    "gr": ("sbuf", [128, 8], "int32"), "gm": ("sbuf", [128, 8], "int32"), "gq": ("sbuf", [128, 8], "float32"),
-    "kg": ("sbuf", [128, 8], "float32"), "z7": ("sbuf", [128, 8], "int32"), "o8": ("sbuf", [128, 8], "uint16"),
-    "cu": ("sbuf", [128, 4], "uint16"), "k8a": ("sbuf", [128, 128], "float32"), "k8": ("sbuf", [128, 128], "float32"),
-    "s8": ("sbuf", [128, 128], "bfloat16"), "b1a": ("sbuf", [128, 256], "bfloat16"),
-    "la": ("sbuf", [128, 3 * 256], "int32"), "lut": ("sbuf", [128, 6 * 256], "bfloat16"), "sg": ("sbuf", [128, 512], "bfloat16"),
-    "fl": ("sbuf", [128, 2048], "bfloat16"), "inc": ("sbuf", [128, 1024], "bfloat16"),
-    "k0": ("sbuf", [128, 128], "bfloat16"), "k1": ("sbuf", [128, 256], "bfloat16"), "k2": ("sbuf", [128, 256], "bfloat16"),
-    "kso": ("sbuf", [128, 128], "bfloat16"), "ks1": ("sbuf", [128, 128], "bfloat16"),
-    "kb2": ("sbuf", [128, 256], "bfloat16"), "kbs": ("sbuf", [128, 256], "bfloat16"), "prs": ("sbuf", [128, 256], "bfloat16"),
-    "js": ("sbuf", [128, 8192], "bfloat16"), "jv": ("sbuf", [128, 4096], "bfloat16"), "jw": ("sbuf", [128, 4096], "bfloat16"),
-    "cs": ("sbuf", [128, 16], "float32"), "rr": ("sbuf", [128, 128], "float32"), "ra": ("sbuf", [128, 96], "float32"),
-    "rb": ("sbuf", [128, 192], "float32"), "rc": ("sbuf", [128, 192], "float32"),
-    "col": ("sbuf", [128, 16], "float32"), "ke": ("sbuf", [128, 2], "float32"), "kl": ("sbuf", [128, 4], "float32"),
-    "kl2": ("sbuf", [128, 3], "float32"), "ba": ("sbuf", [128, 12], "float32"), "nc": ("sbuf", [128, 12], "float32"),
-    "sx": ("sbuf", [128, 16], "float32"), "dz": ("sbuf", [128, 8], "float32"), "dd": ("sbuf", [128, 8], "float32"),
-    "tm": ("sbuf", [128, 384], "float32"), "tg": ("sbuf", [128, 16], "float32"), "lnb": ("sbuf", [1, 2], "float32"),
-    "t0": ("sbuf", [128, 4], "uint16"), "te": ("sbuf", [128, 2], "uint16"), "t1": ("sbuf", [128, 4], "uint16"),
-    "tp": ("sbuf", [128, 8], "uint16"), "t2": ("sbuf", [128, 6], "uint16"), "tn": ("sbuf", [128, 18], "uint16"),
-    "tf": ("sbuf", [128, 16], "uint16"),
-    "g0": ("sbuf", [128, 432], "float32"), "g1": ("sbuf", [128, 432], "float32"),
+    "sl1c": ("sbuf", [128, H1], CODE), "sl1s": ("sbuf", [128, H1], PLANE),
+    "sl2c": ("sbuf", [128, H2], CODE), "sl2s": ("sbuf", [128, H2], PLANE),
+    "tab": ("sbuf", [128, 32], "uint16"), "lt1": ("sbuf", [128, 4], "uint16"), "lt3": ("sbuf", [128, 4], "uint16"),
+    "lt2": ("sbuf", [128, 6], "uint16"), "nfa": ("sbuf", [128, 1], "float32"), "nfo": ("sbuf", [128, 1], "float32"),
+    "lv": ("sbuf", [128, 256], "int32"), "zi": ("sbuf", [128, 2], "int32"), "za": ("sbuf", [128, 2], "int32"),
+    "zb": ("sbuf", [128, 2], "int32"), "ra16": ("sbuf", [128, 1], "float32"), "ra32": ("sbuf", [128, 1], "float32"),
+    "b16": ("sbuf", [128, 8], "float32"), "b32": ("sbuf", [128, 8], "float32"), "kf": ("sbuf", [128, 8], "float32"),
+    "kg": ("sbuf", [128, 8], "float32"), "ki": ("sbuf", [128, 8], "float32"), "cu": ("sbuf", [128, 4], "uint16"),
+    "la": ("sbuf", [128, 768], "int32"), "lut": ("sbuf", [128, 1024], "bfloat16"),
+    "one": ("sbuf", [128, 128], "bfloat16"), "sgc": ("sbuf", [128, 4 * PAIR], "bfloat16"), "sgd": ("sbuf", [128, 4 * H1], "bfloat16"),
+    "sge": ("sbuf", [128, 4 * NEAR], "bfloat16"),
+    "f0": ("sbuf", [128, 128], "bfloat16"), "f1": ("sbuf", [128, 256], "bfloat16"), "f2": ("sbuf", [128, 512], "bfloat16"),
+    "fs": ("sbuf", [128, 512], "bfloat16"), "k0": ("sbuf", [128, 128], "bfloat16"),
+    "k1": ("sbuf", [128, PAIR], "bfloat16"), "r1": ("sbuf", [128, 128], "bfloat16"),
+    "k2": ("sbuf", [128, NEAR], "bfloat16"), "r2": ("sbuf", [128, 128], "bfloat16"), "w2": ("sbuf", [128, PAIR], "bfloat16"),
+    "x2": ("sbuf", [128, 128], "bfloat16"), "ks": ("sbuf", [128, NEAR], "bfloat16"), "rs": ("sbuf", [128, 128], "bfloat16"),
+    "ws": ("sbuf", [128, PAIR], "bfloat16"), "xs": ("sbuf", [128, 128], "bfloat16"),
+    "js": ("sbuf", [128, 4096], "bfloat16"), "jv": ("sbuf", [128, 4096], "bfloat16"), "jw": ("sbuf", [128, 4096], "bfloat16"),
+    "cs": ("sbuf", [128, 20], "float32"), "hs": ("sbuf", [128, 4], "float32"), "rr": ("sbuf", [128, 32], "float32"),
+    "ra": ("sbuf", [128, 32], "float32"), "rb": ("sbuf", [128, 64], "float32"), "rc": ("sbuf", [128, 64], "float32"),
+    "ad": ("sbuf", [128, 8], "float32"),
+    "ke": ("sbuf", [128, 8], "float32"), "na": ("sbuf", [128, 1], "float32"), "nd": ("sbuf", [128, 1], "float32"),
+    "ga": ("sbuf", [128, 8], "float32"), "gb": ("sbuf", [128, 8], "float32"), "gw": ("sbuf", [128, 8], "float32"),
+    "gd": ("sbuf", [128, 8], "float32"), "gt": ("sbuf", [128, 8], "float32"),
+    "t0": ("sbuf", [128, 4], "uint16"), "t1": ("sbuf", [128, 6], "uint16"), "t2": ("sbuf", [128, 8], "uint16"),
+    "tf": ("sbuf", [128, 16], "uint16"), "lnb": ("sbuf", [1, 2], "float32"),
+    "g0": ("sbuf", [128, ZERO + 16], "float32"), "g1": ("sbuf", [128, ZERO + 16], "float32"),
     "y0": ("sbuf", [128, 256], "float32"), "y1": ("sbuf", [128, 256], "float32"),
     "ps": ("psum", [128, 2048], "float32"),
 }
-ARR = ["rma", "rmb", "rmc", "h0c", "h0s", "e1c", "e1s", "l1c", "l1s", "e2c", "e2s", "l2c", "l2s"]
-SEMAPHORES = ["qv", "qs", "qt", "qp", "ld", "lx", "lw", "sya", "syb", "sln", "loc"] + ARR
+ARR = ["rm", "la0", "la1", "nf", "h0c", "h0s", "h1c", "h1s", "h2c", "h2s"]
+SEMAPHORES = ["qv", "qs", "qt", "qp", "ld", "lx", "lw", "cp1", "cp2", "sya", "syb", "sln", "loc"] + ARR
 
 
 def rank_program(g, core, T, topo):
     q = T.rank_of(core)
     if q is None:
         return
-    V, SC, TE = g.vector, g.scalar, g.tensor
-    queue = {"v": V, "s": SC, "t": TE, "p": g, "y": g.sync}
+    V, SC, TE, Y = g.vector, g.scalar, g.tensor, g.sync
+    queue = {"v": V, "s": SC, "t": TE, "p": g, "y": Y}
     done = {"v": 0, "s": 0, "t": 0, "p": 0}
     seen = {}
 
@@ -82,363 +85,317 @@ def rank_program(g, core, T, topo):
         g.remote_dma(out, in_, T.sem[sem], T.sem["loc"], pid, rid, topo.mask(core, dst))
         sent[0] += len(topo.engines(core, dst))
 
-    def arrived(sem, src):
-        return (sem, len(topo.engines(src, core)))
+    def spread(dsts, outs, in_, sem, *deps):
+        need("p", *deps)
+        ids = []
+        m = topo.mask(core, dsts[0])
+        for d in dsts:
+            rid, pid = topo.addr(d, core)
+            ids.append(DstId(rid=rid, pnc=pid))
+            m &= topo.mask(core, d)
+        g.remote_dma_fused([RemoteDMATransfer(dst_ids=ids, dma_engine_mask=m, remote_sem=T.sem[sem], srcs=[in_], dsts=outs)],
+                           local_sem=T.sem["loc"])
+        sent[0] += bin(m).count("1")
 
-    peer = [T.cores[q ^ (1 << b)] for b in range(3)]
+    def arrived(sem, *srcs):
+        return (sem, sum(len(topo.engines(s, core)) for s in srcs))
+
+    at = lambda x: T.cores[q ^ x]
     codes = lambda t, a, b: t[:, a:b].bitcast(U8)
-    words = lambda t, a, b: t[:, a:b].bitcast(U32)
+
+    r, hi, up, far = q & 3, q & 1, (q >> 1) & 1, q >> 2
+    po, ps = H0 * hi, COLS * (1 - hi)
+    cp, cb = H1 * up, PAIR * (1 - up)
+    gn, gf = H2 * far, NEAR * (1 - far)
+    mask_of = lambda x: T.tab[:, 8 * (r ^ x):8 * (r ^ x) + 8]
+    run = lambda t, x: t[:, 128 * (r ^ x):128 * (r ^ x) + 128]
+    t2a = 16 * (1 - up)
+    mask_2 = T.tab[:, t2a:t2a + 16]
+    run_2 = lambda t: t[:, 16 * t2a:16 * t2a + 256]
 
     for i in range(8):
-        (g.sync if i % 2 == 0 else SC).dma_start(T.dmi[16 * i:16 * i + 16, :], T.dm[:, :]).then_inc(T.sem.ld, 16)
-    g.sync.dma_start(T.xt[:, :], T.x[:, :]).then_inc(T.sem.lx, 16)
+        (Y if i % 2 == 0 else SC).dma_start(T.dmi[16 * i:16 * i + 16, :], T.dm[:, :]).then_inc(T.sem.ld, 16)
+    Y.dma_start(T.xt[:, :], T.x[:, :]).then_inc(T.sem.lx, 16)
 
-    odd = sum(1 << r for r in range(N) if (r ^ q) & 1)
-    even = sum(1 << r for r in range(N) if not (r ^ q) & 1)
-    bit = lambda r: 1 << r
-
-    def iota(o, pat, base=0):
-        return mark("p", g.iota(o, pat, base, 0, allow_small_or_imprecise_dtypes=True))
-    tlv = mark("p", g.iota(T.lv[:, :], [[1, 256]], 0, 0))
-    tzi = mark("p", g.iota(T.zi[:, :], [[128, 16]], 0, 1))
-    M0, M1, M2, MS, B0, B1 = range(6)
-    tl = {}
     look = lambda l: T.lut[:, 256 * l:256 * l + 256]
-    bits = lambda r, c: [[0, 256 >> (r + 1)], [c, 2], [0, 1 << r]]
+    M0, M1, MS, M2 = range(4)
+    tl = {}
+    iota = lambda o, pat: mark("p", g.iota(o, pat, 0, 0, allow_small_or_imprecise_dtypes=True))
+    tlv = mark("p", g.iota(T.lv[:, :], [[1, 256]], 0, 0))
+    tzi = mark("p", g.iota(T.zi[:, :], [[0, 2]], 0, 1))
+    tb16 = iota(T.b16[:, :], [[16, 8]])
+    e_ = q ^ 4
+    tl[M2] = iota(look(M2), [[0, 256 >> (e_ + 1)], [1, 2], [0, 1 << e_]])
 
-    def lut(i, j, m, absent):
+    def lut(l, ranks):
+        m = sum(1 << e for e in ranks)
         need("v", tlv)
-        a = mark("v", V.tensor_scalar(T.la[:, 256 * j:256 * j + 256], T.lv[:, :], m, None, A.bitwise_and))
+        a = mark("v", V.tensor_scalar(T.la[:, 256 * l:256 * l + 256], T.lv[:, :], m, None, A.bitwise_and))
         need("v", a)
-        i_ = T.la[:, 256 * j:256 * j + 256]
-        if absent:
-            return mark("v", V.tensor_scalar(look(i), i_, 0.0, BIG, A.is_equal, A.mult))
-        return mark("v", V.tensor_scalar(look(i), i_, 0.0, None, A.is_gt))
-    a = mark("v", V.memset(T.sg[:, :], 1.0))
-    need("v", a)
-    tsg = mark("v", V.memset(T.sg[:, 256:257], 0.0))
-    tl[M0] = lut(M0, 0, odd, False)
-    need("v", tzi)
-    tzr = mark("v", V.tensor_scalar(T.zr[:, :], T.zi[:, :], 15, None, A.bitwise_and))
-    a = mark("v", V.tensor_scalar(T.zm[:, :], T.zi[:, :], 3, 240, A.logical_shift_right, A.bitwise_and))
-    need("v", a, tzr)
-    tkq = mark("v", V.tensor_tensor(T.kq[:, :], T.zr[:, :], T.zm[:, :], A.add))
-    need("v", tkq)
-    tkf = mark("v", V.tensor_scalar(T.kf[:, :], T.kq[:, :], 0.5, None, A.add))
-    mark("v", V.tensor_scalar(T.gr[:, :], T.zi[:, 0:8], 31, None, A.bitwise_and))
-    a = mark("v", V.tensor_scalar(T.gm[:, :], T.zi[:, 0:8], 2, 224, A.logical_shift_right, A.bitwise_and))
-    need("v", a)
-    a = mark("v", V.tensor_tensor(T.gq[:, :], T.gr[:, :], T.gm[:, :], A.add))
-    need("v", a)
-    tkg = mark("v", V.tensor_scalar(T.kg[:, :], T.gq[:, :], 0.5, None, A.add))
-    tl[M2] = iota(look(M2), bits(q ^ 4, 1))
-    tl[MS] = iota(look(MS), bits(q, 1))
+        tl[l] = mark("v", V.tensor_scalar(look(l), T.la[:, 256 * l:256 * l + 256], 0.0, None, A.is_gt))
 
-    use = {"js": 0, "jv": 0, "cs": 0, "fl": 0}
+    tone = mark("v", V.memset(T.one[:, :], 1.0))
+    lut(M0, [e for e in range(N) if (e ^ q) & 1])
+    need("v", tzi)
+    tza = mark("v", V.tensor_scalar(T.za[:, :], T.zi[:, :], 15, None, A.bitwise_and))
+    need("v", tza)
+    a = mark("v", V.tensor_scalar(T.ra16[:, :], T.za[:, 0:1], 0.5, None, A.add))
+    need("s", a, tb16)
+    tkf = mark("s", SC.activation(T.kf[:, :], T.b16[:, :], F.Identity, bias=T.ra16[:, :]))
+
+    use = {"js": 0, "jv": 0, "cs": 0}
 
     def take(name, n):
         o = use[name]
         use[name] += n
         return o
 
-    def scan(out, fl, n, init, *deps):
-        need("v", tsg, *deps)
-        return mark("v", V.tensor_tensor_scan(out, T.sg[:, 0:n], fl, init, A.mult, A.add))
+    def scan(out, fl, init, *deps):
+        need("v", tone, *deps)
+        return mark("v", V.tensor_tensor_scan(out, T.one[:, :], fl, init, A.mult, A.add))
 
-    def flags(e, l, tab, n, *deps):
-        o = take("fl", n)
+    def flags(e, out, l, tab, *deps):
         need(e, tl[l], *deps)
-        out, src = T.fl[:, o:o + n], look(l).indirect(tab)
         if e == "v":
-            return out, mark(e, V.tensor_copy(out, src))
-        return out, mark(e, SC.activation(out, src, F.Copy))
+            return mark(e, V.tensor_copy(out, look(l).indirect(tab)))
+        return mark(e, SC.activation(out, look(l).indirect(tab), F.Copy))
 
-    def held(l, tab, inc, out, *deps):
-        need("v", tl[l], *deps)
-        return mark("v", V.tensor_tensor(out, look(l).indirect(tab), inc, A.add))
+    def gather(out, win, tab, *deps):
+        need("s", *deps)
+        return mark("s", SC.activation(out, win.indirect(tab), F.Copy))
 
-    def on_vector(key, n, kcols, nv, *deps):
+    k_ = lambda t, j: (lambda i: t[:, j + i:j + i + 1])
+
+    def on_vector(key, n, kcol, nv, sg, *deps):
         o = take("jv", nv * n)
         need("v", *deps)
         for i in range(nv):
-            a_ = mark("v", V.tensor_scalar(T.jv[:, o + i * n:o + i * n + n], key, kcols(i), 2.0, A.is_le, A.mult))
-        need("v", a_, tsg)
-        sg = T.sg[:, 256 - n:256 - n + nv * n] if nv == 2 else T.sg[:, 0:n]
-        a_ = mark("v", V.tensor_tensor_scan(T.jw[:, o:o + nv * n], sg, T.jv[:, o:o + nv * n], 0.0, A.mult, A.add))
+            a_ = mark("v", V.tensor_scalar(T.jv[:, o + i * n:o + i * n + n], key, kcol(i), 0.5, A.is_le, A.subtract))
+        need("v", a_)
+        a_ = mark("v", V.tensor_tensor_scan(T.jw[:, o:o + nv * n], sg[:, 0:nv * n], T.jv[:, o:o + nv * n], 0.0, A.mult, A.add))
         return T.jw[:, o + n - 1:o + nv * n:n], a_
 
-    def on_scalar(key, n, kcols, ns, out, at, *deps):
+    def on_scalar(key, n, kcol, ns, *deps):
+        o_ = take("cs", ns)
         need("s", *deps)
         for i in range(ns):
             o = take("js", n)
-            a_ = mark("s", SC.activation(T.js[:, o:o + n], key, F.Sign, bias=kcols(i), scale=-1.0, accum_out=out[:, at + i:at + i + 1]))
-        return a_
+            a_ = mark("s", SC.activation(T.js[:, o:o + n], key, F.Sign, bias=kcol(i), scale=-1.0, accum_out=T.cs[:, o_ + i:o_ + i + 1]))
+        return T.cs[:, o_:o_ + ns], a_
 
-    def table(tab, key, n, kt, nv, ns, *deps):
-        o = take("cs", ns)
-        b_ = on_scalar(key, n, lambda i: kt[:, nv + i:nv + i + 1], ns, T.cs, o, *deps)
-        s_, a_ = on_vector(key, n, lambda i: kt[:, i:i + 1], nv, *deps)
-        return (tab, nv, ns, s_, a_, o, b_, n)
+    def table(tab, key, n, nv, ns, sg, *deps):
+        sb = on_scalar(key[:, 0:n - 1], n - 1, k_(T.kf, nv), ns, tkf, *deps)
+        sa = on_vector(key[:, 0:n], n, k_(T.kf, 0), nv, sg, tkf, *deps)
+        return tab, n, nv, ns, sa, sb
 
-    def finish(tab, nv, ns, s_, a_, o, b_, n):
-        need("v", a_)
-        mark("v", V.tensor_scalar(tab[:, 0:nv], s_, 0.5, None, A.mult))
-        need("v", b_)
-        return mark("v", V.tensor_scalar(tab[:, nv:nv + ns], T.cs[:, o:o + ns], 0.5, n / 2, A.mult, A.add))
+    def finish(tab, n, nv, ns, sa, sb):
+        need("v", sa[1])
+        mark("v", V.tensor_scalar(tab[:, 0:nv], sa[0], n / 2, n - 1.0, A.add, A.min))
+        need("v", sb[1])
+        return mark("v", V.tensor_scalar(tab[:, nv:nv + ns], sb[0], 0.5, (n - 1) / 2, A.mult, A.add))
 
-    def turn(tab, j, n, at, c, *deps):
+    def pick(out, src, n, tab, *deps):
         need("v", *deps)
-        a_ = mark("v", V.transpose(T.ra[:, 32 * j:32 * j + 32], T.rr[:, at:at + 32]))
-        need("v", a_, tcu)
-        a_ = mark("v", V.tensor_copy(T.rb[:, 64 * j:64 * j + 64], T.ra[:, 32 * j:32 * j + 32].indirect(T.cu[:, :])))
-        need("v", a_)
-        a_ = mark("v", V.transpose(T.rc[:, 64 * j:64 * j + 64], T.rb[:, 64 * j:64 * j + 64]))
-        need("v", a_)
-        mark("v", V.tensor_scalar(tab[:, 0:2 * n:2], T.rc[:, 64 * j:64 * j + n], 0.5, c, A.mult, A.add))
-        return mark("v", V.tensor_scalar(tab[:, 1:2 * n:2], T.rc[:, 64 * j + 32:64 * j + 32 + n], 0.5, c, A.mult, A.add))
-
-    def pick(out, oa, ob, src, n, tab, *deps):
-        need("v", *deps)
-        a_ = mark("v", V.tensor_copy(words(T[out + "c"], oa, ob), words(T[src + "c"], 0, n).indirect(tab)))
+        a_ = mark("v", V.tensor_copy(T[out + "c"][:, 0:n].bitcast(U32), T[src + "c"][:, :].bitcast(U32).indirect(tab)))
         need("s", *deps)
-        b_ = mark("s", SC.activation(T[out + "s"][:, oa:ob], T[src + "s"][:, 0:n].indirect(tab), F.Copy))
+        b_ = mark("s", SC.activation(T[out + "s"][:, 0:n], T[src + "s"][:, :].indirect(tab), F.Copy))
         return a_, b_
 
-    def quant(c, a_, b_):
-        return mark("v", V.quantize_mx(T[c + "c"][:, a_:b_], T[c + "s"][:, a_:b_], T.xt[:, :]))
-
-    def ship(dst, to, a_, b_, src, sa, sb, sem, tok):
-        send(dst, codes(T[to + "c"], a_, b_), codes(T[src + "c"], sa, sb), sem + "c", tok[0])
-        send(dst, T[to + "s"][:, a_:b_], T[src + "s"][:, sa:sb], sem + "s", tok[1])
-
-    own, ot1 = T.pair[:, 0:8], T.pair[:, 8:16]
-    INC = {"1r": 0, "2r": 128, "sr": 256, "2b": 384, "sb": 640}
-    inc = lambda k, n=128: T.inc[:, INC[k]:INC[k] + n]
-    last = lambda k, n=128: T.inc[:, INC[k] + n - 1:INC[k] + n]
-    col = lambda i: T.col[:, i:i + 1]
-    kgc = lambda o: (lambda i: T.kg[:, o + i:o + i + 1])
+    def ship(dst, to, a_, src, n, sem, tok):
+        send(dst, codes(T[to + "c"], a_, a_ + n), codes(T[src + "c"], 0, n), sem + "c", tok[0])
+        send(dst, T[to + "s"][:, a_:a_ + n], T[src + "s"][:, 0:n], sem + "s", tok[1])
 
     need("v", ("ld", 128))
-    tpo = mark("v", V.tensor_copy(own, T.dmi[:, :]))
-    send(peer[0], T.pair[:, 8:16], own, "rma", tpo)
+    tpo = mark("v", V.tensor_copy(mask_of(0), T.dmi[:, :]))
+    spread([at(1), at(2), at(3)], [mask_of(0)] * 3, mask_of(0), "rm", tpo)
 
-    f0, f = flags("v", M0, own, 128, tpo)
-    ti = scan(T.k0[:, :], f0, 128, 0.0, f)
-    c0 = table(T.t0, T.k0[:, 0:127], 127, T.kf, 1, 3, ti, tkf)
+    f = flags("v", T.f0[:, :], M0, mask_of(0), tpo)
+    ti = scan(T.k0[:, :], T.f0[:, :], 0.0, f)
+    c0 = table(T.t0, T.k0, COLS, 1, 3, T.one, ti)
     need("v", ("lx", 16))
-    tq0 = quant("c0", 0, 128)
+    tq0 = mark("v", V.quantize_mx(T.c0c[:, :], T.c0s[:, :], T.xt[:, :]))
     t0 = finish(*c0)
-    p0 = pick("sl0", 0, H0, "c0", 128, T.t0[:, :], t0, tq0)
-    ship(peer[0], "c1", 128, 128 + H0, "sl0", 0, H0, "h0", p0)
+    spread([at(1), at(3)], [T.lt1[:, :], T.lt3[:, :]], T.t0[:, :], "la0", t0)
+    p0 = pick("sl0", "c0", H0, T.t0[:, :], t0, tq0)
+    ship(at(1), "c1", COLS * hi, "sl0", H0, "h0", p0)
+    tb32 = iota(T.b32[:, :], [[32, 8]])
 
-    h = 4 * (q >> 2)
-    cnt_at = lambda r: 4 + r
-    bas_at = lambda r: r if r < 4 else 8 + r
-    near = lambda x: h + ((q & 3) ^ x)
-    rc_ = lambda x: T.run[:, cnt_at(near(x)):cnt_at(near(x)) + 1]
-    rb_ = lambda x: T.run[:, bas_at(near(x)):bas_at(near(x)) + 1]
-    need("s", tkf)
-    const = lambda o, n, c: mark("s", SC.activation(o, T.kf[:, 0:n], F.Copy, bias=c, scale=0.0))
-    const(T.sx[:, 7:8], 1, 0.0)
-    const(T.dd[:, 7:8], 1, 4096.0)
-    for x in range(3):
-        const(rb_(x), 1, (0.0, 128.0, 192.0)[x])
-    const(T.g0[:, 416:432], 16, 0.0)
-    tcg = const(T.g1[:, 416:432], 16, 0.0)
+    need("y", tq0)
+    Y.dma_start(codes(T.c1c, po, po + COLS), codes(T.c0c, 0, COLS)).then_inc(T.sem.cp1, 16)
+    Y.dma_start(T.c1s[:, po:po + COLS], T.c0s[:, :]).then_inc(T.sem.cp1, 16)
+    Y.dma_start(codes(T.c2c, cp + po, cp + po + COLS), codes(T.c0c, 0, COLS)).then_inc(T.sem.cp2, 16)
+    Y.dma_start(T.c2s[:, cp + po:cp + po + COLS], T.c0s[:, :]).then_inc(T.sem.cp2, 16)
+    Y.dma_start(T.wt[:, :], T.w[:, :]).then_inc(T.sem.lw, 16)
+    h0a = [arrived("h0c", at(1)), arrived("h0s", at(1))]
+    need("y", *h0a)
+    Y.dma_start(codes(T.c2c, cp + ps, cp + ps + H0), codes(T.c1c, ps, ps + H0)).then_inc(T.sem.cp2, 16)
+    Y.dma_start(T.c2s[:, cp + ps:cp + ps + H0], T.c1s[:, ps:ps + H0]).then_inc(T.sem.cp2, 16)
+    w1, w2 = ("cp1", 32), ("cp2", 64)
 
-    tl[M1] = lut(M1, 1, bit(q ^ 2) | bit(q ^ 6), False)
-    f1fl, f1f = flags("s", M1, own, 128, tpo)
-    quant("c1", 0, 128)
-    tq1 = quant("c1", 192, 320)
-    t1o = scan(T.k1[:, 0:128], f1fl, 128, 0.0, f1f)
-    n1o = T.k1[:, 127:128]
-    need("v", t1o)
-    ta = mark("v", V.tensor_scalar(col(0), n1o, float(E1), None, A.min))
-    need("v", ta, tkf)
-    tke = mark("v", V.tensor_scalar(T.ke[:, :], T.kf[:, 0:2], col(0), -float(E1), A.add, A.add))
-    tkl = mark("v", V.tensor_scalar(T.kl[:, :], T.kf[:, 0:4], col(0), None, A.add))
-    ce = table(T.te, T.k1[:, 0:127], 127, T.ke, 1, 1, t1o, tke)
-    te = finish(*ce)
-    pe = pick("se1", 0, E1, "c0", 128, T.te[:, :], te, tq0)
-    ship(peer[1], "c2", 128, 128 + E1, "se1", 0, E1, "e1", pe)
-    need("y", pe[0])
-    g.sync.dma_start(T.wt[:, :], T.w[:, :]).then_inc(T.sem.lw, 16)
+    def resets(t, n, c):
+        a_ = mark("v", V.memset(t[:, :], 1.0))
+        need("v", a_)
+        return mark("v", V.memset(t[:, 0:c * n:n], 0.0))
 
-    arm = arrived("rma", peer[0])
-    send(peer[1], T.tabb[:, :], T.pair[:, :], "rmb", arm, tpo)
-    iota(T.nc[:, 0:4], [[0, 4]], 128)
-    iota(T.nc[:, 4:6], [[0, 2]], 384)
-    tcn = iota(T.nc[:, 9:12], [[0, 3]], 512)
-    tk8 = iota(T.k8a[:, :], [[16, 16], [0, 8]])
-    need("p", tsg)
-    ts8 = mark("p", g.affine_select(T.s8[:, :], T.sg[:, 0:128], [[0, 16], [1, 8]], A.not_equal, 0.0, 0, 0))
+    lut(M1, [q ^ 2, q ^ 6])
+    half = lambda h: T.f1[:, 128 * h:128 * h + 128]
+    e1 = flags("s", half(hi), M1, mask_of(0), tpo)
+    e2 = flags("s", run(T.f2, 0), M2, mask_of(0), tpo)
+    tsc = resets(T.sgc, PAIR, 4)
+    lut(MS, [q])
+    es = flags("s", run(T.fs, 0), MS, mask_of(0), tpo)
+    mark("v", V.memset(T.g0[:, ZERO:ZERO + 16], 0.0))
+    tz = mark("v", V.memset(T.g1[:, ZERO:ZERO + 16], 0.0))
 
-    tl[B0] = lut(B0, 2, even, True)
-    f2ol, f2o = flags("s", M2, own, 128, tpo)
-    fsol, fso = flags("s", MS, own, 128, tpo)
-    f2fl, f2f = flags("s", M2, ot1, 128, arm)
-    f1l, f = flags("v", M1, ot1, 128, arm)
-    f1r = scan(inc("1r"), f1l, 128, n1o, f, t1o)
-    tk1b = held(B0, ot1, inc("1r"), T.k1[:, 128:256], f1r, arm)
-    c1 = table(T.t1, T.k1[:, :], 256, T.kl, 2, 2, t1o, tk1b, tkl)
-    t2o = scan(T.k2[:, 0:128], f2ol, 128, 0.0, f2o)
-    tso = scan(T.kso[:, :], fsol, 128, 0.0, fso)
-    trr = mark("v", V.memset(T.rr[:, :], 0.0))
-    on_scalar(T.kso[:, :], 128, kgc(0), 2, T.rr, 64, tso, tkg, trr)
-    tt1 = finish(*c1)
-    h0a = [arrived("h0c", peer[0]), arrived("h0s", peer[0])]
-    p1 = pick("sl1", 0, L1, "c1", 200, T.t1[:, :], tt1, tq1, *h0a)
-    ship(peer[1], "c2", 160, 160 + L1, "sl1", 0, L1, "l1", p1)
+    rm = arrived("rm", at(1), at(2), at(3))
+    la0 = arrived("la0", at(1), at(3))
+    la1 = arrived("la1", at(2))
+    d1 = flags("s", half(1 - hi), M1, mask_of(1), rm)
+    init, tok = 0.0, []
+    for h in range(2):
+        b, c = (T.k1, po) if h == hi else (T.r1, 0)
+        tok.append(scan(b[:, c:c + COLS], half(h), init, e1 if h == hi else d1, *tok))
+        init = b[:, c + COLS - 1:c + COLS]
+    d2 = flags("v", run(T.f2, 1), M2, mask_of(1), rm)
+    tk1 = gather(T.k1[:, ps:ps + H0], T.r1[:, :], T.lt1[:, :], la0, *tok)
+    t1 = finish(*table(T.t1, T.k1, PAIR, 3, 3, T.sgc, tk1, tsc, *tok))
+    send(at(2), T.lt2[:, :], T.t1[:, :], "la1", t1)
+    p1 = pick("sl1", "c1", H1, T.t1[:, :], t1, w1, *h0a)
+    ship(at(2), "c2", PAIR * up, "sl1", H1, "h1", p1)
 
-    a = iota(T.b1a[:, :], bits(q, -int(BIG)), int(BIG))
-    need("p", a)
-    tl[B1] = mark("p", g.affine_select(look(B1), T.b1a[:, :], bits(q ^ 4, 1), A.is_equal, 0.0, 0, 0))
+    def sums(fl, k, r_, w, x_, *deps):
+        init, tok, ends = 0.0, list(deps), []
+        for e in range(4):
+            b, c = ((k, cp + po), (r_, 0), (w, po), (x_, 0))[e ^ r]
+            tok.append(scan(b[:, c:c + COLS], run(fl, e ^ r), init, *tok))
+            ends.append((b, c + COLS - 1))
+            init = b[:, c + COLS - 1:c + COLS]
+        return tok[-1], ends
 
-    f2r = scan(inc("2r"), f2fl, 128, T.k2[:, 127:128], f2f, t2o)
-    tk2 = held(B0, ot1, inc("2r"), T.k2[:, 128:256], f2r, arm)
-    tcp = on_scalar(T.k2[:, :], 256, kgc(1), 3, T.rr, 1, t2o, tk2, tkg, trr)
-    s_, a = on_vector(T.k2[:, :], 256, kgc(0), 1, tk2, tkg)
-    need("v", a, trr)
-    tcv = mark("v", V.tensor_scalar(T.rr[:, 0:1], s_, -256.0, None, A.add))
-    brm = arrived("rmb", peer[1])
-    np_ = last("2r")
-    need("v", f2r)
-    ta = mark("v", V.tensor_scalar(col(1), np_, float(E2), None, A.min))
-    need("v", ta)
-    tkl2 = mark("v", V.tensor_scalar(T.kl2[:, :], T.kg[:, 0:3], col(1), None, A.add))
-    fc = lambda x: T.fmo[:, cnt_at(near(x)):cnt_at(near(x)) + 1]
-    fb = lambda x: T.fmo[:, bas_at(near(x)):bas_at(near(x)) + 1]
-    c_1, c_3, c_4 = T.k2[:, 127:128], T.inc[:, INC["2b"] + 127:INC["2b"] + 128], T.inc[:, INC["2b"] + 255:INC["2b"] + 256]
-    mark("v", V.memset(fb(0), 288.0))
-    mark("v", V.tensor_scalar(fb(1), c_1, 288.0, None, A.add))
-    tfb = mark("v", V.tensor_scalar(fb(2), np_, float(E2), 288.0, A.max, A.add))
-    cnp2, cof2, cdl, cpa = col(2), col(3), col(4), col(5)
-    a = mark("v", V.tensor_scalar(cnp2, np_, 2.0, None, A.mult))
-    need("v", tkl2)
-    b = mark("v", V.tensor_scalar(T.ba[:, 0:3], T.kl2[:, :], 2.0, -1.0, A.mult, A.add))
-    need("v", a, b)
-    tba = mark("v", V.tensor_scalar(T.ba[:, 3:6], T.ba[:, 0:3], cnp2, None, A.min))
-    mark("v", V.tensor_scalar(T.cu[:, 0:2], T.zr[:, 0:2], 0.0, None, A.add))
-    tcu = mark("v", V.tensor_scalar(T.cu[:, 2:4], T.zr[:, 2:4], 16.0, None, A.add))
-    ttp = turn(T.tp, 0, 4, 0, 128.0, tcv, tcp)
+    def slots(k, r_, w, x_, tok):
+        gather(k[:, cp + ps:cp + ps + H0], r_[:, :], T.lt1[:, :], la0, tok)
+        return gather(w[:, ps:ps + H0], x_[:, :], T.lt3[:, :])
 
-    fl2b, ff2b = flags("s", M2, T.tabb[:, :], 256, brm)
-    f2b = scan(inc("2b", 256), fl2b, 256, np_, ff2b, f2r)
-    pp = pick("c2", 0, 128, "c1", 200, T.tp[:, :], ttp, tq1, *h0a)
-    ship(peer[2], "a2", 0, E2, "c2", 0, E2, "e2", pp)
-    tkb2 = held(B1, T.tabb[:, :], inc("2b", 256), T.kb2[:, :], f2b, brm)
-    need("s", tl[B1], brm)
-    a = mark("s", SC.activation(T.prs[:, 0:128], look(B1).indirect(T.tabb[:, 0:8]), F.Copy))
-    need("s", a)
-    tpa = mark("s", SC.activation(T.prs[:, 128:256], T.prs[:, 0:128], F.Copy, accum_out=cpa))
-    need("s", tpa)
-    tof = mark("s", SC.activation(cof2, cpa, F.Relu, bias=-2.0 * (COLS - E1), scale=2.0 / BIG))
-    need("s", t2o, f2r, f2b, tfb)
-    mark("s", SC.activation(fc(0), c_1, F.Copy))
-    mark("s", SC.activation(fc(1), c_1, F.Identity, bias=np_, scale=-1.0))
-    a = mark("s", SC.activation(fc(2), np_, F.Identity, bias=c_3, scale=-1.0))
-    mark("s", SC.activation(fc(3), c_3, F.Identity, bias=c_4, scale=-1.0))
-    need("s", a)
-    tfs = mark("s", SC.activation(fb(3), fc(2), F.Identity, bias=fb(2)))
-    send(peer[2], T.run[:, 2 * h:2 * h + 8], T.fmo[:, 2 * h:2 * h + 8], "rmc", tfb, tfs)
-    oc = take("cs", 2)
-    tcb = on_scalar(T.kb2[:, :], 256, lambda i: T.kl2[:, 1 + i:2 + i], 2, T.cs, oc, tkb2, tkl2)
-    fslr, fsrf = flags("s", MS, ot1, 128, arm)
-    fslb, fsbf = flags("s", MS, T.tabb[:, :], 256, brm)
-    s_, tcv = on_vector(T.kb2[:, :], 256, lambda i: T.kl2[:, i:i + 1], 1, tkb2, tkl2)
-    need("v", tof)
-    a = mark("v", V.tensor_scalar(cdl, cof2, 256.0, cnp2, A.add, A.subtract))
-    need("v", a, tba)
-    a = mark("v", V.tensor_scalar(T.ba[:, 6:9], T.ba[:, 0:3], cnp2, cdl, A.is_ge, A.mult))
+    d2b = flags("v", run_2(T.f2), M2, mask_2, rm)
+    ts2, end2 = sums(T.f2, T.k2, T.r2, T.w2, T.x2, e2, d2, d2b)
+    ds = flags("s", run(T.fs, 1), MS, mask_of(1), rm)
+    dsb = flags("s", run_2(T.fs), MS, mask_2, rm)
+    need("s", ts2)
+    b, c = end2[3]
+    tnf = mark("s", SC.activation(T.nfo[:, :], b[:, c:c + 1], F.Copy))
+    send(at(4), T.nfa[:, :], T.nfo[:, :], "nf", tnf)
+    tw2 = slots(T.k2, T.r2, T.w2, T.x2, ts2)
+    psum_, pst = on_scalar(T.k2[:, cp:cp + PAIR - up], PAIR - up, k_(T.kf, 4), 4, tkf, tw2, ts2)
+    tss, ends = sums(T.fs, T.ks, T.rs, T.ws, T.xs, es, ds, dsb)
+    pv, pvt = on_vector(T.k2[:, cp:cp + PAIR], PAIR, k_(T.kf, 0), 4, T.sgc, tkf, tw2, ts2, tsc)
+    tsd = resets(T.sgd, H1, 4)
+    need("v", tzi)
+    a = mark("v", V.tensor_scalar(T.zb[:, :], T.zi[:, :], 31, None, A.bitwise_and))
     need("v", a)
-    tb = mark("v", V.tensor_tensor(T.ba[:, 9:12], T.ba[:, 3:6], T.ba[:, 6:9], A.add))
-    need("v", tcv, tb, trr)
-    a = mark("v", V.tensor_scalar(T.rr[:, 32:33], s_, T.ba[:, 9:10], -256.0, A.add, A.add))
-    tq2 = quant("c2", 224, 352)
-    need("v", tcb)
-    b = mark("v", V.tensor_tensor(T.rr[:, 33:35], T.cs[:, oc:oc + 2], T.ba[:, 10:12], A.add))
-    tt2 = turn(T.t2, 1, 3, 32, 128.0, a, b)
-    l1a = [arrived(k, peer[1]) for k in ("e1c", "e1s", "l1c", "l1s")]
-    p2 = pick("sl2", 0, L2, "c2", 232, T.t2[:, :], tt2, tq2, pp[0], pp[1], *l1a)
-    ship(peer[2], "a2", E2, 128, "sl2", 0, L2, "l2", p2)
+    a32 = mark("v", V.tensor_scalar(T.ra32[:, :], T.zb[:, 0:1], 0.5, None, A.add))
+    need("s", a32, tb32)
+    tkg = mark("s", SC.activation(T.kg[:, :], T.b32[:, :], F.Identity, bias=T.ra32[:, :]))
+    need("s", tkg)
+    tki = mark("s", SC.activation(T.ki[:, :], T.kg[:, :], F.Copy, bias=-0.5))
+    tse = resets(T.sge, NEAR, 4)
+    trr = mark("v", V.memset(T.rr[:, :], 0.0))
 
-    tno = on_scalar(T.kso[:, :], 128, kgc(2), 2, T.rr, 66, tso, tkg, trr)
-    fsr = scan(inc("sr"), fslr, 128, 0.0, fsrf)
-    tks1 = held(B0, ot1, inc("sr"), T.ks1[:, :], fsr, arm)
-    tn1 = on_scalar(T.ks1[:, :], 128, kgc(0), 2, T.rr, 68, tks1, tkg, trr)
-    fsb = scan(inc("sb", 256), fslb, 256, 0.0, fsbf)
-    tkbs = held(B1, T.tabb[:, :], inc("sb", 256), T.kbs[:, :], fsb, brm)
-    need("s", tso, fsr, fsb)
-    mark("s", SC.activation(rc_(0), T.kso[:, 127:128], F.Copy))
-    mark("s", SC.activation(rc_(1), last("sr"), F.Copy))
-    mark("s", SC.activation(rc_(2), last("sb"), F.Copy))
-    tr2 = mark("s", SC.activation(rc_(3), last("sb"), F.Identity, bias=last("sb", 256), scale=-1.0))
-    tl2 = mark("s", SC.activation(T.lnb[0:1, 1:2], T.kso[0:1, 127:128], F.Copy))
-    tn2 = on_scalar(T.kbs[:, :], 256, kgc(0), 3, T.rr, 70, tkbs, tkg, trr)
+    tk2 = gather(T.k2[:, cb:cb + H1], T.w2[:, :], T.lt2[:, :], la1, tw2)
+    bsum_, bst = on_scalar(T.k2[:, cb:cb + H1 - 1 + up], H1 - 1 + up, k_(T.kf, 4), 4, tk2)
+    bv, bvt = on_vector(T.k2[:, cb:cb + H1], H1, k_(T.kf, 0), 4, T.sgd, tk2, tsd)
+    need("v", pvt, bvt)
+    a = mark("v", V.tensor_tensor(T.ad[:, 0:4], pv, bv, A.add))
+    need("v", a)
+    mark("v", V.tensor_scalar(T.t2[:, 0:4], T.ad[:, 0:4], NEAR / 2, NEAR - 1.0, A.add, A.min))
+    need("v", pst, bst)
+    a = mark("v", V.tensor_tensor(T.ad[:, 4:8], psum_, bsum_, A.add))
+    need("v", a)
+    t2 = mark("v", V.tensor_scalar(T.t2[:, 4:8], T.ad[:, 4:8], 0.5, (NEAR - 1) / 2, A.mult, A.add))
+    h1a = [arrived("h1c", at(2)), arrived("h1s", at(2))]
+    tws = slots(T.ks, T.rs, T.ws, T.xs, tss)
+    ship(at(4), "a2", 0, "sl2", H2, "h2", pick("sl2", "c2", H2, T.t2[:, :], t2, w2, *h1a))
+    tks = gather(T.ks[:, cb:cb + H1], T.ws[:, :], T.lt2[:, :], la1, tws)
+
     need("v", ("lw", 16))
     tqw = mark("v", V.quantize_mx(T.wqc[:, :], T.wqs[:, :], T.wt[:, :]))
-    need("v", tof, tcn)
-    tnc = mark("v", V.tensor_scalar(T.nc[:, 6:9], T.nc[:, 9:12], cof2, None, A.add))
-    need("v", tk8, tkf)
-    tk8 = mark("v", V.tensor_scalar(T.k8[:, :], T.k8a[:, :], T.kf[:, 0:1], None, A.add))
-    a = mark("v", V.tensor_scalar(T.z7[:, :], T.zi[:, 0:8], 7, None, A.bitwise_and))
-    need("v", a)
-    to8 = mark("v", V.tensor_copy(T.o8[:, :], T.z7[:, :]))
-    tr1 = mark("v", V.tensor_scalar(rb_(3), last("sb"), 192.0, None, A.add))
-
-    need("v", arrived("rmc", peer[2]), tr1, tr2, tcg)
-    tsx = mark("v", V.tensor_tensor_scan(T.sx[:, 8:16], T.sg[:, 0:8], T.run[:, 4:12], 0.0, A.mult, A.add))
-    need("v", tsx)
-    mark("v", V.tensor_tensor(T.dz[:, 0:4], T.run[:, 0:4], T.sx[:, 7:11], A.subtract))
-    b = mark("v", V.tensor_tensor(T.dz[:, 4:8], T.run[:, 12:16], T.sx[:, 11:15], A.subtract))
-    need("v", b)
-    tdd = mark("v", V.tensor_tensor(T.dd[:, 0:7], T.dz[:, 1:8], T.dz[:, 0:7], A.subtract))
-
-    need("v", tnc, tno, tn1, tn2)
-    a = mark("v", V.tensor_tensor(T.rr[:, 96:105], T.rr[:, 64:73], T.nc[:, 0:9], A.add))
-    tn = turn(T.tn, 2, 9, 96, 0.0, a)
-    na = pick("nn", 0, 192, "c1", 200, T.tn[:, 0:12], tn, tq1, *h0a)
-    nb = pick("nn", 192, 288, "c2", 232, T.tn[:, 12:18], tn, tq2, pp[0], pp[1], *l1a)
 
     def product(o, bank, c, n, *deps):
         need("t", tqw, *deps)
         return mark("t", TE.matmul_mx(T.ps[:, 512 * bank:512 * bank + n], T.wqc[:, 128 * o:128 * o + 128], T.wqs[:, 128 * o:128 * o + 128],
                                       T[c + "c"][:, 0:n], T[c + "s"][:, 0:n], True, True))
-    m0 = product(0, 0, "nn", 288, na[0], na[1], nb[0], nb[1])
-    m1 = product(1, 1, "nn", 288)
+    m0 = product(0, 0, "c2", NEAR, w2, *h1a)
+    m1 = product(1, 1, "c2", NEAR)
+
+    b, c = ends[3]
+    nn = b[:, c:c + 1]
+    need("v", arrived("nf", at(4)), tki, tkg, tss)
+    tke, kE = tkg, T.kg
+    if far:
+        tke, kE = mark("v", V.tensor_scalar(T.ke[:, :], T.kg[:, :], T.nfa[:, :], None, A.subtract)), T.ke
+    ta = mark("v", V.tensor_scalar(T.na[:, :], T.nfa[:, :], nn, None, A.add))
+    lsum, lst = on_scalar(T.ks[:, :], NEAR, k_(kE, 4), 4, tke, tks, tss)
+    lv, lvt = on_vector(T.ks[:, :], NEAR, k_(kE, 0), 4, T.sge, tke, tks, tss, tse)
+    if far:
+        a = mark("v", V.tensor_scalar(T.nd[:, :], T.nfa[:, :], -1.0, float(H2), A.mult, A.add))
+        mark("v", V.tensor_scalar(T.ga[:, :], T.ki[:, :], T.nfa[:, :], None, A.min))
+        need("v", a)
+        a = mark("v", V.tensor_scalar(T.gw[:, :], T.ki[:, :], T.nfa[:, :], T.nd[:, :], A.is_ge, A.mult))
+        need("v", a)
+        a = mark("v", V.tensor_tensor(T.gd[:, :], T.ga[:, :], T.gw[:, :], A.add))
+        part = T.gd
+    else:
+        a = mark("v", V.tensor_scalar(T.ga[:, :], T.ki[:, :], nn, 0.0, A.subtract, A.max))
+        part = T.ga
+    need("v", ta)
+    b = mark("v", V.tensor_scalar(T.gb[:, :], T.ki[:, :], T.na[:, :], BIG, A.is_ge, A.mult))
+    need("v", a, b)
+    tgt = mark("v", V.tensor_tensor(T.gt[:, :], part[:, :], T.gb[:, :], A.add))
+    need("v", tza)
+    mark("v", V.tensor_scalar(T.cu[:, 0:2], T.za[:, :], 0.0, None, A.add))
+    tcu = mark("v", V.tensor_scalar(T.cu[:, 2:4], T.za[:, :], 16.0, None, A.add))
+
+    need("s", lst)
+    ths = mark("s", SC.activation(T.hs[:, :], lsum, F.Copy, scale=0.5))
+    need("v", lvt, tgt, trr)
+    mark("v", V.tensor_tensor(T.rr[:, 0:4], lv, T.gt[:, 0:4], A.add))
+    need("v", ths)
+    a = mark("v", V.tensor_tensor(T.rr[:, 4:8], T.hs[:, :], T.gt[:, 4:8], A.add))
+    need("v", a)
+    a = mark("v", V.transpose(T.ra[:, :], T.rr[:, :]))
+    need("v", a, tcu)
+    a = mark("v", V.tensor_copy(T.rb[:, :], T.ra[:, :].indirect(T.cu[:, :])))
+    need("v", a)
+    a = mark("v", V.transpose(T.rc[:, :], T.rb[:, :]))
+    need("v", a)
+    mark("v", V.tensor_scalar(T.tf[:, 0:16:2], T.rc[:, 0:8], NEAR / 2, float(ZERO), A.add, A.min))
+    ttf = mark("v", V.tensor_scalar(T.tf[:, 1:16:2], T.rc[:, 32:40], NEAR / 2, float(ZERO), A.add, A.min))
     need("s", m0)
-    g0a = mark("s", SC.activation(T.g0[:, 0:288], T.ps[:, 0:288], F.Copy))
+    g0a = mark("s", SC.activation(T.g0[:, gn:gn + NEAR], T.ps[:, 0:NEAR], F.Copy))
     need("s", m1)
-    g1a = mark("s", SC.activation(T.g1[:, 0:288], T.ps[:, 512:800], F.Copy))
+    g1a = mark("s", SC.activation(T.g1[:, gn:gn + NEAR], T.ps[:, 512:512 + NEAR], F.Copy))
+    ends_ = lambda e: ends[e][0][0:1, ends[e][1]:ends[e][1] + 1]
+    need("s", ta, tss)
+    mark("s", SC.activation(T.lnb[0:1, 0:1], T.na[0:1, :], F.Copy))
+    if r:
+        tln = mark("s", SC.activation(T.lnb[0:1, 1:2], ends_(r - 1), F.Identity, bias=ends_(r), scale=-1.0))
+    else:
+        tln = mark("s", SC.activation(T.lnb[0:1, 1:2], ends_(r), F.Copy))
 
-    need("s", tsx)
-    tln = mark("s", SC.activation(T.lnb[0:1, 0:1], T.sx[0:1, 15:16], F.Copy))
-    need("v", to8, tk8)
-    c = mark("v", V.tensor_tensor(T.tm[:, 0:128], T.sx[:, 8:16].indirect(T.o8[:, :]), T.k8[:, :], A.is_le))
-    need("v", c, tdd)
-    a = mark("v", V.tensor_tensor(T.tm[:, 128:256], T.dd[:, 0:8].indirect(T.o8[:, :]), T.tm[:, 0:128], A.mult))
-    need("v", a, ts8)
-    a = mark("v", V.tensor_tensor_scan(T.tm[:, 256:384], T.s8[:, :], T.tm[:, 128:256], 0.0, A.mult, A.add))
-    need("v", a)
-    a = mark("v", V.tensor_tensor(T.tg[:, :], T.tm[:, 263:384:8], T.kq[:, :], A.add))
-    need("v", a)
-    ttf = mark("v", V.tensor_scalar(T.tf[:, :], T.tg[:, :], T.dz[:, 0:1], 416.0, A.add, A.min))
-
-    l2a = [arrived(k, peer[2]) for k in ("e2c", "e2s", "l2c", "l2s")]
-    m2 = product(0, 2, "a2", 128, *l2a)
-    m3 = product(1, 3, "a2", 128)
+    h2a = [arrived("h2c", at(4)), arrived("h2s", at(4))]
+    m2 = product(0, 2, "a2", H2, *h2a)
+    m3 = product(1, 3, "a2", H2)
     need("v", m2)
-    b0 = mark("v", V.tensor_copy(T.g0[:, 288:416], T.ps[:, 1024:1152]))
+    b0 = mark("v", V.tensor_copy(T.g0[:, gf:gf + H2], T.ps[:, 1024:1024 + H2]))
     need("s", m3)
-    b1 = mark("s", SC.activation(T.g1[:, 288:416], T.ps[:, 1536:1664], F.Copy))
-    need("v", b0, g0a, tcg, ttf)
+    b1 = mark("s", SC.activation(T.g1[:, gf:gf + H2], T.ps[:, 1536:1536 + H2], F.Copy))
+    need("v", b0, g0a, tz, ttf)
     y0 = mark("v", V.tensor_copy(T.y0[:, :], T.g0[:, :].indirect(T.tf[:, :])))
-    need("s", b1, g1a, tcg, ttf)
+    need("s", b1, g1a, tz, ttf)
     y1 = mark("s", SC.activation(T.y1[:, :], T.g1[:, :].indirect(T.tf[:, :]), F.Copy))
-    need("y", tln, tl2)
-    g.sync.dma_start(T.ln[:, :], T.lnb[:, :]).then_inc(T.sem.sln, 16)
+    need("y", tln)
+    Y.dma_start(T.ln[:, :], T.lnb[:, :]).then_inc(T.sem.sln, 16)
     need("y", y0)
-    g.sync.dma_start(T.y[:, 0:S], T.y0[:, :]).then_inc(T.sem.sya, 16)
+    Y.dma_start(T.y[:, 0:S], T.y0[:, :]).then_inc(T.sem.sya, 16)
     need("s", y1)
     SC.dma_start(T.y[:, S:2 * S], T.y1[:, :]).then_inc(T.sem.syb, 16)
 

@@ -28,9 +28,7 @@ SCRATCH = {
     "zb": ("sbuf", [128, 2], "int32"), "ra16": ("sbuf", [128, 1], "float32"), "ra32": ("sbuf", [128, 1], "float32"),
     "b16": ("sbuf", [128, 8], "float32"), "b32": ("sbuf", [128, 8], "float32"), "kf": ("sbuf", [128, 8], "float32"),
     "kg": ("sbuf", [128, 8], "float32"), "ki": ("sbuf", [128, 8], "float32"), "cu": ("sbuf", [128, 4], "uint16"),
-    "la": ("sbuf", [128, 768], "int32"), "lut": ("sbuf", [128, 1024], "bfloat16"),
-    "one": ("sbuf", [128, 128], "bfloat16"), "sgc": ("sbuf", [128, 4 * PAIR], "bfloat16"), "sgd": ("sbuf", [128, 4 * H1], "bfloat16"),
-    "sge": ("sbuf", [128, 4 * NEAR], "bfloat16"),
+    "la": ("sbuf", [128, 768], "int32"), "lut": ("sbuf", [128, 1024], "bfloat16"), "one": ("sbuf", [128, NEAR], "bfloat16"),
     "f0": ("sbuf", [128, 128], "bfloat16"), "f1": ("sbuf", [128, 256], "bfloat16"), "f2": ("sbuf", [128, 512], "bfloat16"),
     "fs": ("sbuf", [128, 512], "bfloat16"), "k0": ("sbuf", [128, 128], "bfloat16"),
     "k1": ("sbuf", [128, PAIR], "bfloat16"), "r1": ("sbuf", [128, 128], "bfloat16"),
@@ -124,6 +122,7 @@ def rank_program(g, core, T, topo):
     tlv = mark("p", g.iota(T.lv[:, :], [[1, 256]], 0, 0))
     tzi = mark("p", g.iota(T.zi[:, :], [[0, 2]], 0, 1))
     tb16 = iota(T.b16[:, :], [[16, 8]])
+    tb32 = iota(T.b32[:, :], [[32, 8]])
     e_ = q ^ 4
     tl[M2] = iota(look(M2), [[0, 256 >> (e_ + 1)], [1, 2], [0, 1 << e_]])
 
@@ -150,9 +149,9 @@ def rank_program(g, core, T, topo):
         use[name] += n
         return o
 
-    def scan(out, fl, init, *deps):
+    def scan(out, fl, init, *deps, n=COLS):
         need("v", tone, *deps)
-        return mark("v", V.tensor_tensor_scan(out, T.one[:, :], fl, init, A.mult, A.add))
+        return mark("v", V.tensor_tensor_scan(out, T.one[:, 0:n], fl, init, A.mult, A.add))
 
     def flags(e, out, l, tab, *deps):
         need(e, tl[l], *deps)
@@ -166,13 +165,14 @@ def rank_program(g, core, T, topo):
 
     k_ = lambda t, j: (lambda i: t[:, j + i:j + i + 1])
 
-    def on_vector(key, n, kcol, nv, sg, *deps):
+    def on_vector(key, n, kcol, nv, *deps):
         o = take("jv", nv * n)
         need("v", *deps)
         for i in range(nv):
             a_ = mark("v", V.tensor_scalar(T.jv[:, o + i * n:o + i * n + n], key, kcol(i), 0.5, A.is_le, A.subtract))
         need("v", a_)
-        a_ = mark("v", V.tensor_tensor_scan(T.jw[:, o:o + nv * n], sg[:, 0:nv * n], T.jv[:, o:o + nv * n], 0.0, A.mult, A.add))
+        for i in range(nv):
+            a_ = scan(T.jw[:, o + i * n:o + i * n + n], T.jv[:, o + i * n:o + i * n + n], 0.0, n=n)
         return T.jw[:, o + n - 1:o + nv * n:n], a_
 
     def on_scalar(key, n, kcol, ns, *deps):
@@ -183,9 +183,9 @@ def rank_program(g, core, T, topo):
             a_ = mark("s", SC.activation(T.js[:, o:o + n], key, F.Sign, bias=kcol(i), scale=-1.0, accum_out=T.cs[:, o_ + i:o_ + i + 1]))
         return T.cs[:, o_:o_ + ns], a_
 
-    def table(tab, key, n, nv, ns, sg, *deps):
+    def table(tab, key, n, nv, ns, *deps):
         sb = on_scalar(key[:, 0:n - 1], n - 1, k_(T.kf, nv), ns, tkf, *deps)
-        sa = on_vector(key[:, 0:n], n, k_(T.kf, 0), nv, sg, tkf, *deps)
+        sa = on_vector(key[:, 0:n], n, k_(T.kf, 0), nv, tkf, *deps)
         return tab, n, nv, ns, sa, sb
 
     def finish(tab, n, nv, ns, sa, sb):
@@ -211,14 +211,13 @@ def rank_program(g, core, T, topo):
 
     f = flags("v", T.f0[:, :], M0, mask_of(0), tpo)
     ti = scan(T.k0[:, :], T.f0[:, :], 0.0, f)
-    c0 = table(T.t0, T.k0, COLS, 1, 3, T.one, ti)
+    c0 = table(T.t0, T.k0, COLS, 2, 2, ti)
     need("v", ("lx", 16))
     tq0 = mark("v", V.quantize_mx(T.c0c[:, :], T.c0s[:, :], T.xt[:, :]))
     t0 = finish(*c0)
     spread([at(1), at(3)], [T.lt1[:, :], T.lt3[:, :]], T.t0[:, :], "la0", t0)
     p0 = pick("sl0", "c0", H0, T.t0[:, :], t0, tq0)
     ship(at(1), "c1", COLS * hi, "sl0", H0, "h0", p0)
-    tb32 = iota(T.b32[:, :], [[32, 8]])
 
     need("y", tq0)
     Y.dma_start(codes(T.c1c, po, po + COLS), codes(T.c0c, 0, COLS)).then_inc(T.sem.cp1, 16)
@@ -232,33 +231,39 @@ def rank_program(g, core, T, topo):
     Y.dma_start(T.c2s[:, cp + ps:cp + ps + H0], T.c1s[:, ps:ps + H0]).then_inc(T.sem.cp2, 16)
     w1, w2 = ("cp1", 32), ("cp2", 64)
 
-    def resets(t, n, c):
-        a_ = mark("v", V.memset(t[:, :], 1.0))
-        need("v", a_)
-        return mark("v", V.memset(t[:, 0:c * n:n], 0.0))
-
     lut(M1, [q ^ 2, q ^ 6])
+    need("s", tone)
+    mark("s", SC.activation(T.g0[:, ZERO:ZERO + 16], T.one[:, 0:16], F.Copy, scale=0.0))
+    tz = mark("s", SC.activation(T.g1[:, ZERO:ZERO + 16], T.one[:, 0:16], F.Copy, scale=0.0))
     half = lambda h: T.f1[:, 128 * h:128 * h + 128]
     e1 = flags("s", half(hi), M1, mask_of(0), tpo)
     e2 = flags("s", run(T.f2, 0), M2, mask_of(0), tpo)
-    tsc = resets(T.sgc, PAIR, 4)
     lut(MS, [q])
     es = flags("s", run(T.fs, 0), MS, mask_of(0), tpo)
-    mark("v", V.memset(T.g0[:, ZERO:ZERO + 16], 0.0))
-    tz = mark("v", V.memset(T.g1[:, ZERO:ZERO + 16], 0.0))
+    a = mark("v", V.tensor_scalar(T.zb[:, :], T.zi[:, :], 31, None, A.bitwise_and))
+    mark("v", V.tensor_scalar(T.cu[:, 0:2], T.za[:, :], 0.0, None, A.add))
+    need("v", a)
+    a = mark("v", V.tensor_scalar(T.ra32[:, :], T.zb[:, 0:1], 0.5, None, A.add))
+    need("s", a, tb32)
+    tkg = mark("s", SC.activation(T.kg[:, :], T.b32[:, :], F.Identity, bias=T.ra32[:, :]))
+    need("s", tkg)
+    tki = mark("s", SC.activation(T.ki[:, :], T.kg[:, :], F.Copy, bias=-0.5))
+    tcu = mark("v", V.tensor_scalar(T.cu[:, 2:4], T.za[:, :], 16.0, None, A.add))
+    trr = mark("v", V.memset(T.rr[:, :], 0.0))
 
     rm = arrived("rm", at(1), at(2), at(3))
     la0 = arrived("la0", at(1), at(3))
     la1 = arrived("la1", at(2))
     d1 = flags("s", half(1 - hi), M1, mask_of(1), rm)
+    d2 = flags("v", run(T.f2, 1), M2, mask_of(1), rm)
     init, tok = 0.0, []
     for h in range(2):
         b, c = (T.k1, po) if h == hi else (T.r1, 0)
         tok.append(scan(b[:, c:c + COLS], half(h), init, e1 if h == hi else d1, *tok))
         init = b[:, c + COLS - 1:c + COLS]
-    d2 = flags("v", run(T.f2, 1), M2, mask_of(1), rm)
+    d2b = flags("v", run_2(T.f2), M2, mask_2, rm)
     tk1 = gather(T.k1[:, ps:ps + H0], T.r1[:, :], T.lt1[:, :], la0, *tok)
-    t1 = finish(*table(T.t1, T.k1, PAIR, 3, 3, T.sgc, tk1, tsc, *tok))
+    t1 = finish(*table(T.t1, T.k1, PAIR, 3, 3, tk1, *tok))
     send(at(2), T.lt2[:, :], T.t1[:, :], "la1", t1)
     p1 = pick("sl1", "c1", H1, T.t1[:, :], t1, w1, *h0a)
     ship(at(2), "c2", PAIR * up, "sl1", H1, "h1", p1)
@@ -272,52 +277,39 @@ def rank_program(g, core, T, topo):
             init = b[:, c + COLS - 1:c + COLS]
         return tok[-1], ends
 
-    def slots(k, r_, w, x_, tok):
-        gather(k[:, cp + ps:cp + ps + H0], r_[:, :], T.lt1[:, :], la0, tok)
-        return gather(w[:, ps:ps + H0], x_[:, :], T.lt3[:, :])
+    slots_1 = lambda k, r_, tok: gather(k[:, cp + ps:cp + ps + H0], r_[:, :], T.lt1[:, :], la0, tok)
+    slots_3 = lambda w, x_, tok: gather(w[:, ps:ps + H0], x_[:, :], T.lt3[:, :], la0, tok)
 
-    d2b = flags("v", run_2(T.f2), M2, mask_2, rm)
     ts2, end2 = sums(T.f2, T.k2, T.r2, T.w2, T.x2, e2, d2, d2b)
+    need("v", ("lw", 16))
+    tqw = mark("v", V.quantize_mx(T.wqc[:, :], T.wqs[:, :], T.wt[:, :]))
     ds = flags("s", run(T.fs, 1), MS, mask_of(1), rm)
-    dsb = flags("s", run_2(T.fs), MS, mask_2, rm)
-    need("s", ts2)
+    tw1 = slots_1(T.k2, T.r2, ts2)
     b, c = end2[3]
     tnf = mark("s", SC.activation(T.nfo[:, :], b[:, c:c + 1], F.Copy))
     send(at(4), T.nfa[:, :], T.nfo[:, :], "nf", tnf)
-    tw2 = slots(T.k2, T.r2, T.w2, T.x2, ts2)
-    psum_, pst = on_scalar(T.k2[:, cp:cp + PAIR - up], PAIR - up, k_(T.kf, 4), 4, tkf, tw2, ts2)
-    tss, ends = sums(T.fs, T.ks, T.rs, T.ws, T.xs, es, ds, dsb)
-    pv, pvt = on_vector(T.k2[:, cp:cp + PAIR], PAIR, k_(T.kf, 0), 4, T.sgc, tkf, tw2, ts2, tsc)
-    tsd = resets(T.sgd, H1, 4)
-    need("v", tzi)
-    a = mark("v", V.tensor_scalar(T.zb[:, :], T.zi[:, :], 31, None, A.bitwise_and))
-    need("v", a)
-    a32 = mark("v", V.tensor_scalar(T.ra32[:, :], T.zb[:, 0:1], 0.5, None, A.add))
-    need("s", a32, tb32)
-    tkg = mark("s", SC.activation(T.kg[:, :], T.b32[:, :], F.Identity, bias=T.ra32[:, :]))
-    need("s", tkg)
-    tki = mark("s", SC.activation(T.ki[:, :], T.kg[:, :], F.Copy, bias=-0.5))
-    tse = resets(T.sge, NEAR, 4)
-    trr = mark("v", V.memset(T.rr[:, :], 0.0))
+    tw2 = slots_3(T.w2, T.x2, ts2)
+    ps_, pst = on_scalar(T.k2[:, cp:cp + PAIR - up], PAIR - up, k_(T.kf, 5), 3, tkf, tw1, ts2)
+    pv_, pvt = on_vector(T.k2[:, cp:cp + PAIR], PAIR, k_(T.kf, 0), 5, tkf, tw1, ts2)
 
     tk2 = gather(T.k2[:, cb:cb + H1], T.w2[:, :], T.lt2[:, :], la1, tw2)
-    bsum_, bst = on_scalar(T.k2[:, cb:cb + H1 - 1 + up], H1 - 1 + up, k_(T.kf, 4), 4, tk2)
-    bv, bvt = on_vector(T.k2[:, cb:cb + H1], H1, k_(T.kf, 0), 4, T.sgd, tk2, tsd)
+    bs_, bst = on_scalar(T.k2[:, cb:cb + H1 - 1 + up], H1 - 1 + up, k_(T.kf, 5), 3, tk2)
+    dsb = flags("s", run_2(T.fs), MS, mask_2, rm)
+    bv_, bvt = on_vector(T.k2[:, cb:cb + H1], H1, k_(T.kf, 0), 5, tk2)
     need("v", pvt, bvt)
-    a = mark("v", V.tensor_tensor(T.ad[:, 0:4], pv, bv, A.add))
+    a = mark("v", V.tensor_tensor(T.ad[:, 0:5], pv_, bv_, A.add))
     need("v", a)
-    mark("v", V.tensor_scalar(T.t2[:, 0:4], T.ad[:, 0:4], NEAR / 2, NEAR - 1.0, A.add, A.min))
+    mark("v", V.tensor_scalar(T.t2[:, 0:5], T.ad[:, 0:5], NEAR / 2, NEAR - 1.0, A.add, A.min))
     need("v", pst, bst)
-    a = mark("v", V.tensor_tensor(T.ad[:, 4:8], psum_, bsum_, A.add))
+    a = mark("v", V.tensor_tensor(T.ad[:, 5:8], ps_, bs_, A.add))
     need("v", a)
-    t2 = mark("v", V.tensor_scalar(T.t2[:, 4:8], T.ad[:, 4:8], 0.5, (NEAR - 1) / 2, A.mult, A.add))
+    t2 = mark("v", V.tensor_scalar(T.t2[:, 5:8], T.ad[:, 5:8], 0.5, (NEAR - 1) / 2, A.mult, A.add))
     h1a = [arrived("h1c", at(2)), arrived("h1s", at(2))]
-    tws = slots(T.ks, T.rs, T.ws, T.xs, tss)
     ship(at(4), "a2", 0, "sl2", H2, "h2", pick("sl2", "c2", H2, T.t2[:, :], t2, w2, *h1a))
+    tss, ends = sums(T.fs, T.ks, T.rs, T.ws, T.xs, es, ds, dsb)
+    tws = slots_3(T.ws, T.xs, tss)
+    slots_1(T.ks, T.rs, tss)
     tks = gather(T.ks[:, cb:cb + H1], T.ws[:, :], T.lt2[:, :], la1, tws)
-
-    need("v", ("lw", 16))
-    tqw = mark("v", V.quantize_mx(T.wqc[:, :], T.wqs[:, :], T.wt[:, :]))
 
     def product(o, bank, c, n, *deps):
         need("t", tqw, *deps)
@@ -333,8 +325,6 @@ def rank_program(g, core, T, topo):
     if far:
         tke, kE = mark("v", V.tensor_scalar(T.ke[:, :], T.kg[:, :], T.nfa[:, :], None, A.subtract)), T.ke
     ta = mark("v", V.tensor_scalar(T.na[:, :], T.nfa[:, :], nn, None, A.add))
-    lsum, lst = on_scalar(T.ks[:, :], NEAR, k_(kE, 4), 4, tke, tks, tss)
-    lv, lvt = on_vector(T.ks[:, :], NEAR, k_(kE, 0), 4, T.sge, tke, tks, tss, tse)
     if far:
         a = mark("v", V.tensor_scalar(T.nd[:, :], T.nfa[:, :], -1.0, float(H2), A.mult, A.add))
         mark("v", V.tensor_scalar(T.ga[:, :], T.ki[:, :], T.nfa[:, :], None, A.min))
@@ -350,14 +340,13 @@ def rank_program(g, core, T, topo):
     b = mark("v", V.tensor_scalar(T.gb[:, :], T.ki[:, :], T.na[:, :], BIG, A.is_ge, A.mult))
     need("v", a, b)
     tgt = mark("v", V.tensor_tensor(T.gt[:, :], part[:, :], T.gb[:, :], A.add))
-    need("v", tza)
-    mark("v", V.tensor_scalar(T.cu[:, 0:2], T.za[:, :], 0.0, None, A.add))
-    tcu = mark("v", V.tensor_scalar(T.cu[:, 2:4], T.za[:, :], 16.0, None, A.add))
 
+    ls_, lst = on_scalar(T.ks[:, :], NEAR, k_(kE, 4), 4, tke, tks, tss)
+    lv_, lvt = on_vector(T.ks[:, :], NEAR, k_(kE, 0), 4, tke, tks, tss)
     need("s", lst)
-    ths = mark("s", SC.activation(T.hs[:, :], lsum, F.Copy, scale=0.5))
+    ths = mark("s", SC.activation(T.hs[:, :], ls_, F.Copy, scale=0.5))
     need("v", lvt, tgt, trr)
-    mark("v", V.tensor_tensor(T.rr[:, 0:4], lv, T.gt[:, 0:4], A.add))
+    mark("v", V.tensor_tensor(T.rr[:, 0:4], lv_, T.gt[:, 0:4], A.add))
     need("v", ths)
     a = mark("v", V.tensor_tensor(T.rr[:, 4:8], T.hs[:, :], T.gt[:, 4:8], A.add))
     need("v", a)
@@ -373,13 +362,6 @@ def rank_program(g, core, T, topo):
     g0a = mark("s", SC.activation(T.g0[:, gn:gn + NEAR], T.ps[:, 0:NEAR], F.Copy))
     need("s", m1)
     g1a = mark("s", SC.activation(T.g1[:, gn:gn + NEAR], T.ps[:, 512:512 + NEAR], F.Copy))
-    ends_ = lambda e: ends[e][0][0:1, ends[e][1]:ends[e][1] + 1]
-    need("s", ta, tss)
-    mark("s", SC.activation(T.lnb[0:1, 0:1], T.na[0:1, :], F.Copy))
-    if r:
-        tln = mark("s", SC.activation(T.lnb[0:1, 1:2], ends_(r - 1), F.Identity, bias=ends_(r), scale=-1.0))
-    else:
-        tln = mark("s", SC.activation(T.lnb[0:1, 1:2], ends_(r), F.Copy))
 
     h2a = [arrived("h2c", at(4)), arrived("h2s", at(4))]
     m2 = product(0, 2, "a2", H2, *h2a)
@@ -392,12 +374,19 @@ def rank_program(g, core, T, topo):
     y0 = mark("v", V.tensor_copy(T.y0[:, :], T.g0[:, :].indirect(T.tf[:, :])))
     need("s", b1, g1a, tz, ttf)
     y1 = mark("s", SC.activation(T.y1[:, :], T.g1[:, :].indirect(T.tf[:, :]), F.Copy))
-    need("y", tln)
-    Y.dma_start(T.ln[:, :], T.lnb[:, :]).then_inc(T.sem.sln, 16)
     need("y", y0)
     Y.dma_start(T.y[:, 0:S], T.y0[:, :]).then_inc(T.sem.sya, 16)
     need("s", y1)
     SC.dma_start(T.y[:, S:2 * S], T.y1[:, :]).then_inc(T.sem.syb, 16)
+    end_ = lambda e: ends[e][0][0:1, ends[e][1]:ends[e][1] + 1]
+    need("s", ta, tss)
+    mark("s", SC.activation(T.lnb[0:1, 0:1], T.na[0:1, :], F.Copy))
+    if r:
+        tln = mark("s", SC.activation(T.lnb[0:1, 1:2], end_(r - 1), F.Identity, bias=end_(r), scale=-1.0))
+    else:
+        tln = mark("s", SC.activation(T.lnb[0:1, 1:2], end_(r), F.Copy))
+    need("y", tln)
+    Y.dma_start(T.ln[:, :], T.lnb[:, :]).then_inc(T.sem.sln, 16)
 
     need("p", ("loc", sent[0]), ("qv", done["v"]), ("qs", done["s"]), ("qt", done["t"]), ("qp", done["p"]))
     need("y", ("sln", 16), ("sya", 16))

@@ -5,18 +5,21 @@ A = AluOpType
 F = ActivationFunctionType
 U8, U32 = dt.uint8, dt.uint32
 N, COLS, S = 8, 128, 256
-BIG = 1024.0
 H0, H1, H2 = 64, 96, 128
 PAIR = COLS + H0
 NEAR = PAIR + H1
 ZERO = NEAR + H2
+N1, N2 = (3, 3), (4, 4)
+NF = 4
+LOW = 64.0
 
 CODE, PLANE = "float8_e4m3fn_x4", "uint8"
+BLK = 208
 SCRATCH = {
-    "dmi": ("sbuf", [128, 8], "int32"), "xt": ("sbuf", [128, 512], "bfloat16"), "wt": ("sbuf", [128, 1024], "bfloat16"),
-    "c0c": ("sbuf", [128, COLS], CODE), "c0s": ("sbuf", [128, COLS], PLANE),
-    "c1c": ("sbuf", [128, PAIR], CODE), "c1s": ("sbuf", [128, PAIR], PLANE),
-    "c2c": ("sbuf", [128, NEAR], CODE), "c2s": ("sbuf", [128, NEAR], PLANE),
+    "dmi": ("sbuf", [128, 8], "int32"), "xt": ("sbuf", [128, 520], "bfloat16"), "wt": ("sbuf", [128, 1024], "bfloat16"),
+    "c0c": ("sbuf", [128, COLS + 2], CODE), "c0s": ("sbuf", [128, COLS + 2], PLANE),
+    "c1c": ("sbuf", [128, PAIR + 2], CODE), "c1s": ("sbuf", [128, PAIR + 2], PLANE),
+    "c2c": ("sbuf", [128, NEAR + 2], CODE), "c2s": ("sbuf", [128, NEAR + 2], PLANE),
     "a2c": ("sbuf", [128, H2], CODE), "a2s": ("sbuf", [128, H2], PLANE),
     "wqc": ("sbuf", [128, 256], CODE), "wqs": ("sbuf", [128, 256], PLANE),
     "sl0c": ("sbuf", [128, H0], CODE), "sl0s": ("sbuf", [128, H0], PLANE),
@@ -24,31 +27,31 @@ SCRATCH = {
     "sl2c": ("sbuf", [128, H2], CODE), "sl2s": ("sbuf", [128, H2], PLANE),
     "tab": ("sbuf", [128, 32], "uint16"), "lt1": ("sbuf", [128, 4], "uint16"), "lt3": ("sbuf", [128, 4], "uint16"),
     "lt2": ("sbuf", [128, 6], "uint16"), "nfa": ("sbuf", [128, 1], "float32"), "nfo": ("sbuf", [128, 1], "float32"),
-    "lv": ("sbuf", [128, 256], "int32"), "zi": ("sbuf", [128, 2], "int32"), "za": ("sbuf", [128, 2], "int32"),
+    "a0": ("sbuf", [128, 8], "int32"), "u0": ("sbuf", [128, 8], "uint16"),
+    "nz": ("sbuf", [128, 256], "bfloat16"), "lut": ("sbuf", [128, 768], "bfloat16"), "lv": ("sbuf", [128, 256], "int32"),
+    "la": ("sbuf", [128, 256], "int32"), "zi": ("sbuf", [128, 2], "int32"), "za": ("sbuf", [128, 2], "int32"),
     "zb": ("sbuf", [128, 2], "int32"), "ra16": ("sbuf", [128, 1], "float32"), "ra32": ("sbuf", [128, 1], "float32"),
     "b16": ("sbuf", [128, 8], "float32"), "b32": ("sbuf", [128, 8], "float32"), "kf": ("sbuf", [128, 8], "float32"),
     "kg": ("sbuf", [128, 8], "float32"), "ki": ("sbuf", [128, 8], "float32"), "cu": ("sbuf", [128, 4], "uint16"),
-    "la": ("sbuf", [128, 768], "int32"), "lut": ("sbuf", [128, 1024], "bfloat16"), "one": ("sbuf", [128, NEAR], "bfloat16"),
-    "f0": ("sbuf", [128, 128], "bfloat16"), "f1": ("sbuf", [128, 256], "bfloat16"), "f2": ("sbuf", [128, 512], "bfloat16"),
-    "fs": ("sbuf", [128, 512], "bfloat16"), "k0": ("sbuf", [128, 128], "bfloat16"),
-    "k1": ("sbuf", [128, PAIR], "bfloat16"), "r1": ("sbuf", [128, 128], "bfloat16"),
-    "k2": ("sbuf", [128, NEAR], "bfloat16"), "r2": ("sbuf", [128, 128], "bfloat16"), "w2": ("sbuf", [128, PAIR], "bfloat16"),
-    "x2": ("sbuf", [128, 128], "bfloat16"), "ks": ("sbuf", [128, NEAR], "bfloat16"), "rs": ("sbuf", [128, 128], "bfloat16"),
-    "ws": ("sbuf", [128, PAIR], "bfloat16"), "xs": ("sbuf", [128, 128], "bfloat16"),
-    "js": ("sbuf", [128, 4096], "bfloat16"), "jv": ("sbuf", [128, 4096], "bfloat16"), "jw": ("sbuf", [128, 4096], "bfloat16"),
-    "cs": ("sbuf", [128, 20], "float32"), "hs": ("sbuf", [128, 4], "float32"), "rr": ("sbuf", [128, 32], "float32"),
-    "ra": ("sbuf", [128, 32], "float32"), "rb": ("sbuf", [128, 64], "float32"), "rc": ("sbuf", [128, 64], "float32"),
-    "ad": ("sbuf", [128, 8], "float32"),
-    "ke": ("sbuf", [128, 8], "float32"), "na": ("sbuf", [128, 1], "float32"), "nd": ("sbuf", [128, 1], "float32"),
-    "ga": ("sbuf", [128, 8], "float32"), "gb": ("sbuf", [128, 8], "float32"), "gw": ("sbuf", [128, 8], "float32"),
-    "gd": ("sbuf", [128, 8], "float32"), "gt": ("sbuf", [128, 8], "float32"),
+    "one": ("sbuf", [128, NEAR], "bfloat16"),
+    "fb": ("sbuf", [128, 7 * BLK], "bfloat16"), "f0": ("sbuf", [128, COLS], "bfloat16"), "f1": ("sbuf", [128, PAIR], "bfloat16"),
+    "f2": ("sbuf", [128, NEAR], "bfloat16"), "fs": ("sbuf", [128, NEAR], "bfloat16"), "k0": ("sbuf", [128, COLS], "bfloat16"),
+    "k1": ("sbuf", [128, PAIR], "bfloat16"), "k2": ("sbuf", [128, NEAR], "bfloat16"), "ks": ("sbuf", [128, NEAR], "bfloat16"),
+    "e1": ("sbuf", [128, 1], "float32"), "ba": ("sbuf", [128, 1], "float32"), "bb": ("sbuf", [128, 1], "float32"),
+    "bs": ("sbuf", [128, 1], "float32"),
+    "js": ("sbuf", [128, 6144], "bfloat16"), "jv": ("sbuf", [128, 6144], "bfloat16"), "jw": ("sbuf", [128, 6144], "bfloat16"),
+    "cs": ("sbuf", [128, 32], "float32"), "hs": ("sbuf", [128, 8], "float32"), "rr": ("sbuf", [128, 32], "bfloat16"),
+    "ra": ("sbuf", [128, 32], "bfloat16"), "rb": ("sbuf", [128, 64], "bfloat16"), "rc": ("sbuf", [128, 64], "bfloat16"),
+    "ad": ("sbuf", [128, 16], "float32"),
+    "ke": ("sbuf", [128, 8], "float32"), "ga": ("sbuf", [128, 8], "float32"), "gb": ("sbuf", [128, 8], "float32"),
+    "gt": ("sbuf", [128, 8], "float32"),
     "t0": ("sbuf", [128, 4], "uint16"), "t1": ("sbuf", [128, 6], "uint16"), "t2": ("sbuf", [128, 8], "uint16"),
     "tf": ("sbuf", [128, 16], "uint16"), "lnb": ("sbuf", [1, 2], "float32"),
     "g0": ("sbuf", [128, ZERO + 16], "float32"), "g1": ("sbuf", [128, ZERO + 16], "float32"),
     "y0": ("sbuf", [128, 256], "float32"), "y1": ("sbuf", [128, 256], "float32"),
     "ps": ("psum", [128, 2048], "float32"),
 }
-ARR = ["rm", "la0", "la1", "nf", "h0c", "h0s", "h1c", "h1s", "h2c", "h2s"]
+ARR = ["rm1", "rm2", "l1", "l2", "l3", "nf", "h0c", "h0s", "h1c", "h1s", "h2c", "h2s"]
 SEMAPHORES = ["qv", "qs", "qt", "qp", "ld", "lx", "lw", "cp1", "cp2", "sya", "syb", "sln", "loc"] + ARR
 
 
@@ -101,215 +104,250 @@ def rank_program(g, core, T, topo):
     at = lambda x: T.cores[q ^ x]
     codes = lambda t, a, b: t[:, a:b].bitcast(U8)
 
-    r, hi, up, far = q & 3, q & 1, (q >> 1) & 1, q >> 2
+    hi, up, far = q & 1, (q >> 1) & 1, q >> 2
     po, ps = H0 * hi, COLS * (1 - hi)
     cp, cb = H1 * up, PAIR * (1 - up)
     gn, gf = H2 * far, NEAR * (1 - far)
-    mask_of = lambda x: T.tab[:, 8 * (r ^ x):8 * (r ^ x) + 8]
-    run = lambda t, x: t[:, 128 * (r ^ x):128 * (r ^ x) + 128]
-    t2a = 16 * (1 - up)
-    mask_2 = T.tab[:, t2a:t2a + 16]
-    run_2 = lambda t: t[:, 16 * t2a:16 * t2a + 256]
+    bits = lambda *ranks: sum(1 << e for e in ranks)
+    look = lambda l: T.lut[:, 256 * l:256 * l + 256]
+    M1, M2, MS = range(3)
+    tab = lambda x: T.tab[:, 8 * x:8 * x + 8]
+    bit = lambda e: [[0, 256 >> (e + 1)], [1, 2], [0, 1 << e]]
+    R1, R2, RS, X2, XS, W2, WS = range(7)
+    blk = lambda b, a, n: T.fb[:, BLK * b + a:BLK * b + a + n]
+    others = lambda b: blk(b, H0, COLS)
+    tail = lambda b: blk(b, H0, BLK - H0)
+    whole = lambda b: blk(b, 0, BLK)
 
     for i in range(8):
         (Y if i % 2 == 0 else SC).dma_start(T.dmi[16 * i:16 * i + 16, :], T.dm[:, :]).then_inc(T.sem.ld, 16)
-    Y.dma_start(T.xt[:, :], T.x[:, :]).then_inc(T.sem.lx, 16)
+    Y.dma_start(T.xt[:, 0:512], T.x[:, :]).then_inc(T.sem.lx, 16)
+    Y.dma_start(T.wt[:, :], T.w[:, :]).then_inc(T.sem.lw, 16)
 
-    look = lambda l: T.lut[:, 256 * l:256 * l + 256]
-    M0, M1, MS, M2 = range(4)
-    tl = {}
     iota = lambda o, pat: mark("p", g.iota(o, pat, 0, 0, allow_small_or_imprecise_dtypes=True))
     tlv = mark("p", g.iota(T.lv[:, :], [[1, 256]], 0, 0))
     tzi = mark("p", g.iota(T.zi[:, :], [[0, 2]], 0, 1))
     tb16 = iota(T.b16[:, :], [[16, 8]])
     tb32 = iota(T.b32[:, :], [[32, 8]])
-    e_ = q ^ 4
-    tl[M2] = iota(look(M2), [[0, 256 >> (e_ + 1)], [1, 2], [0, 1 << e_]])
-
-    def lut(l, ranks):
-        m = sum(1 << e for e in ranks)
-        need("v", tlv)
-        a = mark("v", V.tensor_scalar(T.la[:, 256 * l:256 * l + 256], T.lv[:, :], m, None, A.bitwise_and))
-        need("v", a)
-        tl[l] = mark("v", V.tensor_scalar(look(l), T.la[:, 256 * l:256 * l + 256], 0.0, None, A.is_gt))
-
+    mark("v", V.memset(T.nz[:, 0:1], 0.0))
+    tnz = mark("v", V.memset(T.nz[:, 1:256], 1.0))
     tone = mark("v", V.memset(T.one[:, :], 1.0))
-    lut(M0, [e for e in range(N) if (e ^ q) & 1])
-    need("v", tzi)
-    tza = mark("v", V.tensor_scalar(T.za[:, :], T.zi[:, :], 15, None, A.bitwise_and))
-    need("v", tza)
-    a = mark("v", V.tensor_scalar(T.ra16[:, :], T.za[:, 0:1], 0.5, None, A.add))
-    need("s", a, tb16)
-    tkf = mark("s", SC.activation(T.kf[:, :], T.b16[:, :], F.Identity, bias=T.ra16[:, :]))
+    txz = mark("v", V.memset(T.xt[:, 512:520], 0.0))
+    tfz = mark("v", V.memset(T.fb[:, PAIR:7 * BLK:BLK], 0.0))
+    need("v", tlv)
+    a = mark("v", V.tensor_scalar(T.la[:, :], T.lv[:, :], bits(q ^ 2, q ^ 6), None, A.bitwise_and))
+    need("v", a)
+    tl = {M1: mark("v", V.tensor_scalar(look(M1), T.la[:, :], 0.0, None, A.is_gt)), None: tnz}
+    need("s", tone)
+    mark("s", SC.activation(T.g0[:, ZERO:ZERO + 16], T.one[:, 0:16], F.Copy, scale=0.0))
+    tz = mark("s", SC.activation(T.g1[:, ZERO:ZERO + 16], T.one[:, 0:16], F.Copy, scale=0.0))
 
-    use = {"js": 0, "jv": 0, "cs": 0}
+    use = {"js": 0, "jv": 0, "cs": 0, "ad": 0}
 
     def take(name, n):
         o = use[name]
         use[name] += n
         return o
 
-    def scan(out, fl, init, *deps, n=COLS):
+    def scan(out, fl, init, *deps):
         need("v", tone, *deps)
+        n = int(out.shape[1])
         return mark("v", V.tensor_tensor_scan(out, T.one[:, 0:n], fl, init, A.mult, A.add))
 
-    def flags(e, out, l, tab, *deps):
+    def flags(e, out, l, masks, total, *deps):
         need(e, tl[l], *deps)
+        win = T.nz[:, :] if l is None else look(l)
         if e == "v":
-            return mark(e, V.tensor_copy(out, look(l).indirect(tab)))
-        return mark(e, SC.activation(out, look(l).indirect(tab), F.Copy))
+            return mark(e, V.tensor_copy(out, win.indirect(masks)))
+        return mark(e, SC.activation(out, win.indirect(masks), F.Copy, accum_out=total))
 
-    def gather(out, win, tab, *deps):
-        need("s", *deps)
-        return mark("s", SC.activation(out, win.indirect(tab), F.Copy))
+    def gather(out, win, tab_, *deps):
+        need("s", tfz, *deps)
+        return mark("s", SC.activation(out, win.indirect(tab_), F.Copy))
 
     k_ = lambda t, j: (lambda i: t[:, j + i:j + i + 1])
 
-    def on_vector(key, n, kcol, nv, *deps):
+    def on_vector(key, kcol, skip, init, nv, *deps):
+        b, c, n = key
         o = take("jv", nv * n)
         need("v", *deps)
+        part = lambda t, i: t[:, o + i * n + skip(i):o + i * n + n]
         for i in range(nv):
-            a_ = mark("v", V.tensor_scalar(T.jv[:, o + i * n:o + i * n + n], key, kcol(i), 0.5, A.is_le, A.subtract))
+            a_ = mark("v", V.tensor_scalar(part(T.jv, i), b[:, c + skip(i):c + n], kcol(i), 0.5, A.is_le, A.subtract))
         need("v", a_)
         for i in range(nv):
-            a_ = scan(T.jw[:, o + i * n:o + i * n + n], T.jv[:, o + i * n:o + i * n + n], 0.0, n=n)
-        return T.jw[:, o + n - 1:o + nv * n:n], a_
+            a_ = scan(part(T.jw, i), part(T.jv, i), init(i))
+        return (lambda i: T.jw[:, o + i * n + n - 1:o + i * n + n]), T.jw[:, o + n - 1:o + nv * n:n], a_
 
-    def on_scalar(key, n, kcol, ns, *deps):
+    def on_scalar(key, kcol, skip, ns, *deps):
+        b, c, n = key
         o_ = take("cs", ns)
         need("s", *deps)
+        n -= skip
         for i in range(ns):
             o = take("js", n)
-            a_ = mark("s", SC.activation(T.js[:, o:o + n], key, F.Sign, bias=kcol(i), scale=-1.0, accum_out=T.cs[:, o_ + i:o_ + i + 1]))
+            a_ = mark("s", SC.activation(T.js[:, o:o + n], b[:, c + skip:c + skip + n], F.Sign, bias=kcol(i), scale=-1.0,
+                                         accum_out=T.cs[:, o_ + i:o_ + i + 1]))
         return T.cs[:, o_:o_ + ns], a_
 
-    def table(tab, key, n, nv, ns, *deps):
-        sb = on_scalar(key[:, 0:n - 1], n - 1, k_(T.kf, nv), ns, tkf, *deps)
-        sa = on_vector(key[:, 0:n], n, k_(T.kf, 0), nv, tkf, *deps)
-        return tab, n, nv, ns, sa, sb
+    def early_s(key, first, nv, ns, *deps):
+        return on_scalar(key, k_(T.kf, nv), 16 * nv if first else 0, ns, tkf, *deps)
 
-    def finish(tab, n, nv, ns, sa, sb):
-        need("v", sa[1])
-        mark("v", V.tensor_scalar(tab[:, 0:nv], sa[0], n / 2, n - 1.0, A.add, A.min))
-        need("v", sb[1])
-        return mark("v", V.tensor_scalar(tab[:, nv:nv + ns], sb[0], 0.5, (n - 1) / 2, A.mult, A.add))
+    def early_v(key, first, nv, *deps):
+        return on_vector(key, k_(T.kf, 0), lambda i: 16 * i if first else 0, lambda i: 8.0 * i, nv, tkf, *deps)
 
-    def pick(out, src, n, tab, *deps):
+    def late_s(key, first, nv, ns, *deps):
+        return on_scalar(key, k_(T.kf, nv), 0 if first else 16 * nv, ns, tkf, *deps)
+
+    def late_v(key, first, nv, va, *deps):
+        return on_vector(key, k_(T.kf, 0), lambda i: 0 if first else 16 * i, va[0], nv, tkf, va[2], *deps)
+
+    def complete(tab_, n, nv, ns, va, sa, sb):
+        need("v", va[2])
+        mark("v", V.tensor_scalar(tab_[:, 0:nv], va[1], n / 2, None, A.add))
+        o = take("ad", ns)
+        need("v", sa[1], sb[1])
+        a_ = mark("v", V.tensor_tensor(T.ad[:, o:o + ns], sa[0], sb[0], A.add))
+        need("v", a_)
+        return mark("v", V.tensor_scalar(tab_[:, nv:nv + ns], T.ad[:, o:o + ns], 0.5, (n + 16 * nv) / 2, A.mult, A.add))
+
+    def pick_codes(out, src, n, tab_, *deps):
         need("v", *deps)
-        a_ = mark("v", V.tensor_copy(T[out + "c"][:, 0:n].bitcast(U32), T[src + "c"][:, :].bitcast(U32).indirect(tab)))
+        return mark("v", V.tensor_copy(T[out + "c"][:, 0:n].bitcast(U32), T[src + "c"][:, :].bitcast(U32).indirect(tab_[:, :])))
+
+    def pick_plane(out, src, n, tab_, *deps):
         need("s", *deps)
-        b_ = mark("s", SC.activation(T[out + "s"][:, 0:n], T[src + "s"][:, :].indirect(tab), F.Copy))
-        return a_, b_
+        return mark("s", SC.activation(T[out + "s"][:, 0:n], T[src + "s"][:, :].indirect(tab_[:, :]), F.Copy))
 
     def ship(dst, to, a_, src, n, sem, tok):
         send(dst, codes(T[to + "c"], a_, a_ + n), codes(T[src + "c"], 0, n), sem + "c", tok[0])
         send(dst, T[to + "s"][:, a_:a_ + n], T[src + "s"][:, 0:n], sem + "s", tok[1])
 
     need("v", ("ld", 128))
-    tpo = mark("v", V.tensor_copy(mask_of(0), T.dmi[:, :]))
-    spread([at(1), at(2), at(3)], [mask_of(0)] * 3, mask_of(0), "rm", tpo)
+    tm = mark("v", V.tensor_copy(tab(0), T.dmi[:, :]))
+    send(at(1), tab(1), tab(0), "rm1", tm)
+    spread([at(2), at(3)], [tab(2), tab(3)], tab(0), "rm2")
+    tl[M2] = iota(look(M2), bit(q ^ 4))
 
-    f = flags("v", T.f0[:, :], M0, mask_of(0), tpo)
+    a = mark("v", V.tensor_scalar(T.a0[:, :], T.dmi[:, :], bits(*[e for e in range(N) if (e ^ q) & 1]), None, A.bitwise_and))
+    need("v", tzi)
+    tza = mark("v", V.tensor_scalar(T.za[:, :], T.zi[:, :], 15, None, A.bitwise_and))
+    need("v", a)
+    a = mark("v", V.tensor_copy(T.u0[:, :], T.a0[:, :]))
+    need("v", tza)
+    b = mark("v", V.tensor_scalar(T.ra16[:, :], T.za[:, 0:1], 0.5, None, A.add))
+    need("s", b, tb16)
+    tkf = mark("s", SC.activation(T.kf[:, :], T.b16[:, :], F.Identity, bias=T.ra16[:, :]))
+    f = flags("v", T.f0[:, :], None, T.u0[:, :], None, a)
     ti = scan(T.k0[:, :], T.f0[:, :], 0.0, f)
-    c0 = table(T.t0, T.k0, COLS, 2, 2, ti)
-    need("v", ("lx", 16))
+    key = (T.k0, 0, COLS)
+    sb = on_scalar(key, k_(T.kf, 2), 32, 2, tkf, ti)
+    va = on_vector(key, k_(T.kf, 0), lambda i: 16 * i, lambda i: 8.0 * i, 2, tkf, ti)
+    need("v", ("lx", 16), txz)
     tq0 = mark("v", V.quantize_mx(T.c0c[:, :], T.c0s[:, :], T.xt[:, :]))
-    t0 = finish(*c0)
-    spread([at(1), at(3)], [T.lt1[:, :], T.lt3[:, :]], T.t0[:, :], "la0", t0)
-    p0 = pick("sl0", "c0", H0, T.t0[:, :], t0, tq0)
-    ship(at(1), "c1", COLS * hi, "sl0", H0, "h0", p0)
+    need("v", va[2])
+    mark("v", V.tensor_scalar(T.t0[:, 0:2], va[1], COLS / 2, None, A.add))
+    need("v", sb[1])
+    t0 = mark("v", V.tensor_scalar(T.t0[:, 2:4], sb[0], 0.5, (COLS + 32) / 2, A.mult, A.add))
+    send(at(1), T.lt1[:, :], T.t0[:, :], "l1", t0)
+    ship(at(1), "c1", COLS * hi, "sl0", H0, "h0", (pick_codes("sl0", "c0", H0, T.t0, t0, tq0), pick_plane("sl0", "c0", H0, T.t0, t0, tq0)))
+    send(at(3), T.lt3[:, :], T.t0[:, :], "l3", t0)
+    tl[MS] = iota(look(MS), bit(q))
 
     need("y", tq0)
-    Y.dma_start(codes(T.c1c, po, po + COLS), codes(T.c0c, 0, COLS)).then_inc(T.sem.cp1, 16)
-    Y.dma_start(T.c1s[:, po:po + COLS], T.c0s[:, :]).then_inc(T.sem.cp1, 16)
+    tot = COLS + 2 * hi
+    Y.dma_start(codes(T.c1c, po, po + tot), codes(T.c0c, 0, tot)).then_inc(T.sem.cp1, 16)
+    Y.dma_start(T.c1s[:, po:po + tot], T.c0s[:, 0:tot]).then_inc(T.sem.cp1, 16)
+    w1 = 32
+    if not hi:
+        Y.dma_start(codes(T.c1c, PAIR, PAIR + 2), codes(T.c0c, COLS, COLS + 2)).then_inc(T.sem.cp1, 16)
+        Y.dma_start(T.c1s[:, PAIR:PAIR + 2], T.c0s[:, COLS:COLS + 2]).then_inc(T.sem.cp1, 16)
+        w1 = 64
     Y.dma_start(codes(T.c2c, cp + po, cp + po + COLS), codes(T.c0c, 0, COLS)).then_inc(T.sem.cp2, 16)
-    Y.dma_start(T.c2s[:, cp + po:cp + po + COLS], T.c0s[:, :]).then_inc(T.sem.cp2, 16)
-    Y.dma_start(T.wt[:, :], T.w[:, :]).then_inc(T.sem.lw, 16)
+    Y.dma_start(T.c2s[:, cp + po:cp + po + COLS], T.c0s[:, 0:COLS]).then_inc(T.sem.cp2, 16)
+    Y.dma_start(codes(T.c2c, NEAR, NEAR + 2), codes(T.c0c, COLS, COLS + 2)).then_inc(T.sem.cp2, 16)
+    Y.dma_start(T.c2s[:, NEAR:NEAR + 2], T.c0s[:, COLS:COLS + 2]).then_inc(T.sem.cp2, 16)
     h0a = [arrived("h0c", at(1)), arrived("h0s", at(1))]
     need("y", *h0a)
     Y.dma_start(codes(T.c2c, cp + ps, cp + ps + H0), codes(T.c1c, ps, ps + H0)).then_inc(T.sem.cp2, 16)
     Y.dma_start(T.c2s[:, cp + ps:cp + ps + H0], T.c1s[:, ps:ps + H0]).then_inc(T.sem.cp2, 16)
-    w1, w2 = ("cp1", 32), ("cp2", 64)
+    w1, w2 = ("cp1", w1), ("cp2", 96)
 
-    lut(M1, [q ^ 2, q ^ 6])
-    need("s", tone)
-    mark("s", SC.activation(T.g0[:, ZERO:ZERO + 16], T.one[:, 0:16], F.Copy, scale=0.0))
-    tz = mark("s", SC.activation(T.g1[:, ZERO:ZERO + 16], T.one[:, 0:16], F.Copy, scale=0.0))
-    half = lambda h: T.f1[:, 128 * h:128 * h + 128]
-    e1 = flags("s", half(hi), M1, mask_of(0), tpo)
-    e2 = flags("s", run(T.f2, 0), M2, mask_of(0), tpo)
-    lut(MS, [q])
-    es = flags("s", run(T.fs, 0), MS, mask_of(0), tpo)
+    rm1, rm2 = arrived("rm1", at(1)), arrived("rm2", at(2), at(3))
+    l1, l2, l3 = arrived("l1", at(1)), arrived("l2", at(2)), arrived("l3", at(3))
+    e1 = flags("s", T.f1[:, po:po + COLS], M1, tab(0), None, tm)
+    e2 = flags("s", T.f2[:, cp + po:cp + po + COLS], M2, tab(0), None, tm)
+    d1 = flags("s", others(R1), M1, tab(1), T.e1[:, :] if hi else None, rm1)
     a = mark("v", V.tensor_scalar(T.zb[:, :], T.zi[:, :], 31, None, A.bitwise_and))
     mark("v", V.tensor_scalar(T.cu[:, 0:2], T.za[:, :], 0.0, None, A.add))
+    tcu = mark("v", V.tensor_scalar(T.cu[:, 2:4], T.za[:, :], 16.0, None, A.add))
     need("v", a)
     a = mark("v", V.tensor_scalar(T.ra32[:, :], T.zb[:, 0:1], 0.5, None, A.add))
     need("s", a, tb32)
     tkg = mark("s", SC.activation(T.kg[:, :], T.b32[:, :], F.Identity, bias=T.ra32[:, :]))
     need("s", tkg)
     tki = mark("s", SC.activation(T.ki[:, :], T.kg[:, :], F.Copy, bias=-0.5))
-    tcu = mark("v", V.tensor_scalar(T.cu[:, 2:4], T.za[:, :], 16.0, None, A.add))
     trr = mark("v", V.memset(T.rr[:, :], 0.0))
-
-    rm = arrived("rm", at(1), at(2), at(3))
-    la0 = arrived("la0", at(1), at(3))
-    la1 = arrived("la1", at(2))
-    d1 = flags("s", half(1 - hi), M1, mask_of(1), rm)
-    d2 = flags("v", run(T.f2, 1), M2, mask_of(1), rm)
-    init, tok = 0.0, []
-    for h in range(2):
-        b, c = (T.k1, po) if h == hi else (T.r1, 0)
-        tok.append(scan(b[:, c:c + COLS], half(h), init, e1 if h == hi else d1, *tok))
-        init = b[:, c + COLS - 1:c + COLS]
-    d2b = flags("v", run_2(T.f2), M2, mask_2, rm)
-    tk1 = gather(T.k1[:, ps:ps + H0], T.r1[:, :], T.lt1[:, :], la0, *tok)
-    t1 = finish(*table(T.t1, T.k1, PAIR, 3, 3, tk1, *tok))
-    send(at(2), T.lt2[:, :], T.t1[:, :], "la1", t1)
-    p1 = pick("sl1", "c1", H1, T.t1[:, :], t1, w1, *h0a)
-    ship(at(2), "c2", PAIR * up, "sl1", H1, "h1", p1)
-
-    def sums(fl, k, r_, w, x_, *deps):
-        init, tok, ends = 0.0, list(deps), []
-        for e in range(4):
-            b, c = ((k, cp + po), (r_, 0), (w, po), (x_, 0))[e ^ r]
-            tok.append(scan(b[:, c:c + COLS], run(fl, e ^ r), init, *tok))
-            ends.append((b, c + COLS - 1))
-            init = b[:, c + COLS - 1:c + COLS]
-        return tok[-1], ends
-
-    slots_1 = lambda k, r_, tok: gather(k[:, cp + ps:cp + ps + H0], r_[:, :], T.lt1[:, :], la0, tok)
-    slots_3 = lambda w, x_, tok: gather(w[:, ps:ps + H0], x_[:, :], T.lt3[:, :], la0, tok)
-
-    ts2, end2 = sums(T.f2, T.k2, T.r2, T.w2, T.x2, e2, d2, d2b)
     need("v", ("lw", 16))
     tqw = mark("v", V.quantize_mx(T.wqc[:, :], T.wqs[:, :], T.wt[:, :]))
-    ds = flags("s", run(T.fs, 1), MS, mask_of(1), rm)
-    tw1 = slots_1(T.k2, T.r2, ts2)
-    b, c = end2[3]
-    tnf = mark("s", SC.activation(T.nfo[:, :], b[:, c:c + 1], F.Copy))
-    send(at(4), T.nfa[:, :], T.nfo[:, :], "nf", tnf)
-    tw2 = slots_3(T.w2, T.x2, ts2)
-    ps_, pst = on_scalar(T.k2[:, cp:cp + PAIR - up], PAIR - up, k_(T.kf, 5), 3, tkf, tw1, ts2)
-    pv_, pvt = on_vector(T.k2[:, cp:cp + PAIR], PAIR, k_(T.kf, 0), 5, tkf, tw1, ts2)
 
-    tk2 = gather(T.k2[:, cb:cb + H1], T.w2[:, :], T.lt2[:, :], la1, tw2)
-    bs_, bst = on_scalar(T.k2[:, cb:cb + H1 - 1 + up], H1 - 1 + up, k_(T.kf, 5), 3, tk2)
-    dsb = flags("s", run_2(T.fs), MS, mask_2, rm)
-    bv_, bvt = on_vector(T.k2[:, cb:cb + H1], H1, k_(T.kf, 0), 5, tk2)
-    need("v", pvt, bvt)
-    a = mark("v", V.tensor_tensor(T.ad[:, 0:5], pv_, bv_, A.add))
-    need("v", a)
-    mark("v", V.tensor_scalar(T.t2[:, 0:5], T.ad[:, 0:5], NEAR / 2, NEAR - 1.0, A.add, A.min))
-    need("v", pst, bst)
-    a = mark("v", V.tensor_tensor(T.ad[:, 5:8], ps_, bs_, A.add))
-    need("v", a)
-    t2 = mark("v", V.tensor_scalar(T.t2[:, 5:8], T.ad[:, 5:8], 0.5, (NEAR - 1) / 2, A.mult, A.add))
+    own, came = (T.k1, po, COLS), (T.k1, ps, H0)
+    if hi:
+        ta = scan(T.k1[:, po:po + COLS], T.f1[:, po:po + COLS], T.e1[:, :], e1, d1)
+    else:
+        ta = scan(T.k1[:, po:po + COLS], T.f1[:, po:po + COLS], 0.0, e1)
+    sa = early_s(own, not hi, *N1, ta)
+    va = early_v(own, not hi, N1[0], ta)
+    es = flags("v", T.fs[:, cp + po:cp + po + COLS], MS, tab(0), None, tm)
+    s1 = gather(T.f1[:, ps:ps + H0], tail(R1), T.lt1[:, :], l1, d1)
+    tb = scan(T.k1[:, ps:ps + H0], T.f1[:, ps:ps + H0], 0.0 if hi else T.k1[:, po + COLS - 1:po + COLS], ta, s1)
+    sb = late_s(came, not hi, *N1, tb)
+    vb = late_v(came, not hi, N1[0], va, tb)
+    t1 = complete(T.t1, PAIR, *N1, vb, sa, sb)
+    send(at(2), T.lt2[:, :], T.t1[:, :], "l2", t1)
+    d2 = flags("s", others(R2), M2, tab(1), None, rm1)
+    s2 = gather(T.f2[:, cp + ps:cp + ps + H0], tail(R2), T.lt1[:, :], l1, d2)
+    da = flags("s", blk(W2, po, COLS), M2, tab(2), T.ba[:, :], rm2)
+    db = flags("s", others(X2), M2, tab(3), T.bb[:, :], rm2)
+    need("s", da, db)
+    tbs = mark("s", SC.activation(T.bs[:, :], T.ba[:, :], F.Identity, bias=T.bb[:, :]))
+    ship(at(2), "c2", PAIR * up, "sl1", H1, "h1",
+         (pick_codes("sl1", "c1", H1, T.t1, t1, w1, *h0a), pick_plane("sl1", "c1", H1, T.t1, t1, w1, *h0a)))
+    d3 = flags("v", others(RS), MS, tab(1), None, rm1)
+    d4 = flags("v", others(XS), MS, tab(3), None, rm2)
+
+    own, came = (T.k2, cp, PAIR), (T.k2, cb, H1)
+    end = T.k2[:, cp + PAIR - 1:cp + PAIR]
+    if up:
+        ta = scan(T.k2[:, cp:cp + PAIR], T.f2[:, cp:cp + PAIR], T.bs[:, :], e2, s2, tbs)
+    else:
+        ta = scan(T.k2[:, cp:cp + PAIR], T.f2[:, cp:cp + PAIR], 0.0, e2, s2)
+    s3 = gather(blk(W2, ps, H0), tail(X2), T.lt3[:, :], l3, db)
+    sa = early_s(own, not up, *N2, ta)
+    va = early_v(own, not up, N2[0], ta)
+    need("s", ta, tbs)
+    if up:
+        tnf = mark("s", SC.activation(T.nfo[:, :], end, F.Copy))
+    else:
+        tnf = mark("s", SC.activation(T.nfo[:, :], end, F.Identity, bias=T.bs[:, :]))
+    send(at(4), T.nfa[:, :], T.nfo[:, :], "nf", tnf)
+    d5 = flags("v", blk(WS, po, COLS), MS, tab(2), None, rm2)
+    if far:
+        need("v", tki)
+        tga = mark("v", V.tensor_scalar(T.ga[:, :], T.ki[:, :], float(H2), None, A.min))
+    s5 = gather(T.fs[:, cp + ps:cp + ps + H0], tail(RS), T.lt1[:, :], l1, d3)
+    s6 = gather(blk(WS, ps, H0), tail(XS), T.lt3[:, :], l3, d4)
+    s4 = gather(T.f2[:, cb:cb + H1], whole(W2), T.lt2[:, :], l2, s3, da)
+    tb = scan(T.k2[:, cb:cb + H1], T.f2[:, cb:cb + H1], 0.0 if up else end, ta, s4)
+    sb = late_s(came, not up, *N2, tb)
+    vb = late_v(came, not up, N2[0], va, tb)
+    t2 = complete(T.t2, NEAR, *N2, vb, sa, sb)
+    s7 = gather(T.fs[:, cb:cb + H1], whole(WS), T.lt2[:, :], l2, d5, s6)
     h1a = [arrived("h1c", at(2)), arrived("h1s", at(2))]
-    ship(at(4), "a2", 0, "sl2", H2, "h2", pick("sl2", "c2", H2, T.t2[:, :], t2, w2, *h1a))
-    tss, ends = sums(T.fs, T.ks, T.rs, T.ws, T.xs, es, ds, dsb)
-    tws = slots_3(T.ws, T.xs, tss)
-    slots_1(T.ks, T.rs, tss)
-    tks = gather(T.ks[:, cb:cb + H1], T.ws[:, :], T.lt2[:, :], la1, tws)
+    ship(at(4), "a2", 0, "sl2", H2, "h2",
+         (pick_codes("sl2", "c2", H2, T.t2, t2, w2, *h1a), pick_plane("sl2", "c2", H2, T.t2, t2, w2, *h1a)))
+
+    tss = scan(T.ks[:, :], T.fs[:, :], 0.0, es, s5, s7)
 
     def product(o, bank, c, n, *deps):
         need("t", tqw, *deps)
@@ -318,37 +356,27 @@ def rank_program(g, core, T, topo):
     m0 = product(0, 0, "c2", NEAR, w2, *h1a)
     m1 = product(1, 1, "c2", NEAR)
 
-    b, c = ends[3]
-    nn = b[:, c:c + 1]
-    need("v", arrived("nf", at(4)), tki, tkg, tss)
-    tke, kE = tkg, T.kg
+    nn = T.ks[:, NEAR - 1:NEAR]
+    nf = arrived("nf", at(4))
     if far:
+        need("v", nf, tkg, tki)
+        mark("v", V.tensor_scalar(T.gb[:, :], T.ki[:, :], T.nfa[:, :], float(H2), A.is_ge, A.mult))
         tke, kE = mark("v", V.tensor_scalar(T.ke[:, :], T.kg[:, :], T.nfa[:, :], None, A.subtract)), T.ke
-    ta = mark("v", V.tensor_scalar(T.na[:, :], T.nfa[:, :], nn, None, A.add))
-    if far:
-        a = mark("v", V.tensor_scalar(T.nd[:, :], T.nfa[:, :], -1.0, float(H2), A.mult, A.add))
-        mark("v", V.tensor_scalar(T.ga[:, :], T.ki[:, :], T.nfa[:, :], None, A.min))
-        need("v", a)
-        a = mark("v", V.tensor_scalar(T.gw[:, :], T.ki[:, :], T.nfa[:, :], T.nd[:, :], A.is_ge, A.mult))
-        need("v", a)
-        a = mark("v", V.tensor_tensor(T.gd[:, :], T.ga[:, :], T.gw[:, :], A.add))
-        part = T.gd
+        need("v", tga, tke)
+        tgt = mark("v", V.tensor_tensor(T.gt[:, :], T.ga[:, :], T.gb[:, :], A.max))
     else:
-        a = mark("v", V.tensor_scalar(T.ga[:, :], T.ki[:, :], nn, 0.0, A.subtract, A.max))
-        part = T.ga
-    need("v", ta)
-    b = mark("v", V.tensor_scalar(T.gb[:, :], T.ki[:, :], T.na[:, :], BIG, A.is_ge, A.mult))
-    need("v", a, b)
-    tgt = mark("v", V.tensor_tensor(T.gt[:, :], part[:, :], T.gb[:, :], A.add))
+        tke, kE = tkg, T.kg
+        need("v", tki, tss)
+        tgt = mark("v", V.tensor_scalar(T.gt[:, :], T.ki[:, :], nn, 0.0, A.subtract, A.max))
 
-    ls_, lst = on_scalar(T.ks[:, :], NEAR, k_(kE, 4), 4, tke, tks, tss)
-    lv_, lvt = on_vector(T.ks[:, :], NEAR, k_(kE, 0), 4, tke, tks, tss)
+    ls_, lst = on_scalar((T.ks, 0, NEAR), k_(kE, NF), 0, 8 - NF, tke, tss)
+    _, lv_, lvt = on_vector((T.ks, 0, NEAR), k_(kE, 0), lambda i: 0, lambda i: -LOW, NF, tke, tss)
     need("s", lst)
-    ths = mark("s", SC.activation(T.hs[:, :], ls_, F.Copy, scale=0.5))
+    ths = mark("s", SC.activation(T.hs[:, 0:8 - NF], ls_, F.Copy, scale=0.5, bias=-LOW))
     need("v", lvt, tgt, trr)
-    mark("v", V.tensor_tensor(T.rr[:, 0:4], lv_, T.gt[:, 0:4], A.add))
+    mark("v", V.tensor_tensor(T.rr[:, 0:NF], lv_, T.gt[:, 0:NF], A.add))
     need("v", ths)
-    a = mark("v", V.tensor_tensor(T.rr[:, 4:8], T.hs[:, :], T.gt[:, 4:8], A.add))
+    a = mark("v", V.tensor_tensor(T.rr[:, NF:8], T.hs[:, 0:8 - NF], T.gt[:, NF:8], A.add))
     need("v", a)
     a = mark("v", V.transpose(T.ra[:, :], T.rr[:, :]))
     need("v", a, tcu)
@@ -356,8 +384,8 @@ def rank_program(g, core, T, topo):
     need("v", a)
     a = mark("v", V.transpose(T.rc[:, :], T.rb[:, :]))
     need("v", a)
-    mark("v", V.tensor_scalar(T.tf[:, 0:16:2], T.rc[:, 0:8], NEAR / 2, float(ZERO), A.add, A.min))
-    ttf = mark("v", V.tensor_scalar(T.tf[:, 1:16:2], T.rc[:, 32:40], NEAR / 2, float(ZERO), A.add, A.min))
+    mark("v", V.tensor_scalar(T.tf[:, 0:16:2], T.rc[:, 0:8], NEAR / 2 + LOW, float(ZERO), A.add, A.min))
+    ttf = mark("v", V.tensor_scalar(T.tf[:, 1:16:2], T.rc[:, 32:40], NEAR / 2 + LOW, float(ZERO), A.add, A.min))
     need("s", m0)
     g0a = mark("s", SC.activation(T.g0[:, gn:gn + NEAR], T.ps[:, 0:NEAR], F.Copy))
     need("s", m1)
@@ -378,13 +406,13 @@ def rank_program(g, core, T, topo):
     Y.dma_start(T.y[:, 0:S], T.y0[:, :]).then_inc(T.sem.sya, 16)
     need("s", y1)
     SC.dma_start(T.y[:, S:2 * S], T.y1[:, :]).then_inc(T.sem.syb, 16)
-    end_ = lambda e: ends[e][0][0:1, ends[e][1]:ends[e][1] + 1]
-    need("s", ta, tss)
-    mark("s", SC.activation(T.lnb[0:1, 0:1], T.na[0:1, :], F.Copy))
-    if r:
-        tln = mark("s", SC.activation(T.lnb[0:1, 1:2], end_(r - 1), F.Identity, bias=end_(r), scale=-1.0))
+    need("s", tss, nf)
+    mark("s", SC.activation(T.lnb[0:1, 0:1], T.nfa[0:1, :], F.Identity, bias=T.ks[0:1, NEAR - 1:NEAR]))
+    c = cp + po
+    if c:
+        tln = mark("s", SC.activation(T.lnb[0:1, 1:2], T.ks[0:1, c - 1:c], F.Identity, bias=T.ks[0:1, c + COLS - 1:c + COLS], scale=-1.0))
     else:
-        tln = mark("s", SC.activation(T.lnb[0:1, 1:2], end_(r), F.Copy))
+        tln = mark("s", SC.activation(T.lnb[0:1, 1:2], T.ks[0:1, COLS - 1:COLS], F.Copy))
     need("y", tln)
     Y.dma_start(T.ln[:, :], T.lnb[:, :]).then_inc(T.sem.sln, 16)
 

@@ -10,7 +10,7 @@ PAIR = COLS + H0
 NEAR = PAIR + H1
 ZERO = NEAR + H2
 N1, N2 = (3, 3), (4, 4)
-NF = 4
+NF, NE = 3, 2
 LOW = 64.0
 
 CODE, PLANE = "float8_e4m3fn_x4", "uint8"
@@ -26,14 +26,13 @@ SCRATCH = {
     "sl1c": ("sbuf", [128, H1], CODE), "sl1s": ("sbuf", [128, H1], PLANE),
     "sl2c": ("sbuf", [128, H2], CODE), "sl2s": ("sbuf", [128, H2], PLANE),
     "tab": ("sbuf", [128, 32], "uint16"), "lt1": ("sbuf", [128, 4], "uint16"), "lt3": ("sbuf", [128, 4], "uint16"),
-    "lt2": ("sbuf", [128, 6], "uint16"), "nfa": ("sbuf", [128, 1], "float32"), "nfo": ("sbuf", [128, 1], "float32"),
-    "a0": ("sbuf", [128, 8], "int32"), "u0": ("sbuf", [128, 8], "uint16"),
-    "nz": ("sbuf", [128, 256], "bfloat16"), "lut": ("sbuf", [128, 768], "bfloat16"), "lv": ("sbuf", [128, 256], "int32"),
-    "la": ("sbuf", [128, 256], "int32"), "zi": ("sbuf", [128, 2], "int32"), "za": ("sbuf", [128, 2], "int32"),
-    "zb": ("sbuf", [128, 2], "int32"), "ra16": ("sbuf", [128, 1], "float32"), "ra32": ("sbuf", [128, 1], "float32"),
-    "b16": ("sbuf", [128, 8], "float32"), "b32": ("sbuf", [128, 8], "float32"), "kf": ("sbuf", [128, 8], "float32"),
-    "kg": ("sbuf", [128, 8], "float32"), "ki": ("sbuf", [128, 8], "float32"), "cu": ("sbuf", [128, 4], "uint16"),
-    "one": ("sbuf", [128, NEAR], "bfloat16"),
+    "lt2": ("sbuf", [128, 6], "uint16"), "nfa": ("sbuf", [128, 2], "float32"), "nfo": ("sbuf", [128, 2], "float32"),
+    "lut": ("sbuf", [128, 1024], "bfloat16"), "lv": ("sbuf", [128, 16], "int32"), "la": ("sbuf", [128, 16], "int32"),
+    "pa": ("sbuf", [128, 16], "bfloat16"), "pb": ("sbuf", [128, 128], "bfloat16"), "zi": ("sbuf", [128, 2], "int32"),
+    "za": ("sbuf", [128, 2], "int32"), "zb": ("sbuf", [128, 2], "int32"), "ra16": ("sbuf", [128, 1], "float32"),
+    "ra32": ("sbuf", [128, 1], "float32"), "b16": ("sbuf", [128, 8], "float32"), "b32": ("sbuf", [128, 8], "float32"),
+    "kf": ("sbuf", [128, 8], "float32"), "kg": ("sbuf", [128, 8], "float32"), "ki": ("sbuf", [128, 8], "float32"),
+    "cu": ("sbuf", [128, 4], "uint16"), "one": ("sbuf", [128, NEAR], "bfloat16"),
     "fb": ("sbuf", [128, 7 * BLK], "bfloat16"), "f0": ("sbuf", [128, COLS], "bfloat16"), "f1": ("sbuf", [128, PAIR], "bfloat16"),
     "f2": ("sbuf", [128, NEAR], "bfloat16"), "fs": ("sbuf", [128, NEAR], "bfloat16"), "k0": ("sbuf", [128, COLS], "bfloat16"),
     "k1": ("sbuf", [128, PAIR], "bfloat16"), "k2": ("sbuf", [128, NEAR], "bfloat16"), "ks": ("sbuf", [128, NEAR], "bfloat16"),
@@ -110,7 +109,7 @@ def rank_program(g, core, T, topo):
     gn, gf = H2 * far, NEAR * (1 - far)
     bits = lambda *ranks: sum(1 << e for e in ranks)
     look = lambda l: T.lut[:, 256 * l:256 * l + 256]
-    M1, M2, MS = range(3)
+    M0, M1, M2, MS = range(4)
     tab = lambda x: T.tab[:, 8 * x:8 * x + 8]
     bit = lambda e: [[0, 256 >> (e + 1)], [1, 2], [0, 1 << e]]
     R1, R2, RS, X2, XS, W2, WS = range(7)
@@ -125,22 +124,36 @@ def rank_program(g, core, T, topo):
     Y.dma_start(T.wt[:, :], T.w[:, :]).then_inc(T.sem.lw, 16)
 
     iota = lambda o, pat: mark("p", g.iota(o, pat, 0, 0, allow_small_or_imprecise_dtypes=True))
-    tlv = mark("p", g.iota(T.lv[:, :], [[1, 256]], 0, 0))
+    tlv = mark("p", g.iota(T.lv[:, :], [[1, 16]], 0, 0))
     tzi = mark("p", g.iota(T.zi[:, :], [[0, 2]], 0, 1))
     tb16 = iota(T.b16[:, :], [[16, 8]])
-    tb32 = iota(T.b32[:, :], [[32, 8]])
-    mark("v", V.memset(T.nz[:, 0:1], 0.0))
-    tnz = mark("v", V.memset(T.nz[:, 1:256], 1.0))
+    par = bits(*[e for e in range(4) if (e ^ q) & 1])
+    low = (q ^ 2) & 3
+    tpb = iota(T.pb[:, 0:16 << low], [[0, 8], [1, 2], [0, 1 << low]])
+    a = mark("v", V.memset(look(M0), 1.0))
+    need("v", tlv)
+    b = mark("v", V.tensor_scalar(T.la[:, :], T.lv[:, :], par, None, A.bitwise_and))
     tone = mark("v", V.memset(T.one[:, :], 1.0))
+    need("v", b)
+    b = mark("v", V.tensor_scalar(T.pa[:, :], T.la[:, :], 0.0, None, A.is_gt))
+    need("v", tzi)
+    tza = mark("v", V.tensor_scalar(T.za[:, :], T.zi[:, :], 15, None, A.bitwise_and))
+    need("s", a, b)
+    tl = {}
+    for u in range(16):
+        if not u & par:
+            tl[M0] = mark("s", SC.activation(T.lut[:, 16 * u:16 * u + 16], T.pa[:, :], F.Copy))
+    a = mark("v", V.memset(look(M1), 1.0))
+    need("v", tza)
+    b = mark("v", V.tensor_scalar(T.ra16[:, :], T.za[:, 0:1], 0.5, None, A.add))
+    need("s", b, tb16)
+    tkf = mark("s", SC.activation(T.kf[:, :], T.b16[:, :], F.Identity, bias=T.ra16[:, :]))
     txz = mark("v", V.memset(T.xt[:, 512:520], 0.0))
     tfz = mark("v", V.memset(T.fb[:, PAIR:7 * BLK:BLK], 0.0))
-    need("v", tlv)
-    a = mark("v", V.tensor_scalar(T.la[:, :], T.lv[:, :], bits(q ^ 2, q ^ 6), None, A.bitwise_and))
-    need("v", a)
-    tl = {M1: mark("v", V.tensor_scalar(look(M1), T.la[:, :], 0.0, None, A.is_gt)), None: tnz}
-    need("s", tone)
-    mark("s", SC.activation(T.g0[:, ZERO:ZERO + 16], T.one[:, 0:16], F.Copy, scale=0.0))
-    tz = mark("s", SC.activation(T.g1[:, ZERO:ZERO + 16], T.one[:, 0:16], F.Copy, scale=0.0))
+    need("s", a, tpb)
+    n = 16 << low
+    for u in range(0, 256, 2 * n):
+        tl[M1] = mark("s", SC.activation(T.lut[:, 256 + u:256 + u + n], T.pb[:, 0:n], F.Copy))
 
     use = {"js": 0, "jv": 0, "cs": 0, "ad": 0}
 
@@ -156,10 +169,9 @@ def rank_program(g, core, T, topo):
 
     def flags(e, out, l, masks, total, *deps):
         need(e, tl[l], *deps)
-        win = T.nz[:, :] if l is None else look(l)
         if e == "v":
-            return mark(e, V.tensor_copy(out, win.indirect(masks)))
-        return mark(e, SC.activation(out, win.indirect(masks), F.Copy, accum_out=total))
+            return mark(e, V.tensor_copy(out, look(l).indirect(masks)))
+        return mark(e, SC.activation(out, look(l).indirect(masks), F.Copy, accum_out=total))
 
     def gather(out, win, tab_, *deps):
         need("s", tfz, *deps)
@@ -167,16 +179,21 @@ def rank_program(g, core, T, topo):
 
     k_ = lambda t, j: (lambda i: t[:, j + i:j + i + 1])
 
-    def on_vector(key, kcol, skip, init, nv, *deps):
+    def compare(key, kcol, skip, nv, *deps):
         b, c, n = key
         o = take("jv", nv * n)
         need("v", *deps)
-        part = lambda t, i: t[:, o + i * n + skip(i):o + i * n + n]
         for i in range(nv):
-            a_ = mark("v", V.tensor_scalar(part(T.jv, i), b[:, c + skip(i):c + n], kcol(i), 0.5, A.is_le, A.subtract))
+            a_ = mark("v", V.tensor_scalar(T.jv[:, o + i * n + skip(i):o + i * n + n], b[:, c + skip(i):c + n], kcol(i), 0.5,
+                                           A.is_le, A.subtract))
+        return o, n, skip, nv, a_
+
+    def total(cmp, init, *deps):
+        o, n, skip, nv, a_ = cmp
         need("v", a_)
         for i in range(nv):
-            a_ = scan(part(T.jw, i), part(T.jv, i), init(i))
+            at_ = slice(o + i * n + skip(i), o + i * n + n)
+            a_ = scan(T.jw[:, at_], T.jv[:, at_], init(i), *deps)
         return (lambda i: T.jw[:, o + i * n + n - 1:o + i * n + n]), T.jw[:, o + n - 1:o + nv * n:n], a_
 
     def on_scalar(key, kcol, skip, ns, *deps):
@@ -194,20 +211,20 @@ def rank_program(g, core, T, topo):
         return on_scalar(key, k_(T.kf, nv), 16 * nv if first else 0, ns, tkf, *deps)
 
     def early_v(key, first, nv, *deps):
-        return on_vector(key, k_(T.kf, 0), lambda i: 16 * i if first else 0, lambda i: 8.0 * i, nv, tkf, *deps)
+        return total(compare(key, k_(T.kf, 0), lambda i: 16 * i if first else 0, nv, tkf, *deps), lambda i: 8.0 * i)
 
     def late_s(key, first, nv, ns, *deps):
         return on_scalar(key, k_(T.kf, nv), 0 if first else 16 * nv, ns, tkf, *deps)
 
-    def late_v(key, first, nv, va, *deps):
-        return on_vector(key, k_(T.kf, 0), lambda i: 0 if first else 16 * i, va[0], nv, tkf, va[2], *deps)
+    def late_v(key, first, nv, *deps):
+        return compare(key, k_(T.kf, 0), lambda i: 0 if first else 16 * i, nv, tkf, *deps)
 
     def complete(tab_, n, nv, ns, va, sa, sb):
-        need("v", va[2])
-        mark("v", V.tensor_scalar(tab_[:, 0:nv], va[1], n / 2, None, A.add))
         o = take("ad", ns)
         need("v", sa[1], sb[1])
         a_ = mark("v", V.tensor_tensor(T.ad[:, o:o + ns], sa[0], sb[0], A.add))
+        need("v", va[2])
+        mark("v", V.tensor_scalar(tab_[:, 0:nv], va[1], n / 2, None, A.add))
         need("v", a_)
         return mark("v", V.tensor_scalar(tab_[:, nv:nv + ns], T.ad[:, o:o + ns], 0.5, (n + 16 * nv) / 2, A.mult, A.add))
 
@@ -226,23 +243,17 @@ def rank_program(g, core, T, topo):
     need("v", ("ld", 128))
     tm = mark("v", V.tensor_copy(tab(0), T.dmi[:, :]))
     send(at(1), tab(1), tab(0), "rm1", tm)
-    spread([at(2), at(3)], [tab(2), tab(3)], tab(0), "rm2")
+    tb32 = iota(T.b32[:, :], [[32, 8]])
     tl[M2] = iota(look(M2), bit(q ^ 4))
 
-    a = mark("v", V.tensor_scalar(T.a0[:, :], T.dmi[:, :], bits(*[e for e in range(N) if (e ^ q) & 1]), None, A.bitwise_and))
-    need("v", tzi)
-    tza = mark("v", V.tensor_scalar(T.za[:, :], T.zi[:, :], 15, None, A.bitwise_and))
-    need("v", a)
-    a = mark("v", V.tensor_copy(T.u0[:, :], T.a0[:, :]))
-    need("v", tza)
-    b = mark("v", V.tensor_scalar(T.ra16[:, :], T.za[:, 0:1], 0.5, None, A.add))
-    need("s", b, tb16)
-    tkf = mark("s", SC.activation(T.kf[:, :], T.b16[:, :], F.Identity, bias=T.ra16[:, :]))
-    f = flags("v", T.f0[:, :], None, T.u0[:, :], None, a)
+    f = flags("v", T.f0[:, :], M0, tab(0), None, tm)
     ti = scan(T.k0[:, :], T.f0[:, :], 0.0, f)
     key = (T.k0, 0, COLS)
     sb = on_scalar(key, k_(T.kf, 2), 32, 2, tkf, ti)
-    va = on_vector(key, k_(T.kf, 0), lambda i: 16 * i, lambda i: 8.0 * i, 2, tkf, ti)
+    need("s", tone)
+    mark("s", SC.activation(T.g0[:, ZERO:ZERO + 16], T.one[:, 0:16], F.Copy, scale=0.0))
+    tz = mark("s", SC.activation(T.g1[:, ZERO:ZERO + 16], T.one[:, 0:16], F.Copy, scale=0.0))
+    va = total(compare(key, k_(T.kf, 0), lambda i: 16 * i, 2, tkf, ti), lambda i: 8.0 * i)
     need("v", ("lx", 16), txz)
     tq0 = mark("v", V.quantize_mx(T.c0c[:, :], T.c0s[:, :], T.xt[:, :]))
     need("v", va[2])
@@ -250,6 +261,7 @@ def rank_program(g, core, T, topo):
     need("v", sb[1])
     t0 = mark("v", V.tensor_scalar(T.t0[:, 2:4], sb[0], 0.5, (COLS + 32) / 2, A.mult, A.add))
     send(at(1), T.lt1[:, :], T.t0[:, :], "l1", t0)
+    spread([at(2), at(3)], [tab(2), tab(3)], tab(0), "rm2")
     ship(at(1), "c1", COLS * hi, "sl0", H0, "h0", (pick_codes("sl0", "c0", H0, T.t0, t0, tq0), pick_plane("sl0", "c0", H0, T.t0, t0, tq0)))
     send(at(3), T.lt3[:, :], T.t0[:, :], "l3", t0)
     tl[MS] = iota(look(MS), bit(q))
@@ -276,7 +288,6 @@ def rank_program(g, core, T, topo):
     rm1, rm2 = arrived("rm1", at(1)), arrived("rm2", at(2), at(3))
     l1, l2, l3 = arrived("l1", at(1)), arrived("l2", at(2)), arrived("l3", at(3))
     e1 = flags("s", T.f1[:, po:po + COLS], M1, tab(0), None, tm)
-    e2 = flags("s", T.f2[:, cp + po:cp + po + COLS], M2, tab(0), None, tm)
     d1 = flags("s", others(R1), M1, tab(1), T.e1[:, :] if hi else None, rm1)
     a = mark("v", V.tensor_scalar(T.zb[:, :], T.zi[:, :], 31, None, A.bitwise_and))
     mark("v", V.tensor_scalar(T.cu[:, 0:2], T.za[:, :], 0.0, None, A.add))
@@ -299,20 +310,19 @@ def rank_program(g, core, T, topo):
     sa = early_s(own, not hi, *N1, ta)
     va = early_v(own, not hi, N1[0], ta)
     es = flags("v", T.fs[:, cp + po:cp + po + COLS], MS, tab(0), None, tm)
+    d2 = flags("s", others(R2), M2, tab(1), None, rm1)
     s1 = gather(T.f1[:, ps:ps + H0], tail(R1), T.lt1[:, :], l1, d1)
     tb = scan(T.k1[:, ps:ps + H0], T.f1[:, ps:ps + H0], 0.0 if hi else T.k1[:, po + COLS - 1:po + COLS], ta, s1)
+    vb = total(late_v(came, not hi, N1[0], tb), va[0], va[2])
+    e2 = flags("s", T.f2[:, cp + po:cp + po + COLS], M2, tab(0), None, tm)
     sb = late_s(came, not hi, *N1, tb)
-    vb = late_v(came, not hi, N1[0], va, tb)
     t1 = complete(T.t1, PAIR, *N1, vb, sa, sb)
     send(at(2), T.lt2[:, :], T.t1[:, :], "l2", t1)
-    d2 = flags("s", others(R2), M2, tab(1), None, rm1)
     s2 = gather(T.f2[:, cp + ps:cp + ps + H0], tail(R2), T.lt1[:, :], l1, d2)
     da = flags("s", blk(W2, po, COLS), M2, tab(2), T.ba[:, :], rm2)
     db = flags("s", others(X2), M2, tab(3), T.bb[:, :], rm2)
     need("s", da, db)
     tbs = mark("s", SC.activation(T.bs[:, :], T.ba[:, :], F.Identity, bias=T.bb[:, :]))
-    ship(at(2), "c2", PAIR * up, "sl1", H1, "h1",
-         (pick_codes("sl1", "c1", H1, T.t1, t1, w1, *h0a), pick_plane("sl1", "c1", H1, T.t1, t1, w1, *h0a)))
     d3 = flags("v", others(RS), MS, tab(1), None, rm1)
     d4 = flags("v", others(XS), MS, tab(3), None, rm2)
 
@@ -322,15 +332,20 @@ def rank_program(g, core, T, topo):
         ta = scan(T.k2[:, cp:cp + PAIR], T.f2[:, cp:cp + PAIR], T.bs[:, :], e2, s2, tbs)
     else:
         ta = scan(T.k2[:, cp:cp + PAIR], T.f2[:, cp:cp + PAIR], 0.0, e2, s2)
-    s3 = gather(blk(W2, ps, H0), tail(X2), T.lt3[:, :], l3, db)
-    sa = early_s(own, not up, *N2, ta)
-    va = early_v(own, not up, N2[0], ta)
+    ship(at(2), "c2", PAIR * up, "sl1", H1, "h1",
+         (pick_codes("sl1", "c1", H1, T.t1, t1, w1, *h0a), pick_plane("sl1", "c1", H1, T.t1, t1, w1, *h0a)))
     need("s", ta, tbs)
     if up:
-        tnf = mark("s", SC.activation(T.nfo[:, :], end, F.Copy))
+        mark("s", SC.activation(T.nfo[:, 0:1], end, F.Copy))
+        tnf = mark("s", SC.activation(T.nfo[:, 1:2], end, F.Copy, scale=-1.0))
     else:
-        tnf = mark("s", SC.activation(T.nfo[:, :], end, F.Identity, bias=T.bs[:, :]))
+        tnf = mark("s", SC.activation(T.nfo[:, 0:1], end, F.Identity, bias=T.bs[:, :]))
+        need("s", tnf)
+        tnf = mark("s", SC.activation(T.nfo[:, 1:2], T.nfo[:, 0:1], F.Copy, scale=-1.0))
     send(at(4), T.nfa[:, :], T.nfo[:, :], "nf", tnf)
+    sa = early_s(own, not up, *N2, ta)
+    va = early_v(own, not up, N2[0], ta)
+    s3 = gather(blk(W2, ps, H0), tail(X2), T.lt3[:, :], l3, db)
     d5 = flags("v", blk(WS, po, COLS), MS, tab(2), None, rm2)
     if far:
         need("v", tki)
@@ -339,15 +354,23 @@ def rank_program(g, core, T, topo):
     s6 = gather(blk(WS, ps, H0), tail(XS), T.lt3[:, :], l3, d4)
     s4 = gather(T.f2[:, cb:cb + H1], whole(W2), T.lt2[:, :], l2, s3, da)
     tb = scan(T.k2[:, cb:cb + H1], T.f2[:, cb:cb + H1], 0.0 if up else end, ta, s4)
-    sb = late_s(came, not up, *N2, tb)
-    vb = late_v(came, not up, N2[0], va, tb)
-    t2 = complete(T.t2, NEAR, *N2, vb, sa, sb)
     s7 = gather(T.fs[:, cb:cb + H1], whole(WS), T.lt2[:, :], l2, d5, s6)
+    sb = late_s(came, not up, *N2, tb)
+    vb = late_v(came, not up, N2[0], tb)
+    tss = scan(T.ks[:, :], T.fs[:, :], 0.0, es, s5, s7)
+    nf = arrived("nf", at(4))
+    tke, kE = tkg, T.kg
+    if far:
+        need("s", nf, tkg)
+        tke, kE = mark("s", SC.activation(T.ke[:, :], T.kg[:, :], F.Identity, bias=T.nfa[:, 1:2])), T.ke
+        need("s", tke)
+    vb = total(vb, va[0], va[2])
+    near = (T.ks, 0, NEAR)
+    on_scalar(near, k_(kE, NF), 0, NE, tke, tss)
+    t2 = complete(T.t2, NEAR, *N2, vb, sa, sb)
     h1a = [arrived("h1c", at(2)), arrived("h1s", at(2))]
     ship(at(4), "a2", 0, "sl2", H2, "h2",
          (pick_codes("sl2", "c2", H2, T.t2, t2, w2, *h1a), pick_plane("sl2", "c2", H2, T.t2, t2, w2, *h1a)))
-
-    tss = scan(T.ks[:, :], T.fs[:, :], 0.0, es, s5, s7)
 
     def product(o, bank, c, n, *deps):
         need("t", tqw, *deps)
@@ -356,23 +379,21 @@ def rank_program(g, core, T, topo):
     m0 = product(0, 0, "c2", NEAR, w2, *h1a)
     m1 = product(1, 1, "c2", NEAR)
 
-    nn = T.ks[:, NEAR - 1:NEAR]
-    nf = arrived("nf", at(4))
-    if far:
-        need("v", nf, tkg, tki)
-        mark("v", V.tensor_scalar(T.gb[:, :], T.ki[:, :], T.nfa[:, :], float(H2), A.is_ge, A.mult))
-        tke, kE = mark("v", V.tensor_scalar(T.ke[:, :], T.kg[:, :], T.nfa[:, :], None, A.subtract)), T.ke
-        need("v", tga, tke)
-        tgt = mark("v", V.tensor_tensor(T.gt[:, :], T.ga[:, :], T.gb[:, :], A.max))
-    else:
-        tke, kE = tkg, T.kg
-        need("v", tki, tss)
-        tgt = mark("v", V.tensor_scalar(T.gt[:, :], T.ki[:, :], nn, 0.0, A.subtract, A.max))
-
-    ls_, lst = on_scalar((T.ks, 0, NEAR), k_(kE, NF), 0, 8 - NF, tke, tss)
-    _, lv_, lvt = on_vector((T.ks, 0, NEAR), k_(kE, 0), lambda i: 0, lambda i: -LOW, NF, tke, tss)
+    cmp = compare(near, k_(kE, 0), lambda i: 0, NF, tke, tss)
+    _, lst = on_scalar(near, k_(kE, NF + NE), 0, 8 - NF - NE, tke, tss)
+    ls_ = T.cs[:, use["cs"] - 8 + NF:use["cs"]]
     need("s", lst)
     ths = mark("s", SC.activation(T.hs[:, 0:8 - NF], ls_, F.Copy, scale=0.5, bias=-LOW))
+    need("v", tki)
+    if far:
+        need("v", nf)
+        a = mark("v", V.tensor_scalar(T.gb[:, :], T.ki[:, :], T.nfa[:, 0:1], float(H2), A.is_ge, A.mult))
+        _, lv_, lvt = total(cmp, lambda i: -LOW)
+        need("v", tga, a)
+        tgt = mark("v", V.tensor_tensor(T.gt[:, :], T.ga[:, :], T.gb[:, :], A.max))
+    else:
+        tgt = mark("v", V.tensor_scalar(T.gt[:, :], T.ki[:, :], T.ks[:, NEAR - 1:NEAR], 0.0, A.subtract, A.max))
+        _, lv_, lvt = total(cmp, lambda i: -LOW)
     need("v", lvt, tgt, trr)
     mark("v", V.tensor_tensor(T.rr[:, 0:NF], lv_, T.gt[:, 0:NF], A.add))
     need("v", ths)
@@ -394,8 +415,8 @@ def rank_program(g, core, T, topo):
     h2a = [arrived("h2c", at(4)), arrived("h2s", at(4))]
     m2 = product(0, 2, "a2", H2, *h2a)
     m3 = product(1, 3, "a2", H2)
-    need("v", m2)
-    b0 = mark("v", V.tensor_copy(T.g0[:, gf:gf + H2], T.ps[:, 1024:1024 + H2]))
+    need("s", m2)
+    b0 = mark("s", SC.activation(T.g0[:, gf:gf + H2], T.ps[:, 1024:1024 + H2], F.Copy))
     need("s", m3)
     b1 = mark("s", SC.activation(T.g1[:, gf:gf + H2], T.ps[:, 1536:1536 + H2], F.Copy))
     need("v", b0, g0a, tz, ttf)
@@ -407,7 +428,7 @@ def rank_program(g, core, T, topo):
     need("s", y1)
     SC.dma_start(T.y[:, S:2 * S], T.y1[:, :]).then_inc(T.sem.syb, 16)
     need("s", tss, nf)
-    mark("s", SC.activation(T.lnb[0:1, 0:1], T.nfa[0:1, :], F.Identity, bias=T.ks[0:1, NEAR - 1:NEAR]))
+    mark("s", SC.activation(T.lnb[0:1, 0:1], T.nfa[0:1, 0:1], F.Identity, bias=T.ks[0:1, NEAR - 1:NEAR]))
     c = cp + po
     if c:
         tln = mark("s", SC.activation(T.lnb[0:1, 1:2], T.ks[0:1, c - 1:c], F.Identity, bias=T.ks[0:1, c + COLS - 1:c + COLS], scale=-1.0))

from concourse.bass import DstId, RemoteDMATransfer
from concourse.mybir import dt, AluOpType, ActivationFunctionType

A = AluOpType
F = ActivationFunctionType
U8, U32 = dt.uint8, dt.uint32
N, COLS, S = 8, 128, 256
H0, H1, H2 = 64, 96, 128
PAIR = COLS + H0
NEAR = PAIR + H1
ZERO = NEAR + H2
N1, N2 = (3, 3), (4, 4)
NF, NE = 3, 2
LOW = 64.0

CODE, PLANE = "float8_e4m3fn_x4", "uint8"
BLK = 208
SCRATCH = {
    "dmi": ("sbuf", [128, 8], "int32"), "xt": ("sbuf", [128, 520], "bfloat16"), "wt": ("sbuf", [128, 1024], "bfloat16"),
    "c0c": ("sbuf", [128, COLS + 2], CODE), "c0s": ("sbuf", [128, COLS + 2], PLANE),
    "c1c": ("sbuf", [128, PAIR + 2], CODE), "c1s": ("sbuf", [128, PAIR + 2], PLANE),
    "c2c": ("sbuf", [128, NEAR + 2], CODE), "c2s": ("sbuf", [128, NEAR + 2], PLANE),
    "a2c": ("sbuf", [128, H2], CODE), "a2s": ("sbuf", [128, H2], PLANE),
    "wqc": ("sbuf", [128, 256], CODE), "wqs": ("sbuf", [128, 256], PLANE),
    "sl0c": ("sbuf", [128, H0], CODE), "sl0s": ("sbuf", [128, H0], PLANE),
    "sl1c": ("sbuf", [128, H1], CODE), "sl1s": ("sbuf", [128, H1], PLANE),
    "sl2c": ("sbuf", [128, H2], CODE), "sl2s": ("sbuf", [128, H2], PLANE),
    "tab": ("sbuf", [128, 32], "uint16"), "lt1": ("sbuf", [128, 4], "uint16"), "lt3": ("sbuf", [128, 4], "uint16"),
    "lt2": ("sbuf", [128, 6], "uint16"), "nfa": ("sbuf", [128, 2], "float32"), "nfo": ("sbuf", [128, 2], "float32"),
    "lut": ("sbuf", [128, 1024], "bfloat16"), "lv": ("sbuf", [128, 16], "int32"), "la": ("sbuf", [128, 16], "int32"),
    "pa": ("sbuf", [128, 16], "bfloat16"), "pb": ("sbuf", [128, 128], "bfloat16"), "zi": ("sbuf", [128, 2], "int32"),
    "za": ("sbuf", [128, 2], "int32"), "zb": ("sbuf", [128, 2], "int32"), "ra16": ("sbuf", [128, 1], "float32"),
    "ra32": ("sbuf", [128, 1], "float32"), "b16": ("sbuf", [128, 8], "float32"), "b32": ("sbuf", [128, 8], "float32"),
    "kf": ("sbuf", [128, 8], "float32"), "kg": ("sbuf", [128, 8], "float32"), "ki": ("sbuf", [128, 8], "float32"),
    "cu": ("sbuf", [128, 4], "uint16"), "one": ("sbuf", [128, NEAR], "bfloat16"),
    "fb": ("sbuf", [128, 7 * BLK], "bfloat16"), "f0": ("sbuf", [128, COLS], "bfloat16"), "f1": ("sbuf", [128, PAIR], "bfloat16"),
    "f2": ("sbuf", [128, NEAR], "bfloat16"), "fs": ("sbuf", [128, NEAR], "bfloat16"), "k0": ("sbuf", [128, COLS], "bfloat16"),
    "k1": ("sbuf", [128, PAIR], "bfloat16"), "k2": ("sbuf", [128, NEAR], "bfloat16"), "ks": ("sbuf", [128, NEAR], "bfloat16"),
    "e1": ("sbuf", [128, 1], "float32"), "ba": ("sbuf", [128, 1], "float32"), "bb": ("sbuf", [128, 1], "float32"),
    "bs": ("sbuf", [128, 1], "float32"),
    "js": ("sbuf", [128, 6144], "bfloat16"), "jv": ("sbuf", [128, 6144], "bfloat16"), "jw": ("sbuf", [128, 6144], "bfloat16"),
    "cs": ("sbuf", [128, 32], "float32"), "hs": ("sbuf", [128, 8], "float32"), "rr": ("sbuf", [128, 32], "bfloat16"),
    "ra": ("sbuf", [128, 32], "bfloat16"), "rb": ("sbuf", [128, 64], "bfloat16"), "rc": ("sbuf", [128, 64], "bfloat16"),
    "ad": ("sbuf", [128, 16], "float32"),
    "ke": ("sbuf", [128, 8], "float32"), "ga": ("sbuf", [128, 8], "float32"), "gb": ("sbuf", [128, 8], "float32"),
    "gt": ("sbuf", [128, 8], "float32"),
    "t0": ("sbuf", [128, 4], "uint16"), "t1": ("sbuf", [128, 6], "uint16"), "t2": ("sbuf", [128, 8], "uint16"),
    "tf": ("sbuf", [128, 16], "uint16"), "lnb": ("sbuf", [1, 2], "float32"),
    "g0": ("sbuf", [128, ZERO + 16], "float32"), "g1": ("sbuf", [128, ZERO + 16], "float32"),
    "y0": ("sbuf", [128, 256], "float32"), "y1": ("sbuf", [128, 256], "float32"),
    "ps": ("psum", [128, 2048], "float32"),
}
ARR = ["rm1", "rm2", "l1", "l2", "l3", "nf", "h0c", "h0s", "h1c", "h1s", "h2c", "h2s"]
SEMAPHORES = ["qv", "qs", "qt", "qp", "ld", "lx", "lw", "cp1", "cp2", "sya", "syb", "sln", "loc"] + ARR


def rank_program(g, core, T, topo):
    q = T.rank_of(core)
    if q is None:
        return
    V, SC, TE, Y = g.vector, g.scalar, g.tensor, g.sync
    queue = {"v": V, "s": SC, "t": TE, "p": g, "y": Y}
    done = {"v": 0, "s": 0, "t": 0, "p": 0}
    seen = {}

    def need(e, *deps):
        best = {}
        for d in deps:
            best[d[0]] = max(best.get(d[0], 0), d[1])
        for s in best:
            if seen.get((e, s), 0) < best[s]:
                queue[e].wait_ge(T.sem[s], best[s])
                seen[(e, s)] = best[s]

    def mark(e, ins):
        ins.then_inc(T.sem["q" + e], 1)
        done[e] += 1
        return ("q" + e, done[e])

    sent = [0]

    def send(dst, out, in_, sem, *deps):
        need("p", *deps)
        rid, pid = topo.addr(dst, core)
        g.remote_dma(out, in_, T.sem[sem], T.sem["loc"], pid, rid, topo.mask(core, dst))
        sent[0] += len(topo.engines(core, dst))

    def spread(dsts, outs, in_, sem, *deps):
        need("p", *deps)
        ids = []
        m = topo.mask(core, dsts[0])
        for d in dsts:
            rid, pid = topo.addr(d, core)
            ids.append(DstId(rid=rid, pnc=pid))
            m &= topo.mask(core, d)
        g.remote_dma_fused([RemoteDMATransfer(dst_ids=ids, dma_engine_mask=m, remote_sem=T.sem[sem], srcs=[in_], dsts=outs)],
                           local_sem=T.sem["loc"])
        sent[0] += bin(m).count("1")

    def arrived(sem, *srcs):
        return (sem, sum(len(topo.engines(s, core)) for s in srcs))

    at = lambda x: T.cores[q ^ x]
    codes = lambda t, a, b: t[:, a:b].bitcast(U8)

    hi, up, far = q & 1, (q >> 1) & 1, q >> 2
    po, ps = H0 * hi, COLS * (1 - hi)
    cp, cb = H1 * up, PAIR * (1 - up)
    gn, gf = H2 * far, NEAR * (1 - far)
    bits = lambda *ranks: sum(1 << e for e in ranks)
    look = lambda l: T.lut[:, 256 * l:256 * l + 256]
    M0, M1, M2, MS = range(4)
    tab = lambda x: T.tab[:, 8 * x:8 * x + 8]
    bit = lambda e: [[0, 256 >> (e + 1)], [1, 2], [0, 1 << e]]
    R1, R2, RS, X2, XS, W2, WS = range(7)
    blk = lambda b, a, n: T.fb[:, BLK * b + a:BLK * b + a + n]
    others = lambda b: blk(b, H0, COLS)
    tail = lambda b: blk(b, H0, BLK - H0)
    whole = lambda b: blk(b, 0, BLK)

    for i in range(8):
        (Y if i % 2 == 0 else SC).dma_start(T.dmi[16 * i:16 * i + 16, :], T.dm[:, :]).then_inc(T.sem.ld, 16)
    Y.dma_start(T.xt[:, 0:512], T.x[:, :]).then_inc(T.sem.lx, 16)
    Y.dma_start(T.wt[:, :], T.w[:, :]).then_inc(T.sem.lw, 16)

    iota = lambda o, pat: mark("p", g.iota(o, pat, 0, 0, allow_small_or_imprecise_dtypes=True))
    tlv = mark("p", g.iota(T.lv[:, :], [[1, 16]], 0, 0))
    tzi = mark("p", g.iota(T.zi[:, :], [[0, 2]], 0, 1))
    tb16 = iota(T.b16[:, :], [[16, 8]])
    par = bits(*[e for e in range(4) if (e ^ q) & 1])
    low = (q ^ 2) & 3
    tpb = iota(T.pb[:, 0:16 << low], [[0, 8], [1, 2], [0, 1 << low]])
    a = mark("v", V.memset(look(M0), 1.0))
    need("v", tlv)
    b = mark("v", V.tensor_scalar(T.la[:, :], T.lv[:, :], par, None, A.bitwise_and))
    tone = mark("v", V.memset(T.one[:, :], 1.0))
    need("v", b)
    b = mark("v", V.tensor_scalar(T.pa[:, :], T.la[:, :], 0.0, None, A.is_gt))
    need("v", tzi)
    tza = mark("v", V.tensor_scalar(T.za[:, :], T.zi[:, :], 15, None, A.bitwise_and))
    need("s", a, b)
    tl = {}
    for u in range(16):
        if not u & par:
            tl[M0] = mark("s", SC.activation(T.lut[:, 16 * u:16 * u + 16], T.pa[:, :], F.Copy))
    a = mark("v", V.memset(look(M1), 1.0))
    need("v", tza)
    b = mark("v", V.tensor_scalar(T.ra16[:, :], T.za[:, 0:1], 0.5, None, A.add))
    need("s", b, tb16)
    tkf = mark("s", SC.activation(T.kf[:, :], T.b16[:, :], F.Identity, bias=T.ra16[:, :]))
    txz = mark("v", V.memset(T.xt[:, 512:520], 0.0))
    tfz = mark("v", V.memset(T.fb[:, PAIR:7 * BLK:BLK], 0.0))
    need("s", a, tpb)
    n = 16 << low
    for u in range(0, 256, 2 * n):
        tl[M1] = mark("s", SC.activation(T.lut[:, 256 + u:256 + u + n], T.pb[:, 0:n], F.Copy))

    use = {"js": 0, "jv": 0, "cs": 0, "ad": 0}

    def take(name, n):
        o = use[name]
        use[name] += n
        return o

    def scan(out, fl, init, *deps):
        need("v", tone, *deps)
        n = int(out.shape[1])
        return mark("v", V.tensor_tensor_scan(out, T.one[:, 0:n], fl, init, A.mult, A.add))

    def flags(e, out, l, masks, total, *deps):
        need(e, tl[l], *deps)
        if e == "v":
            return mark(e, V.tensor_copy(out, look(l).indirect(masks)))
        return mark(e, SC.activation(out, look(l).indirect(masks), F.Copy, accum_out=total))

    def gather(out, win, tab_, *deps):
        need("s", tfz, *deps)
        return mark("s", SC.activation(out, win.indirect(tab_), F.Copy))

    k_ = lambda t, j: (lambda i: t[:, j + i:j + i + 1])

    def compare(key, kcol, skip, nv, *deps):
        b, c, n = key
        o = take("jv", nv * n)
        need("v", *deps)
        for i in range(nv):
            a_ = mark("v", V.tensor_scalar(T.jv[:, o + i * n + skip(i):o + i * n + n], b[:, c + skip(i):c + n], kcol(i), 0.5,
                                           A.is_le, A.subtract))
        return o, n, skip, nv, a_

    def total(cmp, init, *deps):
        o, n, skip, nv, a_ = cmp
        need("v", a_)
        for i in range(nv):
            at_ = slice(o + i * n + skip(i), o + i * n + n)
            a_ = scan(T.jw[:, at_], T.jv[:, at_], init(i), *deps)
        return (lambda i: T.jw[:, o + i * n + n - 1:o + i * n + n]), T.jw[:, o + n - 1:o + nv * n:n], a_

    def on_scalar(key, kcol, skip, ns, *deps):
        b, c, n = key
        o_ = take("cs", ns)
        need("s", *deps)
        n -= skip
        for i in range(ns):
            o = take("js", n)
            a_ = mark("s", SC.activation(T.js[:, o:o + n], b[:, c + skip:c + skip + n], F.Sign, bias=kcol(i), scale=-1.0,
                                         accum_out=T.cs[:, o_ + i:o_ + i + 1]))
        return T.cs[:, o_:o_ + ns], a_

    def early_s(key, first, nv, ns, *deps):
        return on_scalar(key, k_(T.kf, nv), 16 * nv if first else 0, ns, tkf, *deps)

    def early_v(key, first, nv, *deps):
        return total(compare(key, k_(T.kf, 0), lambda i: 16 * i if first else 0, nv, tkf, *deps), lambda i: 8.0 * i)

    def late_s(key, first, nv, ns, *deps):
        return on_scalar(key, k_(T.kf, nv), 0 if first else 16 * nv, ns, tkf, *deps)

    def late_v(key, first, nv, *deps):
        return compare(key, k_(T.kf, 0), lambda i: 0 if first else 16 * i, nv, tkf, *deps)

    def complete(tab_, n, nv, ns, va, sa, sb):
        o = take("ad", ns)
        need("v", sa[1], sb[1])
        a_ = mark("v", V.tensor_tensor(T.ad[:, o:o + ns], sa[0], sb[0], A.add))
        need("v", va[2])
        mark("v", V.tensor_scalar(tab_[:, 0:nv], va[1], n / 2, None, A.add))
        need("v", a_)
        return mark("v", V.tensor_scalar(tab_[:, nv:nv + ns], T.ad[:, o:o + ns], 0.5, (n + 16 * nv) / 2, A.mult, A.add))

    def pick_codes(out, src, n, tab_, *deps):
        need("v", *deps)
        return mark("v", V.tensor_copy(T[out + "c"][:, 0:n].bitcast(U32), T[src + "c"][:, :].bitcast(U32).indirect(tab_[:, :])))

    def pick_plane(out, src, n, tab_, *deps):
        need("s", *deps)
        return mark("s", SC.activation(T[out + "s"][:, 0:n], T[src + "s"][:, :].indirect(tab_[:, :]), F.Copy))

    def ship(dst, to, a_, src, n, sem, tok):
        send(dst, codes(T[to + "c"], a_, a_ + n), codes(T[src + "c"], 0, n), sem + "c", tok[0])
        send(dst, T[to + "s"][:, a_:a_ + n], T[src + "s"][:, 0:n], sem + "s", tok[1])

    need("v", ("ld", 128))
    tm = mark("v", V.tensor_copy(tab(0), T.dmi[:, :]))
    send(at(1), tab(1), tab(0), "rm1", tm)
    tb32 = iota(T.b32[:, :], [[32, 8]])
    tl[M2] = iota(look(M2), bit(q ^ 4))

    f = flags("v", T.f0[:, :], M0, tab(0), None, tm)
    ti = scan(T.k0[:, :], T.f0[:, :], 0.0, f)
    key = (T.k0, 0, COLS)
    sb = on_scalar(key, k_(T.kf, 2), 32, 2, tkf, ti)
    need("s", tone)
    mark("s", SC.activation(T.g0[:, ZERO:ZERO + 16], T.one[:, 0:16], F.Copy, scale=0.0))
    tz = mark("s", SC.activation(T.g1[:, ZERO:ZERO + 16], T.one[:, 0:16], F.Copy, scale=0.0))
    va = total(compare(key, k_(T.kf, 0), lambda i: 16 * i, 2, tkf, ti), lambda i: 8.0 * i)
    need("v", ("lx", 16), txz)
    tq0 = mark("v", V.quantize_mx(T.c0c[:, :], T.c0s[:, :], T.xt[:, :]))
    need("v", va[2])
    mark("v", V.tensor_scalar(T.t0[:, 0:2], va[1], COLS / 2, None, A.add))
    need("v", sb[1])
    t0 = mark("v", V.tensor_scalar(T.t0[:, 2:4], sb[0], 0.5, (COLS + 32) / 2, A.mult, A.add))
    send(at(1), T.lt1[:, :], T.t0[:, :], "l1", t0)
    spread([at(2), at(3)], [tab(2), tab(3)], tab(0), "rm2")
    ship(at(1), "c1", COLS * hi, "sl0", H0, "h0", (pick_codes("sl0", "c0", H0, T.t0, t0, tq0), pick_plane("sl0", "c0", H0, T.t0, t0, tq0)))
    send(at(3), T.lt3[:, :], T.t0[:, :], "l3", t0)
    tl[MS] = iota(look(MS), bit(q))

    need("y", tq0)
    tot = COLS + 2 * hi
    Y.dma_start(codes(T.c1c, po, po + tot), codes(T.c0c, 0, tot)).then_inc(T.sem.cp1, 16)
    Y.dma_start(T.c1s[:, po:po + tot], T.c0s[:, 0:tot]).then_inc(T.sem.cp1, 16)
    w1 = 32
    if not hi:
        Y.dma_start(codes(T.c1c, PAIR, PAIR + 2), codes(T.c0c, COLS, COLS + 2)).then_inc(T.sem.cp1, 16)
        Y.dma_start(T.c1s[:, PAIR:PAIR + 2], T.c0s[:, COLS:COLS + 2]).then_inc(T.sem.cp1, 16)
        w1 = 64
    Y.dma_start(codes(T.c2c, cp + po, cp + po + COLS), codes(T.c0c, 0, COLS)).then_inc(T.sem.cp2, 16)
    Y.dma_start(T.c2s[:, cp + po:cp + po + COLS], T.c0s[:, 0:COLS]).then_inc(T.sem.cp2, 16)
    Y.dma_start(codes(T.c2c, NEAR, NEAR + 2), codes(T.c0c, COLS, COLS + 2)).then_inc(T.sem.cp2, 16)
    Y.dma_start(T.c2s[:, NEAR:NEAR + 2], T.c0s[:, COLS:COLS + 2]).then_inc(T.sem.cp2, 16)
    h0a = [arrived("h0c", at(1)), arrived("h0s", at(1))]
    need("y", *h0a)
    Y.dma_start(codes(T.c2c, cp + ps, cp + ps + H0), codes(T.c1c, ps, ps + H0)).then_inc(T.sem.cp2, 16)
    Y.dma_start(T.c2s[:, cp + ps:cp + ps + H0], T.c1s[:, ps:ps + H0]).then_inc(T.sem.cp2, 16)
    w1, w2 = ("cp1", w1), ("cp2", 96)

    rm1, rm2 = arrived("rm1", at(1)), arrived("rm2", at(2), at(3))
    l1, l2, l3 = arrived("l1", at(1)), arrived("l2", at(2)), arrived("l3", at(3))
    e1 = flags("s", T.f1[:, po:po + COLS], M1, tab(0), None, tm)
    d1 = flags("s", others(R1), M1, tab(1), T.e1[:, :] if hi else None, rm1)
    a = mark("v", V.tensor_scalar(T.zb[:, :], T.zi[:, :], 31, None, A.bitwise_and))
    mark("v", V.tensor_scalar(T.cu[:, 0:2], T.za[:, :], 0.0, None, A.add))
    tcu = mark("v", V.tensor_scalar(T.cu[:, 2:4], T.za[:, :], 16.0, None, A.add))
    need("v", a)
    a = mark("v", V.tensor_scalar(T.ra32[:, :], T.zb[:, 0:1], 0.5, None, A.add))
    need("s", a, tb32)
    tkg = mark("s", SC.activation(T.kg[:, :], T.b32[:, :], F.Identity, bias=T.ra32[:, :]))
    need("s", tkg)
    tki = mark("s", SC.activation(T.ki[:, :], T.kg[:, :], F.Copy, bias=-0.5))
    trr = mark("v", V.memset(T.rr[:, :], 0.0))
    need("v", ("lw", 16))
    tqw = mark("v", V.quantize_mx(T.wqc[:, :], T.wqs[:, :], T.wt[:, :]))

    own, came = (T.k1, po, COLS), (T.k1, ps, H0)
    if hi:
        ta = scan(T.k1[:, po:po + COLS], T.f1[:, po:po + COLS], T.e1[:, :], e1, d1)
    else:
        ta = scan(T.k1[:, po:po + COLS], T.f1[:, po:po + COLS], 0.0, e1)
    sa = early_s(own, not hi, *N1, ta)
    va = early_v(own, not hi, N1[0], ta)
    es = flags("v", T.fs[:, cp + po:cp + po + COLS], MS, tab(0), None, tm)
    d2 = flags("s", others(R2), M2, tab(1), None, rm1)
    s1 = gather(T.f1[:, ps:ps + H0], tail(R1), T.lt1[:, :], l1, d1)
    tb = scan(T.k1[:, ps:ps + H0], T.f1[:, ps:ps + H0], 0.0 if hi else T.k1[:, po + COLS - 1:po + COLS], ta, s1)
    vb = total(late_v(came, not hi, N1[0], tb), va[0], va[2])
    e2 = flags("s", T.f2[:, cp + po:cp + po + COLS], M2, tab(0), None, tm)
    sb = late_s(came, not hi, *N1, tb)
    t1 = complete(T.t1, PAIR, *N1, vb, sa, sb)
    send(at(2), T.lt2[:, :], T.t1[:, :], "l2", t1)
    s2 = gather(T.f2[:, cp + ps:cp + ps + H0], tail(R2), T.lt1[:, :], l1, d2)
    da = flags("s", blk(W2, po, COLS), M2, tab(2), T.ba[:, :], rm2)
    db = flags("s", others(X2), M2, tab(3), T.bb[:, :], rm2)
    need("s", da, db)
    tbs = mark("s", SC.activation(T.bs[:, :], T.ba[:, :], F.Identity, bias=T.bb[:, :]))
    d3 = flags("v", others(RS), MS, tab(1), None, rm1)
    d4 = flags("v", others(XS), MS, tab(3), None, rm2)

    own, came = (T.k2, cp, PAIR), (T.k2, cb, H1)
    end = T.k2[:, cp + PAIR - 1:cp + PAIR]
    if up:
        ta = scan(T.k2[:, cp:cp + PAIR], T.f2[:, cp:cp + PAIR], T.bs[:, :], e2, s2, tbs)
    else:
        ta = scan(T.k2[:, cp:cp + PAIR], T.f2[:, cp:cp + PAIR], 0.0, e2, s2)
    ship(at(2), "c2", PAIR * up, "sl1", H1, "h1",
         (pick_codes("sl1", "c1", H1, T.t1, t1, w1, *h0a), pick_plane("sl1", "c1", H1, T.t1, t1, w1, *h0a)))
    need("s", ta, tbs)
    if up:
        mark("s", SC.activation(T.nfo[:, 0:1], end, F.Copy))
        tnf = mark("s", SC.activation(T.nfo[:, 1:2], end, F.Copy, scale=-1.0))
    else:
        tnf = mark("s", SC.activation(T.nfo[:, 0:1], end, F.Identity, bias=T.bs[:, :]))
        need("s", tnf)
        tnf = mark("s", SC.activation(T.nfo[:, 1:2], T.nfo[:, 0:1], F.Copy, scale=-1.0))
    send(at(4), T.nfa[:, :], T.nfo[:, :], "nf", tnf)
    sa = early_s(own, not up, *N2, ta)
    va = early_v(own, not up, N2[0], ta)
    s3 = gather(blk(W2, ps, H0), tail(X2), T.lt3[:, :], l3, db)
    d5 = flags("v", blk(WS, po, COLS), MS, tab(2), None, rm2)
    if far:
        need("v", tki)
        tga = mark("v", V.tensor_scalar(T.ga[:, :], T.ki[:, :], float(H2), None, A.min))
    s5 = gather(T.fs[:, cp + ps:cp + ps + H0], tail(RS), T.lt1[:, :], l1, d3)
    s6 = gather(blk(WS, ps, H0), tail(XS), T.lt3[:, :], l3, d4)
    s4 = gather(T.f2[:, cb:cb + H1], whole(W2), T.lt2[:, :], l2, s3, da)
    tb = scan(T.k2[:, cb:cb + H1], T.f2[:, cb:cb + H1], 0.0 if up else end, ta, s4)
    s7 = gather(T.fs[:, cb:cb + H1], whole(WS), T.lt2[:, :], l2, d5, s6)
    sb = late_s(came, not up, *N2, tb)
    vb = late_v(came, not up, N2[0], tb)
    tss = scan(T.ks[:, :], T.fs[:, :], 0.0, es, s5, s7)
    nf = arrived("nf", at(4))
    tke, kE = tkg, T.kg
    if far:
        need("s", nf, tkg)
        tke, kE = mark("s", SC.activation(T.ke[:, :], T.kg[:, :], F.Identity, bias=T.nfa[:, 1:2])), T.ke
        need("s", tke)
    vb = total(vb, va[0], va[2])
    near = (T.ks, 0, NEAR)
    on_scalar(near, k_(kE, NF), 0, NE, tke, tss)
    t2 = complete(T.t2, NEAR, *N2, vb, sa, sb)
    h1a = [arrived("h1c", at(2)), arrived("h1s", at(2))]
    ship(at(4), "a2", 0, "sl2", H2, "h2",
         (pick_codes("sl2", "c2", H2, T.t2, t2, w2, *h1a), pick_plane("sl2", "c2", H2, T.t2, t2, w2, *h1a)))

    def product(o, bank, c, n, *deps):
        need("t", tqw, *deps)
        return mark("t", TE.matmul_mx(T.ps[:, 512 * bank:512 * bank + n], T.wqc[:, 128 * o:128 * o + 128], T.wqs[:, 128 * o:128 * o + 128],
                                      T[c + "c"][:, 0:n], T[c + "s"][:, 0:n], True, True))
    m0 = product(0, 0, "c2", NEAR, w2, *h1a)
    m1 = product(1, 1, "c2", NEAR)

    cmp = compare(near, k_(kE, 0), lambda i: 0, NF, tke, tss)
    _, lst = on_scalar(near, k_(kE, NF + NE), 0, 8 - NF - NE, tke, tss)
    ls_ = T.cs[:, use["cs"] - 8 + NF:use["cs"]]
    need("s", lst)
    ths = mark("s", SC.activation(T.hs[:, 0:8 - NF], ls_, F.Copy, scale=0.5, bias=-LOW))
    need("v", tki)
    if far:
        need("v", nf)
        a = mark("v", V.tensor_scalar(T.gb[:, :], T.ki[:, :], T.nfa[:, 0:1], float(H2), A.is_ge, A.mult))
        _, lv_, lvt = total(cmp, lambda i: -LOW)
        need("v", tga, a)
        tgt = mark("v", V.tensor_tensor(T.gt[:, :], T.ga[:, :], T.gb[:, :], A.max))
    else:
        tgt = mark("v", V.tensor_scalar(T.gt[:, :], T.ki[:, :], T.ks[:, NEAR - 1:NEAR], 0.0, A.subtract, A.max))
        _, lv_, lvt = total(cmp, lambda i: -LOW)
    need("v", lvt, tgt, trr)
    mark("v", V.tensor_tensor(T.rr[:, 0:NF], lv_, T.gt[:, 0:NF], A.add))
    need("v", ths)
    a = mark("v", V.tensor_tensor(T.rr[:, NF:8], T.hs[:, 0:8 - NF], T.gt[:, NF:8], A.add))
    need("v", a)
    a = mark("v", V.transpose(T.ra[:, :], T.rr[:, :]))
    need("v", a, tcu)
    a = mark("v", V.tensor_copy(T.rb[:, :], T.ra[:, :].indirect(T.cu[:, :])))
    need("v", a)
    a = mark("v", V.transpose(T.rc[:, :], T.rb[:, :]))
    need("v", a)
    mark("v", V.tensor_scalar(T.tf[:, 0:16:2], T.rc[:, 0:8], NEAR / 2 + LOW, float(ZERO), A.add, A.min))
    ttf = mark("v", V.tensor_scalar(T.tf[:, 1:16:2], T.rc[:, 32:40], NEAR / 2 + LOW, float(ZERO), A.add, A.min))
    need("s", m0)
    g0a = mark("s", SC.activation(T.g0[:, gn:gn + NEAR], T.ps[:, 0:NEAR], F.Copy))
    need("s", m1)
    g1a = mark("s", SC.activation(T.g1[:, gn:gn + NEAR], T.ps[:, 512:512 + NEAR], F.Copy))

    h2a = [arrived("h2c", at(4)), arrived("h2s", at(4))]
    m2 = product(0, 2, "a2", H2, *h2a)
    m3 = product(1, 3, "a2", H2)
    need("s", m2)
    b0 = mark("s", SC.activation(T.g0[:, gf:gf + H2], T.ps[:, 1024:1024 + H2], F.Copy))
    need("s", m3)
    b1 = mark("s", SC.activation(T.g1[:, gf:gf + H2], T.ps[:, 1536:1536 + H2], F.Copy))
    need("v", b0, g0a, tz, ttf)
    y0 = mark("v", V.tensor_copy(T.y0[:, :], T.g0[:, :].indirect(T.tf[:, :])))
    need("s", b1, g1a, tz, ttf)
    y1 = mark("s", SC.activation(T.y1[:, :], T.g1[:, :].indirect(T.tf[:, :]), F.Copy))
    need("y", y0)
    Y.dma_start(T.y[:, 0:S], T.y0[:, :]).then_inc(T.sem.sya, 16)
    need("s", y1)
    SC.dma_start(T.y[:, S:2 * S], T.y1[:, :]).then_inc(T.sem.syb, 16)
    need("s", tss, nf)
    mark("s", SC.activation(T.lnb[0:1, 0:1], T.nfa[0:1, 0:1], F.Identity, bias=T.ks[0:1, NEAR - 1:NEAR]))
    c = cp + po
    if c:
        tln = mark("s", SC.activation(T.lnb[0:1, 1:2], T.ks[0:1, c - 1:c], F.Identity, bias=T.ks[0:1, c + COLS - 1:c + COLS], scale=-1.0))
    else:
        tln = mark("s", SC.activation(T.lnb[0:1, 1:2], T.ks[0:1, COLS - 1:COLS], F.Copy))
    need("y", tln)
    Y.dma_start(T.ln[:, :], T.lnb[:, :]).then_inc(T.sem.sln, 16)

    need("p", ("loc", sent[0]), ("qv", done["v"]), ("qs", done["s"]), ("qt", done["t"]), ("qp", done["p"]))
    need("y", ("sln", 16), ("sya", 16))
    need("s", ("syb", 16))
